import numpy as np
import ml_dtypes


def mxq(x, axis, fmt="e4m3"):
    dtype, down = {"e4m3": (ml_dtypes.float8_e4m3fn, 7), "e5m2": (ml_dtypes.float8_e5m2, 14)}[fmt]
    v = np.moveaxis(np.asarray(x, np.float32).astype(ml_dtypes.bfloat16).astype(np.float64), axis, -1)
    blocks = v.reshape(v.shape[:-1] + (-1, 32))
    amax = np.abs(blocks).max(-1, keepdims=True)
    byte = np.maximum(np.where(amax > 0, np.frexp(amax)[1] - 1 + 127, 0) - down, 1)
    scale = np.exp2(byte - 127.0)
    codes = (blocks / scale).astype(np.float32).astype(dtype).astype(np.float64)
    return np.moveaxis((codes * scale).reshape(v.shape), -1, axis)


WIDE = False


def mx_kscale(k):
    if not WIDE:
        return np.ones(k)
    levels = np.array([24, -24, 12, -12, 0])
    if k % 512:
        return np.exp2(np.random.permutation(np.resize(levels, k // 32))).repeat(32)
    a = np.empty((k // 512, 16))
    for p in range(k // 512):
        a[p, :8] = np.random.permutation(np.resize(levels, 8))
        for g in range(8):
            far = levels[np.abs(levels - a[p, g]) >= 10]
            a[p, g + 8] = far[np.random.randint(len(far))]
    return np.exp2(a.ravel()).repeat(32)


def f64(x):
    return np.asarray(x).astype(np.float64)


def striped(idx):
    return np.tile(idx.reshape(-1, 16).T, (8, 1)).astype(np.uint16)


def unstriped(offs):
    return offs[:16].T.reshape(-1).astype(np.int64)


E2M1 = np.array([0.0, 0.5, 1.0, 1.5, 2.0, 3.0, 4.0, 6.0, -0.0, -0.5, -1.0, -1.5, -2.0, -3.0, -4.0, -6.0])


def pack_weight(w, fmt):
    k, n = w.shape
    w = f64(np.asarray(w, np.float32).astype(ml_dtypes.bfloat16)).reshape(k // 32, 32, n)
    amax = np.abs(w).max(1)
    if fmt == "e4m3":
        byte = np.frexp(amax)[1] - 1 + 127 - 7
    else:
        mant, ex = np.frexp(amax / 6.0)
        byte = np.where(mant > 0.5, ex, ex - 1) + 127
    byte = np.clip(np.where(amax > 0, byte, 1), 1, 254)
    scaled = (w * np.exp2(127.0 - byte)[:, None, :]).reshape(k, n).astype(np.float32)
    by_word = np.ascontiguousarray(scaled.reshape(k // 512, 128, 4, n).transpose(0, 1, 3, 2))
    if fmt == "e4m3":
        words = by_word.astype(ml_dtypes.float8_e4m3fn).view(np.uint8)
    else:
        c = by_word.astype(ml_dtypes.float4_e2m1fn).view(np.uint8) & 0xF
        words = (c[..., 0::2] | (c[..., 1::2] << 4)).reshape(k // 512, 128, 2 * n)
    return np.ascontiguousarray(words), np.ascontiguousarray(byte.astype(np.uint8).reshape(k // 512, 16, n))


def unpack_weight(words, scales, fmt):
    g, _, n = scales.shape
    words = np.ascontiguousarray(words).reshape(g, 128, n, -1)
    if fmt == "e4m3":
        vals = words.view(ml_dtypes.float8_e4m3fn).astype(np.float64)
    else:
        nib = np.empty((g, 128, n, 4), np.uint8)
        nib[..., 0::2] = words & 0xF
        nib[..., 1::2] = words >> 4
        vals = E2M1[nib]
    vals = vals * np.repeat(np.exp2(scales.astype(np.float64) - 127.0), 8, axis=1)[..., None]
    return vals.transpose(0, 1, 3, 2).reshape(g * 512, n)


def pack_table4(v):
    words, scales = pack_weight(v, "e2m1")
    g, t = words.shape[0] // 2, v.shape[1]
    return np.ascontiguousarray(words.reshape(g, 2, 128, t, 2).transpose(0, 2, 3, 1, 4).reshape(g, 128, t, 4)), scales


def unpack_table4(words, scales):
    g, _, t, _ = words.shape
    return unpack_weight(words.reshape(g, 128, t, 2, 2).transpose(0, 3, 1, 2, 4).reshape(2 * g, 128, 2 * t), scales, "e2m1")


def silu(f):
    return f / (1.0 + np.exp(-np.maximum(f, -700.0)))


def sigm(f):
    return 1.0 / (1.0 + np.exp(-np.maximum(f, -700.0)))


K, M, N, J, T = 1024, 512, 512, 1024, 4096


def setup_inputs():
    n = np.random.standard_normal
    s = mx_kscale(K)[:, None]
    u = mx_kscale(J)[:, None]
    al = n((J, N)) / np.sqrt(J) / u
    al4 = pack_weight(al, "e2m1")
    alrest = al - unpack_weight(*al4, "e2m1")
    p_tab = pack_table4(0.5 * n((K, T)) / np.sqrt(K) / s)
    p_al8 = pack_weight(alrest, "e4m3")
    return {
        "x": (n((K, M)) * s).astype(np.float32),
        "tab_words": p_tab[0],
        "tab_scales": p_tab[1],
        "cw": (np.random.uniform(0.5, 2.0, J) * u[:, 0]).astype(np.float32),
        "cb": (0.3 * n(J)).astype(np.float32),
        "al4_words": al4[0],
        "al4_scales": al4[1],
        "al8_words": p_al8[0],
        "al8_scales": p_al8[1],
        "b": (0.3 * n(N)).astype(np.float32),
        "offs": striped(np.random.permutation(T)[:J]),
    }


def reference(x, tab_words, tab_scales, cw, cb, al4_words, al4_scales, al8_words, al8_scales, b, offs):
    idx = unstriped(offs)
    x_ = mxq(f64(x), 0, "e4m3")
    tab_ = unpack_table4(tab_words, tab_scales)[:, idx]
    d = tab_.T @ x_
    h = f64(cw)[:, None] * sigm(d + f64(cb)[:, None])
    h_ = mxq(h, 0, "e4m3")
    al4_ = unpack_weight(al4_words, al4_scales, "e2m1")
    al8_ = unpack_weight(al8_words, al8_scales, "e4m3")
    y = al4_.T @ h_ + al8_.T @ h_
    return silu(y + f64(b)[:, None])

@@ -1,0 +1,262 @@
+from contextlib import ExitStack
+
+import concourse.mybir as mybir
+
+K, M, N, J, T = 1024, 512, 512, 1024, 4096
+FLOPS = 2 * K * J * M + 2 * 2 * J * N * M
+
+F32 = mybir.dt.float32
+BF16 = mybir.dt.bfloat16
+I32 = mybir.dt.int32
+U32 = mybir.dt.uint32
+U16 = mybir.dt.uint16
+U8 = mybir.dt.uint8
+FP8X4 = mybir.dt.float8_e4m3fn_x4
+FP4X4 = mybir.dt.float4_e2m1fn_x4
+ACT = mybir.ActivationFunctionType
+ALU = mybir.AluOpType
+
+P = 128
+PACK = 4
+KP = P * PACK
+HALF = M // 2
+COLS = 128
+SHIFT = 16
+
+
+def tile_list_kernl_sigm_res_silu_kernel(
+    tc, x, tab_words, tab_scales, cw, cb, al4_words, al4_scales, al8_words, al8_scales, b, offs, out
+):
+    nc = tc.nc
+    with ExitStack() as ctx:
+        held = ctx.enter_context(tc.tile_pool(name="held", bufs=1))
+        shared = ctx.enter_context(tc.tile_pool(name="shared", bufs=1))
+        psum = ctx.enter_context(tc.psum_pool(name="psum", bufs=1))
+
+        def placed(shape, dtype, name, offset):
+            return shared.tile(shape, dtype, name=name, tag=name, align_bytes=64, offset=offset)
+
+        def sb(shape, dtype, name, tag=None):
+            return held.tile(shape, dtype, name=name, tag=tag or name, align_bytes=64)
+
+        offsets = held.tile([P, J // 16], U16, name="offsets")
+        nc.sync.dma_start(offsets[:], offs)
+
+        scale_window = placed([P, T // 4], I32, "scale_window", 0)
+        nc.vector.memset(scale_window[:], 0)
+        planes = sb([P, 3 * J // 4], I32, "planes")
+        nc.vector.memset(planes[:], 0)
+        tab_scales_i32 = tab_scales.bitcast(I32)
+        for r in range(4):
+            nc.scalar.dma_start(
+                scale_window[r:P:SHIFT, :], tab_scales_i32[:, r:16:4, :].rearrange("a q n -> q a n")
+            )
+
+        x_raw = {}
+
+        def load_x(a, hf, tile):
+            x_raw[a, hf] = tile
+            rows = x[a * KP : (a + 1) * KP, hf * HALF : (hf + 1) * HALF]
+            nc.sync.dma_start(tile, rows.rearrange("(p i) m -> p i m", i=PACK))
+
+        load_x(0, 0, sb([P, PACK, HALF], F32, "x_first")[:])
+        word_window = sb([P, T], I32, "word_window")
+        nc.sync.dma_start(word_window[:], tab_words[0].rearrange("p t b -> p (t b)").bitcast(I32))
+
+        cb_sb = sb([P, 2, PACK], F32, "cb_sb")
+        cw_sb = sb([P, 2, PACK], F32, "cw_sb")
+        b_sb = sb([P, N // P], F32, "b_sb")
+        nc.gpsimd.dma_start(cb_sb[:], cb.rearrange("(a p t) -> p a t", a=2, t=PACK))
+        nc.gpsimd.dma_start(cw_sb[:], cw.rearrange("(a p t) -> p a t", a=2, t=PACK))
+        al_planes = planes[:, J // 4 :].rearrange("p (w a n) -> p w a n", w=2, a=2)
+        for w, scales in enumerate((al4_scales, al8_scales)):
+            for r in range(4):
+                nc.gpsimd.dma_start(
+                    al_planes[r:P:32, w], scales.bitcast(I32)[:, r:16:4, :].rearrange("a q n -> q a n")
+                )
+        with nc.allow_non_contiguous_dma(reason="one bias value to a partition"):
+            nc.gpsimd.dma_start(b_sb[:], b.rearrange("(c p) -> p c", p=P))
+        planes_u8 = planes[:].bitcast(U8)
+
+        warm = sb([P, 1], F32, "warm")
+        nc.scalar.activation(warm[:], cb_sb[:, 0, 0:1], ACT.Sigmoid)
+
+        picked_scales = sb([P, J], U8, "picked_scales")
+        nc.vector.tensor_copy(picked_scales[:], scale_window[:].bitcast(U8).indirect(offsets[:]))
+        x_rest = placed([P, 3, PACK, HALF], F32, "x_rest", 3072)
+        load_x(1, 0, x_rest[:, 0])
+        load_x(0, 1, x_rest[:, 1])
+        load_x(1, 1, x_rest[:, 2])
+        tab_plane0 = sb([P, J], U8, "tab_plane0")
+        nc.vector.tensor_copy(
+            tab_plane0[:].rearrange("p (t c i) -> p c t i", t=PACK, i=16),
+            picked_scales[:].rearrange("p (c i t) -> p c t i", t=PACK, i=16),
+        )
+        nc.scalar.dma_start(planes[0 : P - SHIFT, 0 : J // 4], tab_plane0[:].bitcast(I32)[SHIFT:P, :])
+        tab_planes = (tab_plane0[:], planes_u8[:, 0:J])
+
+        x_bf16, x_codes, x_scales = {}, {}, {}
+
+        def interleave_x(a, hf, copy):
+            x_bf16[a, hf] = sb([P, HALF, PACK], BF16, "x_bf16_%d%d" % (a, hf))
+            copy(
+                x_bf16[a, hf][:].rearrange("p (c i) t -> p c t i", i=2),
+                x_raw[a, hf].rearrange("p t (c i) -> p c t i", i=2),
+            )
+
+        def quantize(src, name):
+            if name == "x00":
+                codes = placed([P, HALF], U32, name + "_codes", 0)
+            else:
+                codes = sb([P, HALF], U32, name + "_codes")
+            scales = sb([P, HALF], U8, name + "_scales")
+            nc.vector.quantize_mx(codes[:].bitcast(FP8X4), scales[:], src[:].rearrange("p m t -> p (m t)"))
+            return codes, scales
+
+        def quantize_x(a, hf):
+            x_codes[a, hf], x_scales[a, hf] = quantize(x_bf16[a, hf], "x%d%d" % (a, hf))
+
+        picked_words, tab_codes = {}, {}
+
+        def gather_words(g):
+            if g == 0:
+                picked_words[g] = placed([P, KP], U32, "picked_words0", 1024)
+            else:
+                picked_words[g] = sb([P, KP], U32, "picked_words%d" % g)
+            nc.vector.tensor_copy(
+                picked_words[g][:], word_window[:].bitcast(U32).indirect(offsets[:, 32 * g : 32 * (g + 1)])
+            )
+
+        def part_words(g):
+            tab_codes[g] = sb([P, 2 * PACK * 2 * COLS], U8, "tab_codes%d" % g)
+            nc.vector.tensor_copy(
+                tab_codes[g][:].bitcast(U16).rearrange("p (a t c i) -> p a c t i", a=2, t=PACK, i=4),
+                picked_words[g][:].bitcast(U16).rearrange("p (c i t a) -> p a c t i", a=2, t=PACK, i=4),
+            )
+
+        interleave_x(0, 0, nc.scalar.copy)
+        quantize_x(0, 0)
+        gather_words(0)
+        part_words(0)
+        interleave_x(1, 0, nc.scalar.copy)
+        gather_words(1)
+        quantize_x(1, 0)
+        part_words(1)
+        interleave_x(0, 1, nc.scalar.copy)
+        interleave_x(1, 1, nc.vector.tensor_copy)
+        quantize_x(0, 1)
+        quantize_x(1, 1)
+
+        al8_codes = sb([P, 2, N], I32, "al8_codes", tag="word_window")
+        nc.sync.dma_start(al8_codes[:], al8_words.rearrange("a p n i -> p a (n i)").bitcast(I32))
+        al4_codes = sb([P, 2, N // 2], I32, "al4_codes", tag="x_bf16_10")
+        nc.sync.dma_start(al4_codes[:], al4_words.rearrange("a p n -> p a n").bitcast(I32))
+
+        def bank(index, name):
+            return psum.tile([P, 2 * HALF], F32, name=name, tag="bank%d" % index)
+
+        d_banks = {}
+
+        def first_product(hf, g, pair, a):
+            if a == 0:
+                d_banks[hf, g, pair] = bank(4 * hf + 2 * g + pair, "d%d%d%d" % (hf, g, pair))
+            for u in range(2):
+                t = 2 * pair + u
+                codes = tab_codes[g][:, (a * PACK + t) * 2 * COLS : (a * PACK + t + 1) * 2 * COLS]
+                scales = tab_planes[a][:, (2 * t + g) * COLS : (2 * t + g + 1) * COLS]
+                for q in range(2):
+                    cols = slice(q * COLS, (q + 1) * COLS)
+                    nc.tensor.matmul_mx(
+                        d_banks[hf, g, pair][:, u * HALF + q * COLS : u * HALF + (q + 1) * COLS],
+                        lhsT=codes.bitcast(FP4X4),
+                        lhsT_scale=scales,
+                        rhs=x_codes[a, hf][:, cols].bitcast(FP8X4),
+                        rhs_scale=x_scales[a, hf][:, cols],
+                        start=(a == 0 and u == 0 and q == 0),
+                        stop=(a == 1 and u == 1 and q == 1),
+                    )
+
+        logistic, h_bf16, h_codes, h_scales = {}, {}, {}, {}
+
+        def sigmoids(hf, g):
+            logistic[hf, g] = sb([P, PACK, HALF], F32, "logistic%d%d" % (hf, g))
+            for t in range(PACK):
+                nc.scalar.activation(
+                    logistic[hf, g][:, t, :],
+                    d_banks[hf, g, t // 2][:, (t % 2) * HALF : (t % 2 + 1) * HALF],
+                    ACT.Sigmoid,
+                    bias=cb_sb[:, g, t : t + 1],
+                )
+
+        def weigh(hf, g):
+            h_bf16[hf, g] = sb([P, HALF, PACK], BF16, "h_bf16_%d%d" % (hf, g))
+            nc.vector.tensor_tensor(
+                h_bf16[hf, g][:].rearrange("p (c i) t -> p c t i", i=2),
+                logistic[hf, g][:].rearrange("p t (c i) -> p c t i", i=2),
+                cw_sb[:, g, :].unsqueeze(1).unsqueeze(3).to_broadcast([P, HALF // 2, PACK, 2]),
+                ALU.mult,
+            )
+
+        def quantize_h(hf, g):
+            h_codes[hf, g], h_scales[hf, g] = quantize(h_bf16[hf, g], "h%d%d" % (hf, g))
+
+        y_banks = {}
+
+        def second_product(hf, g, c):
+            if g == 0:
+                y_banks[hf, c] = bank(4 * hf + c, "y%d%d" % (hf, c))
+            n0 = c * COLS
+
+            def tier8():
+                nc.tensor.matmul_mx(
+                    y_banks[hf, c][:, 0:HALF],
+                    lhsT=al8_codes[:, g, n0 : n0 + COLS].bitcast(FP8X4),
+                    lhsT_scale=planes_u8[:, 2 * J + g * N + n0 : 2 * J + g * N + n0 + COLS],
+                    rhs=h_codes[hf, g][:].bitcast(FP8X4),
+                    rhs_scale=h_scales[hf, g][:],
+                    start=(g == 0),
+                    stop=(g == 1),
+                )
+
+            if g == 0:
+                tier8()
+            for q in range(2):
+                cols = slice(q * COLS, (q + 1) * COLS)
+                nc.tensor.matmul_mx(
+                    y_banks[hf, c][:, cols],
+                    lhsT=al4_codes[:, g, n0 // 2 : (n0 + COLS) // 2].bitcast(FP4X4),
+                    lhsT_scale=planes_u8[:, J + g * N + n0 : J + g * N + n0 + COLS],
+                    rhs=h_codes[hf, g][:, cols].bitcast(FP8X4),
+                    rhs_scale=h_scales[hf, g][:, cols],
+                    start=False,
+                    stop=False,
+                )
+            if g == 1:
+                tier8()
+
+        def finish(hf, c):
+            result = sb([P, HALF], F32, "result%d%d" % (hf, c))
+            nc.scalar.activation(result[:], y_banks[hf, c][:, 0:HALF], ACT.Silu, bias=b_sb[:, c : c + 1])
+            nc.sync.dma_start(out[c * COLS : (c + 1) * COLS, hf * HALF : (hf + 1) * HALF], result[:])
+
+        for hf in range(2):
+            for g in range(2):
+                for a in range(2):
+                    for pair in range(2):
+                        first_product(hf, g, pair, a)
+                sigmoids(hf, g)
+        weigh(0, 0)
+        weigh(0, 1)
+        quantize_h(0, 0)
+        quantize_h(0, 1)
+        weigh(1, 0)
+        quantize_h(1, 0)
+        weigh(1, 1)
+        quantize_h(1, 1)
+        for hf in range(2):
+            for g in range(2):
+                for c in range(N // COLS):
+                    second_product(hf, g, c)
+        for hf in range(2):
+            for c in range(N // COLS):
+                finish(hf, c)

@@ -42,16 +42,6 @@ def tile_list_kernl_sigm_res_silu_kernel(
         offsets = held.tile([P, J // 16], U16, name="offsets")
         nc.sync.dma_start(offsets[:], offs)
 
-        scale_window = placed([P, T // 4], I32, "scale_window", 0)
-        nc.vector.memset(scale_window[:], 0)
-        planes = sb([P, 3 * J // 4], I32, "planes")
-        nc.vector.memset(planes[:], 0)
-        tab_scales_i32 = tab_scales.bitcast(I32)
-        for r in range(4):
-            nc.scalar.dma_start(
-                scale_window[r:P:SHIFT, :], tab_scales_i32[:, r:16:4, :].rearrange("a q n -> q a n")
-            )
-
         x_raw = {}
 
         def load_x(a, hf, tile):
@@ -60,40 +50,55 @@ def tile_list_kernl_sigm_res_silu_kernel(
             nc.sync.dma_start(tile, rows.rearrange("(p i) m -> p i m", i=PACK))
 
         load_x(0, 0, sb([P, PACK, HALF], F32, "x_first")[:])
-        word_window = sb([P, T], I32, "word_window")
+
+        warm_in = placed([P, 32], F32, "warm_in", 20480 - 64)
+        nc.gpsimd.memset(warm_in[:], 0.0)
+        warm_out = sb([P, 32], F32, "warm_out")
+        nc.scalar.activation(warm_out[:], warm_in[:], ACT.Sigmoid)
+
+        scale_window = placed([P, T // 4], I32, "scale_window", 0)
+        nc.vector.memset(scale_window[:], 0)
+        tab_plane1 = sb([P, J // 4], I32, "tab_plane1")
+        nc.vector.memset(tab_plane1[:], 0)
+        tab_scales_i32 = tab_scales.bitcast(I32)
+        for r in range(4):
+            nc.sync.dma_start(
+                scale_window[r:P:SHIFT, :], tab_scales_i32[:, r:16:4, :].rearrange("a q n -> q a n")
+            )
+
+        word_window = placed([P, T], I32, "word_window", 4096)
         nc.sync.dma_start(word_window[:], tab_words[0].rearrange("p t b -> p (t b)").bitcast(I32))
-
-        cb_sb = sb([P, 2, PACK], F32, "cb_sb")
-        cw_sb = sb([P, 2, PACK], F32, "cw_sb")
-        b_sb = sb([P, N // P], F32, "b_sb")
-        nc.gpsimd.dma_start(cb_sb[:], cb.rearrange("(a p t) -> p a t", a=2, t=PACK))
-        nc.gpsimd.dma_start(cw_sb[:], cw.rearrange("(a p t) -> p a t", a=2, t=PACK))
-        al_planes = planes[:, J // 4 :].rearrange("p (w a n) -> p w a n", w=2, a=2)
-        for w, scales in enumerate((al4_scales, al8_scales)):
-            for r in range(4):
-                nc.gpsimd.dma_start(
-                    al_planes[r:P:32, w], scales.bitcast(I32)[:, r:16:4, :].rearrange("a q n -> q a n")
-                )
-        with nc.allow_non_contiguous_dma(reason="one bias value to a partition"):
-            nc.gpsimd.dma_start(b_sb[:], b.rearrange("(c p) -> p c", p=P))
-        planes_u8 = planes[:].bitcast(U8)
-
-        warm = sb([P, 1], F32, "warm")
-        nc.scalar.activation(warm[:], cb_sb[:, 0, 0:1], ACT.Sigmoid)
-
-        picked_scales = sb([P, J], U8, "picked_scales")
-        nc.vector.tensor_copy(picked_scales[:], scale_window[:].bitcast(U8).indirect(offsets[:]))
-        x_rest = placed([P, 3, PACK, HALF], F32, "x_rest", 3072)
+        x_rest = placed([P, 3, PACK, HALF], F32, "x_rest", 20480)
         load_x(1, 0, x_rest[:, 0])
         load_x(0, 1, x_rest[:, 1])
         load_x(1, 1, x_rest[:, 2])
+
+        picked_scales = sb([P, J], U8, "picked_scales")
+        nc.vector.tensor_copy(picked_scales[:], scale_window[:].bitcast(U8).indirect(offsets[:]))
+        cb_sb = placed([P, 2, PACK], F32, "cb_sb", 2048)
+        cw_sb = placed([P, 2, PACK], F32, "cw_sb", 2048 + 64)
+        b_sb = placed([P, N // P], F32, "b_sb", 2048 + 128)
+        nc.scalar.dma_start(cb_sb[:], cb.rearrange("(a p t) -> p a t", a=2, t=PACK))
+        nc.sync.dma_start(cw_sb[:], cw.rearrange("(a p t) -> p a t", a=2, t=PACK))
+        with nc.allow_non_contiguous_dma(reason="one bias value to a partition"):
+            nc.sync.dma_start(b_sb[:], b.rearrange("(c p) -> p c", p=P))
         tab_plane0 = sb([P, J], U8, "tab_plane0")
         nc.vector.tensor_copy(
             tab_plane0[:].rearrange("p (t c i) -> p c t i", t=PACK, i=16),
             picked_scales[:].rearrange("p (c i t) -> p c t i", t=PACK, i=16),
         )
-        nc.scalar.dma_start(planes[0 : P - SHIFT, 0 : J // 4], tab_plane0[:].bitcast(I32)[SHIFT:P, :])
-        tab_planes = (tab_plane0[:], planes_u8[:, 0:J])
+        nc.scalar.dma_start(tab_plane1[0 : P - SHIFT, :], tab_plane0[:].bitcast(I32)[SHIFT:P, :])
+        tab_planes = (tab_plane0[:], tab_plane1[:].bitcast(U8))
+
+        al_planes = placed([P, 2, 2, N // 4], I32, "al_planes", 0)
+        nc.vector.memset(al_planes[:], 0)
+        for w, scales in enumerate((al8_scales, al4_scales)):
+            for r in range(4):
+                nc.sync.dma_start(
+                    al_planes[r:P:32, w], scales.bitcast(I32)[:, r:16:4, :].rearrange("a q n -> q a n")
+                )
+        al8_planes = al_planes[:, 0].bitcast(U8)
+        al4_planes = al_planes[:, 1].bitcast(U8)
 
         x_bf16, x_codes, x_scales = {}, {}, {}
 
@@ -105,10 +110,7 @@ def tile_list_kernl_sigm_res_silu_kernel(
             )
 
         def quantize(src, name):
-            if name == "x00":
-                codes = placed([P, HALF], U32, name + "_codes", 0)
-            else:
-                codes = sb([P, HALF], U32, name + "_codes")
+            codes = sb([P, HALF], U32, name + "_codes")
             scales = sb([P, HALF], U8, name + "_scales")
             nc.vector.quantize_mx(codes[:].bitcast(FP8X4), scales[:], src[:].rearrange("p m t -> p (m t)"))
             return codes, scales
@@ -119,20 +121,17 @@ def tile_list_kernl_sigm_res_silu_kernel(
         picked_words, tab_codes = {}, {}
 
         def gather_words(g):
-            if g == 0:
-                picked_words[g] = placed([P, KP], U32, "picked_words0", 1024)
-            else:
-                picked_words[g] = sb([P, KP], U32, "picked_words%d" % g)
+            picked_words[g] = sb([P, KP], U32, "picked_words%d" % g, tag="picked_words")
             nc.vector.tensor_copy(
                 picked_words[g][:], word_window[:].bitcast(U32).indirect(offsets[:, 32 * g : 32 * (g + 1)])
             )
 
         def part_words(g):
             tab_codes[g] = sb([P, 2 * PACK * 2 * COLS], U8, "tab_codes%d" % g)
-            nc.vector.tensor_copy(
-                tab_codes[g][:].bitcast(U16).rearrange("p (a t c i) -> p a c t i", a=2, t=PACK, i=4),
-                picked_words[g][:].bitcast(U16).rearrange("p (c i t a) -> p a c t i", a=2, t=PACK, i=4),
-            )
+            parted = tab_codes[g][:].bitcast(U16).rearrange("p (a t c i) -> p a c t i", a=2, t=PACK, i=4)
+            paired = picked_words[g][:].bitcast(U16).rearrange("p (c i t a) -> p a c t i", a=2, t=PACK, i=4)
+            for a in range(2):
+                nc.vector.tensor_copy(parted[:, a], paired[:, a])
 
         interleave_x(0, 0, nc.scalar.copy)
         quantize_x(0, 0)
@@ -143,11 +142,11 @@ def tile_list_kernl_sigm_res_silu_kernel(
         quantize_x(1, 0)
         part_words(1)
         interleave_x(0, 1, nc.scalar.copy)
-        interleave_x(1, 1, nc.vector.tensor_copy)
         quantize_x(0, 1)
+        interleave_x(1, 1, nc.vector.tensor_copy)
         quantize_x(1, 1)
 
-        al8_codes = sb([P, 2, N], I32, "al8_codes", tag="word_window")
+        al8_codes = placed([P, 2, N], I32, "al8_codes", 4096)
         nc.sync.dma_start(al8_codes[:], al8_words.rearrange("a p n i -> p a (n i)").bitcast(I32))
         al4_codes = sb([P, 2, N // 2], I32, "al4_codes", tag="x_bf16_10")
         nc.sync.dma_start(al4_codes[:], al4_words.rearrange("a p n -> p a n").bitcast(I32))
@@ -189,7 +188,7 @@ def tile_list_kernl_sigm_res_silu_kernel(
                 )
 
         def weigh(hf, g):
-            h_bf16[hf, g] = sb([P, HALF, PACK], BF16, "h_bf16_%d%d" % (hf, g))
+            h_bf16[hf, g] = sb([P, HALF, PACK], BF16, "h_bf16_%d%d" % (hf, g), tag="h_bf16_%d" % min(2 * hf + g, 2))
             nc.vector.tensor_tensor(
                 h_bf16[hf, g][:].rearrange("p (c i) t -> p c t i", i=2),
                 logistic[hf, g][:].rearrange("p t (c i) -> p c t i", i=2),
@@ -211,7 +210,7 @@ def tile_list_kernl_sigm_res_silu_kernel(
                 nc.tensor.matmul_mx(
                     y_banks[hf, c][:, 0:HALF],
                     lhsT=al8_codes[:, g, n0 : n0 + COLS].bitcast(FP8X4),
-                    lhsT_scale=planes_u8[:, 2 * J + g * N + n0 : 2 * J + g * N + n0 + COLS],
+                    lhsT_scale=al8_planes[:, g, n0 : n0 + COLS],
                     rhs=h_codes[hf, g][:].bitcast(FP8X4),
                     rhs_scale=h_scales[hf, g][:],
                     start=(g == 0),
@@ -225,7 +224,7 @@ def tile_list_kernl_sigm_res_silu_kernel(
                 nc.tensor.matmul_mx(
                     y_banks[hf, c][:, cols],
                     lhsT=al4_codes[:, g, n0 // 2 : (n0 + COLS) // 2].bitcast(FP4X4),
-                    lhsT_scale=planes_u8[:, J + g * N + n0 : J + g * N + n0 + COLS],
+                    lhsT_scale=al4_planes[:, g, n0 : n0 + COLS],
                     rhs=h_codes[hf, g][:, cols].bitcast(FP8X4),
                     rhs_scale=h_scales[hf, g][:, cols],
                     start=False,
@@ -241,9 +240,11 @@ def tile_list_kernl_sigm_res_silu_kernel(
 
         for hf in range(2):
             for g in range(2):
-                for a in range(2):
-                    for pair in range(2):
-                        first_product(hf, g, pair, a)
+                steps = [(pair, a) for pair in range(2) for a in range(2)]
+                if hf == 0 and g == 0:
+                    steps = [(pair, a) for a in range(2) for pair in range(2)]
+                for pair, a in steps:
+                    first_product(hf, g, pair, a)
                 sigmoids(hf, g)
         weigh(0, 0)
         weigh(0, 1)

@@ -49,14 +49,17 @@ def tile_list_kernl_sigm_res_silu_kernel(
             rows = x[a * KP : (a + 1) * KP, hf * HALF : (hf + 1) * HALF]
             nc.sync.dma_start(tile, rows.rearrange("(p i) m -> p i m", i=PACK))
 
-        load_x(0, 0, sb([P, PACK, HALF], F32, "x_first")[:])
+        x_first = sb([P, PACK, M], F32, "x_first")
+        nc.sync.dma_start(x_first[:], x[KP : 2 * KP, :].rearrange("(p i) m -> p i m", i=PACK))
+        for hf in range(2):
+            x_raw[1, hf] = x_first[:, :, hf * HALF : (hf + 1) * HALF]
 
-        warm_in = placed([P, 32], F32, "warm_in", 20480 - 64)
-        nc.gpsimd.memset(warm_in[:], 0.0)
+        warm_in = placed([P, 5 * 1024 + 32], F32, "warm_in", 4096 - 128)
+        nc.vector.memset(warm_in[:, 0:32], 0.0)
         warm_out = sb([P, 32], F32, "warm_out")
-        nc.scalar.activation(warm_out[:], warm_in[:], ACT.Sigmoid)
+        nc.scalar.activation(warm_out[:], warm_in[:, 0:32], ACT.Sigmoid)
 
-        scale_window = placed([P, T // 4], I32, "scale_window", 0)
+        scale_window = placed([P, T // 4], I32, "scale_window", 40960)
         nc.vector.memset(scale_window[:], 0)
         tab_plane1 = sb([P, J // 4], I32, "tab_plane1")
         nc.vector.memset(tab_plane1[:], 0)
@@ -68,37 +71,34 @@ def tile_list_kernl_sigm_res_silu_kernel(
 
         word_window = placed([P, T], I32, "word_window", 4096)
         nc.sync.dma_start(word_window[:], tab_words[0].rearrange("p t b -> p (t b)").bitcast(I32))
-        x_rest = placed([P, 3, PACK, HALF], F32, "x_rest", 20480)
-        load_x(1, 0, x_rest[:, 0])
-        load_x(0, 1, x_rest[:, 1])
-        load_x(1, 1, x_rest[:, 2])
-
-        picked_scales = sb([P, J], U8, "picked_scales")
-        nc.vector.tensor_copy(picked_scales[:], scale_window[:].bitcast(U8).indirect(offsets[:]))
-        cb_sb = placed([P, 2, PACK], F32, "cb_sb", 2048)
-        cw_sb = placed([P, 2, PACK], F32, "cw_sb", 2048 + 64)
-        b_sb = placed([P, N // P], F32, "b_sb", 2048 + 128)
-        nc.scalar.dma_start(cb_sb[:], cb.rearrange("(a p t) -> p a t", a=2, t=PACK))
+        load_x(0, 0, placed([P, PACK, HALF], F32, "x_00", 20480)[:])
+        cb_sb = placed([P, 2, PACK], F32, "cb_sb", 4096 - 128)
+        cw_sb = placed([P, 2, PACK], F32, "cw_sb", 4096 - 64)
+        nc.sync.dma_start(cb_sb[:], cb.rearrange("(a p t) -> p a t", a=2, t=PACK))
         nc.sync.dma_start(cw_sb[:], cw.rearrange("(a p t) -> p a t", a=2, t=PACK))
-        with nc.allow_non_contiguous_dma(reason="one bias value to a partition"):
-            nc.sync.dma_start(b_sb[:], b.rearrange("(c p) -> p c", p=P))
+
+        picked_scales = placed([P, 12 * J], U8, "picked_scales", 24576)
+        nc.vector.tensor_copy(picked_scales[:, 0:J], scale_window[:].bitcast(U8).indirect(offsets[:]))
         tab_plane0 = sb([P, J], U8, "tab_plane0")
         nc.vector.tensor_copy(
             tab_plane0[:].rearrange("p (t c i) -> p c t i", t=PACK, i=16),
-            picked_scales[:].rearrange("p (c i t) -> p c t i", t=PACK, i=16),
+            picked_scales[:, 0:J].rearrange("p (c i t) -> p c t i", t=PACK, i=16),
         )
         nc.scalar.dma_start(tab_plane1[0 : P - SHIFT, :], tab_plane0[:].bitcast(I32)[SHIFT:P, :])
         tab_planes = (tab_plane0[:], tab_plane1[:].bitcast(U8))
+        load_x(0, 1, placed([P, PACK, HALF], F32, "x_01", 24576)[:])
 
-        al_planes = placed([P, 2, 2, N // 4], I32, "al_planes", 0)
-        nc.vector.memset(al_planes[:], 0)
-        for w, scales in enumerate((al8_scales, al4_scales)):
-            for r in range(4):
-                nc.sync.dma_start(
-                    al_planes[r:P:32, w], scales.bitcast(I32)[:, r:16:4, :].rearrange("a q n -> q a n")
-                )
-        al8_planes = al_planes[:, 0].bitcast(U8)
-        al4_planes = al_planes[:, 1].bitcast(U8)
+        al_planes = {}
+
+        def load_al_planes():
+            planes = sb([P, 2, 2, N // 4], I32, "al_planes", tag="x_bf16_11")
+            nc.gpsimd.memset(planes[:], 0)
+            for w, scales in enumerate((al8_scales, al4_scales)):
+                al_planes[w] = planes[:, w].bitcast(U8)
+                for r in range(4):
+                    nc.sync.dma_start(
+                        planes[r:P:32, w], scales.bitcast(I32)[:, r:16:4, :].rearrange("a q n -> q a n")
+                    )
 
         x_bf16, x_codes, x_scales = {}, {}, {}
 
@@ -109,14 +109,16 @@ def tile_list_kernl_sigm_res_silu_kernel(
                 x_raw[a, hf].rearrange("p t (c i) -> p c t i", i=2),
             )
 
-        def quantize(src, name):
-            codes = sb([P, HALF], U32, name + "_codes")
+        def quantize(src, name, offset=None):
+            codes = sb([P, HALF], U32, name) if offset is None else placed([P, HALF], U32, name, offset)
             scales = sb([P, HALF], U8, name + "_scales")
             nc.vector.quantize_mx(codes[:].bitcast(FP8X4), scales[:], src[:].rearrange("p m t -> p (m t)"))
             return codes, scales
 
         def quantize_x(a, hf):
-            x_codes[a, hf], x_scales[a, hf] = quantize(x_bf16[a, hf], "x%d%d" % (a, hf))
+            x_codes[a, hf], x_scales[a, hf] = quantize(
+                x_bf16[a, hf], "x%d%d" % (a, hf), 34816 + 1024 * hf if a == 1 else None
+            )
 
         picked_words, tab_codes = {}, {}
 
@@ -127,62 +129,78 @@ def tile_list_kernl_sigm_res_silu_kernel(
             )
 
         def part_words(g):
-            tab_codes[g] = sb([P, 2 * PACK * 2 * COLS], U8, "tab_codes%d" % g)
+            tab_codes[g] = sb([P, 2 * PACK * 2 * COLS], U8, "tab_codes%d" % g, tag=("tab_codes0", "x_bf16_00")[g])
             parted = tab_codes[g][:].bitcast(U16).rearrange("p (a t c i) -> p a c t i", a=2, t=PACK, i=4)
             paired = picked_words[g][:].bitcast(U16).rearrange("p (c i t a) -> p a c t i", a=2, t=PACK, i=4)
-            for a in range(2):
+            for a in (1, 0):
                 nc.vector.tensor_copy(parted[:, a], paired[:, a])
 
-        interleave_x(0, 0, nc.scalar.copy)
-        quantize_x(0, 0)
+        for hf in range(2):
+            interleave_x(1, hf, nc.scalar.copy)
+            quantize_x(1, hf)
+        load_al_planes()
+        warm_bank = psum.tile([P, 2 * HALF], F32, name="warm_bank", tag="bank7")
+        for n in range(6):
+            nc.tensor.matmul_mx(
+                warm_bank[:, (n % 2) * HALF : (n % 2 + 1) * HALF],
+                lhsT=x_codes[1, 1][:, 0:COLS].bitcast(FP8X4),
+                lhsT_scale=x_scales[1, 1][:, 0:COLS],
+                rhs=x_codes[1, 1][:].bitcast(FP8X4),
+                rhs_scale=x_scales[1, 1][:],
+                start=True,
+                stop=True,
+            )
         gather_words(0)
         part_words(0)
-        interleave_x(1, 0, nc.scalar.copy)
+        interleave_x(0, 0, nc.scalar.copy)
         gather_words(1)
-        quantize_x(1, 0)
+        quantize_x(0, 0)
         part_words(1)
         interleave_x(0, 1, nc.scalar.copy)
         quantize_x(0, 1)
-        interleave_x(1, 1, nc.vector.tensor_copy)
-        quantize_x(1, 1)
 
         al8_codes = placed([P, 2, N], I32, "al8_codes", 4096)
         nc.sync.dma_start(al8_codes[:], al8_words.rearrange("a p n i -> p a (n i)").bitcast(I32))
-        al4_codes = sb([P, 2, N // 2], I32, "al4_codes", tag="x_bf16_10")
+        al4_codes = placed([P, 2, N // 2], I32, "al4_codes", 8192)
         nc.sync.dma_start(al4_codes[:], al4_words.rearrange("a p n -> p a n").bitcast(I32))
+        b_sb = placed([P, N // P], F32, "b_sb", 12288)
+        with nc.allow_non_contiguous_dma(reason="one bias value to a partition"):
+            nc.sync.dma_start(b_sb[:], b.rearrange("(c p) -> p c", p=P))
 
         def bank(index, name):
             return psum.tile([P, 2 * HALF], F32, name=name, tag="bank%d" % index)
 
         d_banks = {}
 
-        def first_product(hf, g, pair, a):
-            if a == 0:
-                d_banks[hf, g, pair] = bank(4 * hf + 2 * g + pair, "d%d%d%d" % (hf, g, pair))
-            for u in range(2):
-                t = 2 * pair + u
-                codes = tab_codes[g][:, (a * PACK + t) * 2 * COLS : (a * PACK + t + 1) * 2 * COLS]
-                scales = tab_planes[a][:, (2 * t + g) * COLS : (2 * t + g + 1) * COLS]
-                for q in range(2):
-                    cols = slice(q * COLS, (q + 1) * COLS)
+        def first_product(hf, g, a):
+            for q in range(2):
+                cols = slice(q * COLS, (q + 1) * COLS)
+                for t in range(PACK):
+                    if a == 1 and q == 0:
+                        d_banks[hf, g, t] = bank(PACK * g + t, "d%d%d%d" % (hf, g, t))
+                    codes = tab_codes[g][:, (a * PACK + t) * 2 * COLS : (a * PACK + t + 1) * 2 * COLS]
                     nc.tensor.matmul_mx(
-                        d_banks[hf, g, pair][:, u * HALF + q * COLS : u * HALF + (q + 1) * COLS],
+                        d_banks[hf, g, t][:, cols],
                         lhsT=codes.bitcast(FP4X4),
-                        lhsT_scale=scales,
+                        lhsT_scale=tab_planes[a][:, (2 * t + g) * COLS : (2 * t + g + 1) * COLS],
                         rhs=x_codes[a, hf][:, cols].bitcast(FP8X4),
                         rhs_scale=x_scales[a, hf][:, cols],
-                        start=(a == 0 and u == 0 and q == 0),
-                        stop=(a == 1 and u == 1 and q == 1),
+                        start=(a == 1 and q == 0),
+                        stop=(a == 0 and q == 1),
                     )
 
         logistic, h_bf16, h_codes, h_scales = {}, {}, {}, {}
 
         def sigmoids(hf, g):
-            logistic[hf, g] = sb([P, PACK, HALF], F32, "logistic%d%d" % (hf, g))
+            name = "logistic%d%d" % (hf, g)
+            if hf == 0:
+                logistic[hf, g] = placed([P, PACK, HALF], F32, name, 22528 + 4096 * g)
+            else:
+                logistic[hf, g] = sb([P, PACK, HALF], F32, name)
             for t in range(PACK):
                 nc.scalar.activation(
                     logistic[hf, g][:, t, :],
-                    d_banks[hf, g, t // 2][:, (t % 2) * HALF : (t % 2 + 1) * HALF],
+                    d_banks[hf, g, t][:, 0:HALF],
                     ACT.Sigmoid,
                     bias=cb_sb[:, g, t : t + 1],
                 )
@@ -210,7 +228,7 @@ def tile_list_kernl_sigm_res_silu_kernel(
                 nc.tensor.matmul_mx(
                     y_banks[hf, c][:, 0:HALF],
                     lhsT=al8_codes[:, g, n0 : n0 + COLS].bitcast(FP8X4),
-                    lhsT_scale=al8_planes[:, g, n0 : n0 + COLS],
+                    lhsT_scale=al_planes[0][:, g, n0 : n0 + COLS],
                     rhs=h_codes[hf, g][:].bitcast(FP8X4),
                     rhs_scale=h_scales[hf, g][:],
                     start=(g == 0),
@@ -224,7 +242,7 @@ def tile_list_kernl_sigm_res_silu_kernel(
                 nc.tensor.matmul_mx(
                     y_banks[hf, c][:, cols],
                     lhsT=al4_codes[:, g, n0 // 2 : (n0 + COLS) // 2].bitcast(FP4X4),
-                    lhsT_scale=al4_planes[:, g, n0 : n0 + COLS],
+                    lhsT_scale=al_planes[1][:, g, n0 : n0 + COLS],
                     rhs=h_codes[hf, g][:, cols].bitcast(FP8X4),
                     rhs_scale=h_scales[hf, g][:, cols],
                     start=False,
@@ -240,22 +258,13 @@ def tile_list_kernl_sigm_res_silu_kernel(
 
         for hf in range(2):
             for g in range(2):
-                steps = [(pair, a) for pair in range(2) for a in range(2)]
-                if hf == 0 and g == 0:
-                    steps = [(pair, a) for a in range(2) for pair in range(2)]
-                for pair, a in steps:
-                    first_product(hf, g, pair, a)
+                first_product(hf, g, 1)
+                first_product(hf, g, 0)
                 sigmoids(hf, g)
-        weigh(0, 0)
-        weigh(0, 1)
-        quantize_h(0, 0)
-        quantize_h(0, 1)
-        weigh(1, 0)
-        quantize_h(1, 0)
-        weigh(1, 1)
-        quantize_h(1, 1)
         for hf in range(2):
             for g in range(2):
+                weigh(hf, g)
+                quantize_h(hf, g)
                 for c in range(N // COLS):
                     second_product(hf, g, c)
         for hf in range(2):

@@ -105,8 +105,8 @@ def tile_list_kernl_sigm_res_silu_kernel(
         def interleave_x(a, hf, copy):
             x_bf16[a, hf] = sb([P, HALF, PACK], BF16, "x_bf16_%d%d" % (a, hf))
             copy(
-                x_bf16[a, hf][:].rearrange("p (c i) t -> p c t i", i=2),
-                x_raw[a, hf].rearrange("p t (c i) -> p c t i", i=2),
+                x_bf16[a, hf][:].rearrange("p (c i) t -> p c t i", i=4),
+                x_raw[a, hf].rearrange("p t (c i) -> p c t i", i=4),
             )
 
         def quantize(src, name, offset=None):
@@ -194,13 +194,13 @@ def tile_list_kernl_sigm_res_silu_kernel(
         def sigmoids(hf, g):
             name = "logistic%d%d" % (hf, g)
             if hf == 0:
-                logistic[hf, g] = placed([P, PACK, HALF], F32, name, 22528 + 4096 * g)
+                logistic[hf, g] = placed([P, HALF // 4, PACK, 4], F32, name, 22528 + 4096 * g)
             else:
-                logistic[hf, g] = sb([P, PACK, HALF], F32, name)
+                logistic[hf, g] = sb([P, HALF // 4, PACK, 4], F32, name)
             for t in range(PACK):
                 nc.scalar.activation(
-                    logistic[hf, g][:, t, :],
-                    d_banks[hf, g, t][:, 0:HALF],
+                    logistic[hf, g][:, :, t, :],
+                    d_banks[hf, g, t][:, 0:HALF].rearrange("p (c i) -> p c i", i=4),
                     ACT.Sigmoid,
                     bias=cb_sb[:, g, t : t + 1],
                 )
@@ -208,9 +208,9 @@ def tile_list_kernl_sigm_res_silu_kernel(
         def weigh(hf, g):
             h_bf16[hf, g] = sb([P, HALF, PACK], BF16, "h_bf16_%d%d" % (hf, g), tag="h_bf16_%d" % min(2 * hf + g, 2))
             nc.vector.tensor_tensor(
-                h_bf16[hf, g][:].rearrange("p (c i) t -> p c t i", i=2),
-                logistic[hf, g][:].rearrange("p t (c i) -> p c t i", i=2),
-                cw_sb[:, g, :].unsqueeze(1).unsqueeze(3).to_broadcast([P, HALF // 2, PACK, 2]),
+                h_bf16[hf, g][:].rearrange("p (c i) t -> p c t i", i=4),
+                logistic[hf, g][:],
+                cw_sb[:, g, :].unsqueeze(1).unsqueeze(3).to_broadcast([P, HALF // 4, PACK, 4]),
                 ALU.mult,
             )
 

@@ -49,56 +49,25 @@ def tile_list_kernl_sigm_res_silu_kernel(
             rows = x[a * KP : (a + 1) * KP, hf * HALF : (hf + 1) * HALF]
             nc.sync.dma_start(tile, rows.rearrange("(p i) m -> p i m", i=PACK))
 
-        x_first = sb([P, PACK, M], F32, "x_first")
-        nc.sync.dma_start(x_first[:], x[KP : 2 * KP, :].rearrange("(p i) m -> p i m", i=PACK))
+        x_first = placed([P, PACK, M], F32, "x_first", 61440)
+        nc.sync.dma_start(x_first[:], x[0:KP, :].rearrange("(p i) m -> p i m", i=PACK))
         for hf in range(2):
-            x_raw[1, hf] = x_first[:, :, hf * HALF : (hf + 1) * HALF]
+            x_raw[0, hf] = x_first[:, :, hf * HALF : (hf + 1) * HALF]
 
-        warm_in = placed([P, 5 * 1024 + 32], F32, "warm_in", 4096 - 128)
+        warm_in = placed([P, 7 * 1024 + 32], F32, "warm_in", 4096)
         nc.vector.memset(warm_in[:, 0:32], 0.0)
         warm_out = sb([P, 32], F32, "warm_out")
         nc.scalar.activation(warm_out[:], warm_in[:, 0:32], ACT.Sigmoid)
 
-        scale_window = placed([P, T // 4], I32, "scale_window", 40960)
+        scale_window = placed([P, T // 4], I32, "scale_window", 49152)
         nc.vector.memset(scale_window[:], 0)
-        tab_plane1 = sb([P, J // 4], I32, "tab_plane1")
-        nc.vector.memset(tab_plane1[:], 0)
-        tab_scales_i32 = tab_scales.bitcast(I32)
-        for r in range(4):
-            nc.sync.dma_start(
-                scale_window[r:P:SHIFT, :], tab_scales_i32[:, r:16:4, :].rearrange("a q n -> q a n")
-            )
+        for a in range(2):
+            nc.sync.dma_start(scale_window[4 * a : P : 8, :], tab_scales[a].bitcast(I32))
 
         word_window = placed([P, T], I32, "word_window", 4096)
         nc.sync.dma_start(word_window[:], tab_words[0].rearrange("p t b -> p (t b)").bitcast(I32))
-        load_x(0, 0, placed([P, PACK, HALF], F32, "x_00", 20480)[:])
-        cb_sb = placed([P, 2, PACK], F32, "cb_sb", 4096 - 128)
-        cw_sb = placed([P, 2, PACK], F32, "cw_sb", 4096 - 64)
-        nc.sync.dma_start(cb_sb[:], cb.rearrange("(a p t) -> p a t", a=2, t=PACK))
-        nc.sync.dma_start(cw_sb[:], cw.rearrange("(a p t) -> p a t", a=2, t=PACK))
-
-        picked_scales = placed([P, 12 * J], U8, "picked_scales", 24576)
-        nc.vector.tensor_copy(picked_scales[:, 0:J], scale_window[:].bitcast(U8).indirect(offsets[:]))
-        tab_plane0 = sb([P, J], U8, "tab_plane0")
-        nc.vector.tensor_copy(
-            tab_plane0[:].rearrange("p (t c i) -> p c t i", t=PACK, i=16),
-            picked_scales[:, 0:J].rearrange("p (c i t) -> p c t i", t=PACK, i=16),
-        )
-        nc.scalar.dma_start(tab_plane1[0 : P - SHIFT, :], tab_plane0[:].bitcast(I32)[SHIFT:P, :])
-        tab_planes = (tab_plane0[:], tab_plane1[:].bitcast(U8))
-        load_x(0, 1, placed([P, PACK, HALF], F32, "x_01", 24576)[:])
-
-        al_planes = {}
-
-        def load_al_planes():
-            planes = sb([P, 2, 2, N // 4], I32, "al_planes", tag="x_bf16_11")
-            nc.gpsimd.memset(planes[:], 0)
-            for w, scales in enumerate((al8_scales, al4_scales)):
-                al_planes[w] = planes[:, w].bitcast(U8)
-                for r in range(4):
-                    nc.sync.dma_start(
-                        planes[r:P:32, w], scales.bitcast(I32)[:, r:16:4, :].rearrange("a q n -> q a n")
-                    )
+        load_x(1, 0, placed([P, PACK, HALF], F32, "x_10", 20480)[:])
+        load_x(1, 1, placed([P, PACK, HALF], F32, "x_11", 32768)[:])
 
         x_bf16, x_codes, x_scales = {}, {}, {}
 
@@ -109,55 +78,88 @@ def tile_list_kernl_sigm_res_silu_kernel(
                 x_raw[a, hf].rearrange("p t (c i) -> p c t i", i=4),
             )
 
-        def quantize(src, name, offset=None):
-            codes = sb([P, HALF], U32, name) if offset is None else placed([P, HALF], U32, name, offset)
-            scales = sb([P, HALF], U8, name + "_scales")
-            nc.vector.quantize_mx(codes[:].bitcast(FP8X4), scales[:], src[:].rearrange("p m t -> p (m t)"))
-            return codes, scales
+        for hf in range(2):
+            interleave_x(0, hf, nc.scalar.copy)
+
+        picked_scales = placed([P, 2 * J], U8, "picked_scales", 40960 - J)
+        nc.vector.tensor_copy(picked_scales[:, 0:J], scale_window[:].bitcast(U8).indirect(offsets[:]))
+        tab_plane0 = placed([P, J // 4], I32, "tab_plane0", 61440)
+        tab_plane1 = placed([P, J // 4], I32, "tab_plane1", 61440 + J)
+        nc.gpsimd.memset(tab_plane1[:], 0)
+        nc.vector.tensor_copy(
+            tab_plane0[:].bitcast(U8).rearrange("p (t c i) -> p c t i", t=PACK, i=16),
+            picked_scales[:, 0:J].rearrange("p (c i t) -> p c t i", t=PACK, i=16),
+        )
+        for r in range(1, 4):
+            nc.scalar.dma_start(tab_plane0[r:P:32, :], tab_plane0[8 * r : P : 32, :])
+        for r in range(4):
+            queue = nc.gpsimd if r == 3 else nc.scalar
+            queue.dma_start(tab_plane1[r:P:32, :], tab_plane0[8 * r + 4 : P : 32, :])
+        tab_planes = (tab_plane0[:].bitcast(U8), tab_plane1[:].bitcast(U8))
+
+        al_planes = {}
+
+        def load_al_planes():
+            planes = sb([P, 2, 2, N // 4], I32, "al_planes", tag="x_bf16_01")
+            nc.gpsimd.memset(planes[:], 0)
+            for w, scales in enumerate((al8_scales, al4_scales)):
+                al_planes[w] = planes[:, w].bitcast(U8)
+                for r in range(4):
+                    nc.sync.dma_start(
+                        planes[r:P:32, w], scales.bitcast(I32)[:, r:16:4, :].rearrange("a q n -> q a n")
+                    )
+
+        def quantize(src, codes, scales):
+            nc.vector.quantize_mx(codes.bitcast(FP8X4), scales, src[:].rearrange("p m t -> p (m t)"))
 
         def quantize_x(a, hf):
-            x_codes[a, hf], x_scales[a, hf] = quantize(
-                x_bf16[a, hf], "x%d%d" % (a, hf), 34816 + 1024 * hf if a == 1 else None
-            )
+            if hf == 0:
+                x_codes[a] = placed([P, M], U32, "x_codes%d" % a, (40960, 55296)[a])
+                x_scales[a] = sb([P, M], U8, "x_scales%d" % a)
+            cols = slice(hf * HALF, (hf + 1) * HALF)
+            quantize(x_bf16[a, hf], x_codes[a][:, cols], x_scales[a][:, cols])
 
         picked_words, tab_codes = {}, {}
 
         def gather_words(g):
-            picked_words[g] = sb([P, KP], U32, "picked_words%d" % g, tag="picked_words")
+            picked_words[g] = placed([P, (2 - g) * KP], U32, "picked_words%d" % g, (53248, 22528)[g])[:, 0:KP]
             nc.vector.tensor_copy(
-                picked_words[g][:], word_window[:].bitcast(U32).indirect(offsets[:, 32 * g : 32 * (g + 1)])
+                picked_words[g], word_window[:].bitcast(U32).indirect(offsets[:, 32 * g : 32 * (g + 1)])
             )
 
         def part_words(g):
-            tab_codes[g] = sb([P, 2 * PACK * 2 * COLS], U8, "tab_codes%d" % g, tag=("tab_codes0", "x_bf16_00")[g])
+            tab_codes[g] = placed([P, 2 * PACK * 2 * COLS], U8, "tab_codes%d" % g, (57344, 32896)[g])
             parted = tab_codes[g][:].bitcast(U16).rearrange("p (a t c i) -> p a c t i", a=2, t=PACK, i=4)
-            paired = picked_words[g][:].bitcast(U16).rearrange("p (c i t a) -> p a c t i", a=2, t=PACK, i=4)
-            for a in (1, 0):
+            paired = picked_words[g].bitcast(U16).rearrange("p (c i t a) -> p a c t i", a=2, t=PACK, i=4)
+            for a in range(2):
                 nc.vector.tensor_copy(parted[:, a], paired[:, a])
 
         for hf in range(2):
-            interleave_x(1, hf, nc.scalar.copy)
-            quantize_x(1, hf)
+            quantize_x(0, hf)
+        cb_cw = sb([P, 2, 2, PACK], F32, "cb_cw", tag="x_bf16_00")
+        cb_sb, cw_sb = cb_cw[:, 0], cb_cw[:, 1]
+        nc.sync.dma_start(cb_sb, cb.rearrange("(a p t) -> p a t", a=2, t=PACK))
+        nc.sync.dma_start(cw_sb, cw.rearrange("(a p t) -> p a t", a=2, t=PACK))
         load_al_planes()
         warm_bank = psum.tile([P, 2 * HALF], F32, name="warm_bank", tag="bank7")
         for n in range(6):
             nc.tensor.matmul_mx(
                 warm_bank[:, (n % 2) * HALF : (n % 2 + 1) * HALF],
-                lhsT=x_codes[1, 1][:, 0:COLS].bitcast(FP8X4),
-                lhsT_scale=x_scales[1, 1][:, 0:COLS],
-                rhs=x_codes[1, 1][:].bitcast(FP8X4),
-                rhs_scale=x_scales[1, 1][:],
+                lhsT=x_codes[0][:, HALF : HALF + COLS].bitcast(FP8X4),
+                lhsT_scale=x_scales[0][:, HALF : HALF + COLS],
+                rhs=x_codes[0][:, HALF:M].bitcast(FP8X4),
+                rhs_scale=x_scales[0][:, HALF:M],
                 start=True,
                 stop=True,
             )
         gather_words(0)
         part_words(0)
-        interleave_x(0, 0, nc.scalar.copy)
+        interleave_x(1, 0, nc.scalar.copy)
+        quantize_x(1, 0)
         gather_words(1)
-        quantize_x(0, 0)
+        interleave_x(1, 1, nc.scalar.copy)
+        quantize_x(1, 1)
         part_words(1)
-        interleave_x(0, 1, nc.scalar.copy)
-        quantize_x(0, 1)
 
         al8_codes = placed([P, 2, N], I32, "al8_codes", 4096)
         nc.sync.dma_start(al8_codes[:], al8_words.rearrange("a p n i -> p a (n i)").bitcast(I32))
@@ -170,103 +172,108 @@ def tile_list_kernl_sigm_res_silu_kernel(
         def bank(index, name):
             return psum.tile([P, 2 * HALF], F32, name=name, tag="bank%d" % index)
 
-        d_banks = {}
+        d = {}
 
-        def first_product(hf, g, a):
-            for q in range(2):
-                cols = slice(q * COLS, (q + 1) * COLS)
-                for t in range(PACK):
-                    if a == 1 and q == 0:
-                        d_banks[hf, g, t] = bank(PACK * g + t, "d%d%d%d" % (hf, g, t))
-                    codes = tab_codes[g][:, (a * PACK + t) * 2 * COLS : (a * PACK + t + 1) * 2 * COLS]
-                    nc.tensor.matmul_mx(
-                        d_banks[hf, g, t][:, cols],
-                        lhsT=codes.bitcast(FP4X4),
-                        lhsT_scale=tab_planes[a][:, (2 * t + g) * COLS : (2 * t + g + 1) * COLS],
-                        rhs=x_codes[a, hf][:, cols].bitcast(FP8X4),
-                        rhs_scale=x_scales[a, hf][:, cols],
-                        start=(a == 1 and q == 0),
-                        stop=(a == 0 and q == 1),
-                    )
+        def first_product(g, target, m0, width, step):
+            for a in range(2):
+                for q0 in range(0, width, step):
+                    cols = slice(m0 + q0, m0 + q0 + step)
+                    for t in range(PACK):
+                        codes = tab_codes[g][:, (a * PACK + t) * 2 * COLS : (a * PACK + t + 1) * 2 * COLS]
+                        nc.tensor.matmul_mx(
+                            target[t][:, q0 : q0 + step],
+                            lhsT=codes.bitcast(FP4X4),
+                            lhsT_scale=tab_planes[a][:, (2 * t + g) * COLS : (2 * t + g + 1) * COLS],
+                            rhs=x_codes[a][:, cols].bitcast(FP8X4),
+                            rhs_scale=x_scales[a][:, cols],
+                            start=(a == 0 and q0 == 0),
+                            stop=(a == 1 and q0 + step == width),
+                        )
 
         logistic, h_bf16, h_codes, h_scales = {}, {}, {}, {}
 
         def sigmoids(hf, g):
             name = "logistic%d%d" % (hf, g)
-            if hf == 0:
-                logistic[hf, g] = placed([P, HALF // 4, PACK, 4], F32, name, 22528 + 4096 * g)
+            if (hf, g) == (0, 0):
+                logistic[hf, g] = placed([P, HALF // 4, PACK, 4], F32, name, 28736)
             else:
                 logistic[hf, g] = sb([P, HALF // 4, PACK, 4], F32, name)
             for t in range(PACK):
                 nc.scalar.activation(
                     logistic[hf, g][:, :, t, :],
-                    d_banks[hf, g, t][:, 0:HALF].rearrange("p (c i) -> p c i", i=4),
+                    d[hf, g][t].rearrange("p (c i) -> p c i", i=4),
                     ACT.Sigmoid,
                     bias=cb_sb[:, g, t : t + 1],
                 )
 
-        def weigh(hf, g):
-            h_bf16[hf, g] = sb([P, HALF, PACK], BF16, "h_bf16_%d%d" % (hf, g), tag="h_bf16_%d" % min(2 * hf + g, 2))
+        def weigh(hf, g, m0, width):
+            key = (hf, g, m0)
+            h_bf16[key] = sb([P, width, PACK], BF16, "h_bf16_%d%d_%d" % key, tag="h_bf16_%d_%d" % (hf, m0))
             nc.vector.tensor_tensor(
-                h_bf16[hf, g][:].rearrange("p (c i) t -> p c t i", i=4),
-                logistic[hf, g][:],
-                cw_sb[:, g, :].unsqueeze(1).unsqueeze(3).to_broadcast([P, HALF // 4, PACK, 4]),
+                h_bf16[key][:].rearrange("p (c i) t -> p c t i", i=4),
+                logistic[hf, g][:, m0 // 4 : (m0 + width) // 4],
+                cw_sb[:, g, :].unsqueeze(1).unsqueeze(3).to_broadcast([P, width // 4, PACK, 4]),
                 ALU.mult,
             )
 
-        def quantize_h(hf, g):
-            h_codes[hf, g], h_scales[hf, g] = quantize(h_bf16[hf, g], "h%d%d" % (hf, g))
+        def quantize_h(hf, g, m0, width):
+            key = (hf, g, m0)
+            name = "h%d%d_%d" % key
+            h_codes[key] = sb([P, width], U32, name + "_codes")[:]
+            h_scales[key] = sb([P, width], U8, name + "_scales")[:]
+            quantize(h_bf16[key], h_codes[key], h_scales[key])
 
         y_banks = {}
 
-        def second_product(hf, g, c):
-            if g == 0:
-                y_banks[hf, c] = bank(4 * hf + c, "y%d%d" % (hf, c))
+        def second_product(hf, g, m0, width, c):
+            key = (hf, g, m0)
+            if g == 0 and c % 2 == 0:
+                pair = bank(PACK + 2 * hf + c // 2, "y%d%d" % (hf, c))
+                y_banks[hf, c], y_banks[hf, c + 1] = pair[:, 0:HALF], pair[:, HALF:M]
             n0 = c * COLS
-
-            def tier8():
+            nc.tensor.matmul_mx(
+                y_banks[hf, c][:, m0 : m0 + width],
+                lhsT=al8_codes[:, g, n0 : n0 + COLS].bitcast(FP8X4),
+                lhsT_scale=al_planes[0][:, g, n0 : n0 + COLS],
+                rhs=h_codes[key].bitcast(FP8X4),
+                rhs_scale=h_scales[key],
+                start=(g == 0 and c % 2 == 0),
+                stop=False,
+            )
+            for q0 in range(0, width, COLS):
                 nc.tensor.matmul_mx(
-                    y_banks[hf, c][:, 0:HALF],
-                    lhsT=al8_codes[:, g, n0 : n0 + COLS].bitcast(FP8X4),
-                    lhsT_scale=al_planes[0][:, g, n0 : n0 + COLS],
-                    rhs=h_codes[hf, g][:].bitcast(FP8X4),
-                    rhs_scale=h_scales[hf, g][:],
-                    start=(g == 0),
-                    stop=(g == 1),
-                )
-
-            if g == 0:
-                tier8()
-            for q in range(2):
-                cols = slice(q * COLS, (q + 1) * COLS)
-                nc.tensor.matmul_mx(
-                    y_banks[hf, c][:, cols],
+                    y_banks[hf, c][:, m0 + q0 : m0 + q0 + COLS],
                     lhsT=al4_codes[:, g, n0 // 2 : (n0 + COLS) // 2].bitcast(FP4X4),
                     lhsT_scale=al_planes[1][:, g, n0 : n0 + COLS],
-                    rhs=h_codes[hf, g][:, cols].bitcast(FP8X4),
-                    rhs_scale=h_scales[hf, g][:, cols],
+                    rhs=h_codes[key][:, q0 : q0 + COLS].bitcast(FP8X4),
+                    rhs_scale=h_scales[key][:, q0 : q0 + COLS],
                     start=False,
-                    stop=False,
+                    stop=(g == 1 and c % 2 == 1 and m0 + q0 + COLS == HALF),
                 )
-            if g == 1:
-                tier8()
 
         def finish(hf, c):
             result = sb([P, HALF], F32, "result%d%d" % (hf, c))
-            nc.scalar.activation(result[:], y_banks[hf, c][:, 0:HALF], ACT.Silu, bias=b_sb[:, c : c + 1])
+            nc.scalar.activation(result[:], y_banks[hf, c], ACT.Silu, bias=b_sb[:, c : c + 1])
             nc.sync.dma_start(out[c * COLS : (c + 1) * COLS, hf * HALF : (hf + 1) * HALF], result[:])
 
         for hf in range(2):
-            for g in range(2):
-                first_product(hf, g, 1)
-                first_product(hf, g, 0)
-                sigmoids(hf, g)
+            banks = [bank(PACK * hf + t, "d0%d%d" % (hf, t)) for t in range(PACK)]
+            first_product(0, banks, hf * HALF, HALF, COLS)
+            d[hf, 0] = [banks[t][:, 0:HALF] for t in range(PACK)]
+            sigmoids(hf, 0)
+        banks = [bank(t, "d1%d" % t) for t in range(PACK)]
+        first_product(1, banks, 0, M, M)
         for hf in range(2):
-            for g in range(2):
-                weigh(hf, g)
-                quantize_h(hf, g)
-                for c in range(N // COLS):
-                    second_product(hf, g, c)
+            d[hf, 1] = [banks[t][:, hf * HALF : (hf + 1) * HALF] for t in range(PACK)]
+            sigmoids(hf, 1)
+        for g in range(2):
+            for hf in range(2):
+                width = COLS if (hf, g) == (1, 1) else HALF
+                for m0 in range(0, HALF, width):
+                    weigh(hf, g, m0, width)
+                    quantize_h(hf, g, m0, width)
+                    for c in range(N // COLS):
+                        second_product(hf, g, m0, width, c)
         for hf in range(2):
             for c in range(N // COLS):
                 finish(hf, c)

@@ -39,9 +39,6 @@ def tile_list_kernl_sigm_res_silu_kernel(
         def sb(shape, dtype, name, tag=None):
             return held.tile(shape, dtype, name=name, tag=tag or name, align_bytes=64)
 
-        offsets = held.tile([P, J // 16], U16, name="offsets")
-        nc.sync.dma_start(offsets[:], offs)
-
         x_raw = {}
 
         def load_x(a, hf, tile):
@@ -54,6 +51,9 @@ def tile_list_kernl_sigm_res_silu_kernel(
         for hf in range(2):
             x_raw[0, hf] = x_first[:, :, hf * HALF : (hf + 1) * HALF]
 
+        offsets = held.tile([P, J // 16], U16, name="offsets")
+        nc.sync.dma_start(offsets[:], offs)
+
         warm_in = placed([P, 7 * 1024 + 32], F32, "warm_in", 4096)
         nc.vector.memset(warm_in[:, 0:32], 0.0)
         warm_out = sb([P, 32], F32, "warm_out")
@@ -61,6 +61,8 @@ def tile_list_kernl_sigm_res_silu_kernel(
 
         scale_window = placed([P, T // 4], I32, "scale_window", 49152)
         nc.vector.memset(scale_window[:], 0)
+        tab_plane1 = sb([P, J // 4], I32, "tab_plane1")
+        nc.vector.memset(tab_plane1[:], 0)
         for a in range(2):
             nc.sync.dma_start(scale_window[4 * a : P : 8, :], tab_scales[a].bitcast(I32))
 
@@ -72,7 +74,11 @@ def tile_list_kernl_sigm_res_silu_kernel(
         x_bf16, x_codes, x_scales = {}, {}, {}
 
         def interleave_x(a, hf, copy):
-            x_bf16[a, hf] = sb([P, HALF, PACK], BF16, "x_bf16_%d%d" % (a, hf))
+            name = "x_bf16_%d%d" % (a, hf)
+            if (a, hf) == (0, 1):
+                x_bf16[a, hf] = placed([P, HALF, PACK], BF16, name, 73728 - 1024)
+            else:
+                x_bf16[a, hf] = sb([P, HALF, PACK], BF16, name)
             copy(
                 x_bf16[a, hf][:].rearrange("p (c i) t -> p c t i", i=4),
                 x_raw[a, hf].rearrange("p t (c i) -> p c t i", i=4),
@@ -84,8 +90,6 @@ def tile_list_kernl_sigm_res_silu_kernel(
         picked_scales = placed([P, 2 * J], U8, "picked_scales", 40960 - J)
         nc.vector.tensor_copy(picked_scales[:, 0:J], scale_window[:].bitcast(U8).indirect(offsets[:]))
         tab_plane0 = placed([P, J // 4], I32, "tab_plane0", 61440)
-        tab_plane1 = placed([P, J // 4], I32, "tab_plane1", 61440 + J)
-        nc.gpsimd.memset(tab_plane1[:], 0)
         nc.vector.tensor_copy(
             tab_plane0[:].bitcast(U8).rearrange("p (t c i) -> p c t i", t=PACK, i=16),
             picked_scales[:, 0:J].rearrange("p (c i t) -> p c t i", t=PACK, i=16),
@@ -100,8 +104,8 @@ def tile_list_kernl_sigm_res_silu_kernel(
         al_planes = {}
 
         def load_al_planes():
-            planes = sb([P, 2, 2, N // 4], I32, "al_planes", tag="x_bf16_01")
-            nc.gpsimd.memset(planes[:], 0)
+            planes = placed([P, 2, 2, N // 4], I32, "al_planes", 53248)
+            nc.vector.memset(planes[:], 0)
             for w, scales in enumerate((al8_scales, al4_scales)):
                 al_planes[w] = planes[:, w].bitcast(U8)
                 for r in range(4):
@@ -140,7 +144,10 @@ def tile_list_kernl_sigm_res_silu_kernel(
         cb_sb, cw_sb = cb_cw[:, 0], cb_cw[:, 1]
         nc.sync.dma_start(cb_sb, cb.rearrange("(a p t) -> p a t", a=2, t=PACK))
         nc.sync.dma_start(cw_sb, cw.rearrange("(a p t) -> p a t", a=2, t=PACK))
-        load_al_planes()
+        al8_codes = placed([P, 2, N], I32, "al8_codes", 69632)
+        nc.sync.dma_start(al8_codes[:], al8_words.rearrange("a p n i -> p a (n i)").bitcast(I32))
+        al4_codes = placed([P, 2, N // 2], I32, "al4_codes", 73728)
+        nc.sync.dma_start(al4_codes[:], al4_words.rearrange("a p n -> p a n").bitcast(I32))
         warm_bank = psum.tile([P, 2 * HALF], F32, name="warm_bank", tag="bank7")
         for n in range(6):
             nc.tensor.matmul_mx(
@@ -154,6 +161,7 @@ def tile_list_kernl_sigm_res_silu_kernel(
             )
         gather_words(0)
         part_words(0)
+        load_al_planes()
         interleave_x(1, 0, nc.scalar.copy)
         quantize_x(1, 0)
         gather_words(1)
@@ -161,10 +169,6 @@ def tile_list_kernl_sigm_res_silu_kernel(
         quantize_x(1, 1)
         part_words(1)
 
-        al8_codes = placed([P, 2, N], I32, "al8_codes", 4096)
-        nc.sync.dma_start(al8_codes[:], al8_words.rearrange("a p n i -> p a (n i)").bitcast(I32))
-        al4_codes = placed([P, 2, N // 2], I32, "al4_codes", 8192)
-        nc.sync.dma_start(al4_codes[:], al4_words.rearrange("a p n -> p a n").bitcast(I32))
         b_sb = placed([P, N // P], F32, "b_sb", 12288)
         with nc.allow_non_contiguous_dma(reason="one bias value to a partition"):
             nc.sync.dma_start(b_sb[:], b.rearrange("(c p) -> p c", p=P))
@@ -227,9 +231,8 @@ def tile_list_kernl_sigm_res_silu_kernel(
 
         def second_product(hf, g, m0, width, c):
             key = (hf, g, m0)
-            if g == 0 and c % 2 == 0:
-                pair = bank(PACK + 2 * hf + c // 2, "y%d%d" % (hf, c))
-                y_banks[hf, c], y_banks[hf, c + 1] = pair[:, 0:HALF], pair[:, HALF:M]
+            if g == 0:
+                y_banks[hf, c] = bank(PACK * (1 - hf) + c, "y%d%d" % (hf, c))[:, 0:HALF]
             n0 = c * COLS
             nc.tensor.matmul_mx(
                 y_banks[hf, c][:, m0 : m0 + width],
@@ -237,7 +240,7 @@ def tile_list_kernl_sigm_res_silu_kernel(
                 lhsT_scale=al_planes[0][:, g, n0 : n0 + COLS],
                 rhs=h_codes[key].bitcast(FP8X4),
                 rhs_scale=h_scales[key],
-                start=(g == 0 and c % 2 == 0),
+                start=(g == 0),
                 stop=False,
             )
             for q0 in range(0, width, COLS):
@@ -248,7 +251,7 @@ def tile_list_kernl_sigm_res_silu_kernel(
                     rhs=h_codes[key][:, q0 : q0 + COLS].bitcast(FP8X4),
                     rhs_scale=h_scales[key][:, q0 : q0 + COLS],
                     start=False,
-                    stop=(g == 1 and c % 2 == 1 and m0 + q0 + COLS == HALF),
+                    stop=(g == 1 and m0 + q0 + COLS == HALF),
                 )
 
         def finish(hf, c):

@@ -21,7 +21,7 @@ PACK = 4
 KP = P * PACK
 HALF = M // 2
 COLS = 128
-SHIFT = 16
+WARM_PASSES = 12
 
 
 def tile_list_kernl_sigm_res_silu_kernel(
@@ -39,6 +39,18 @@ def tile_list_kernl_sigm_res_silu_kernel(
         def sb(shape, dtype, name, tag=None):
             return held.tile(shape, dtype, name=name, tag=tag or name, align_bytes=64)
 
+        WORDS_AT, X11_AT, X01_AT, PLANES_AT, AL_AT = 0, 16384, 20480, 28672, 30720
+
+        offsets = held.tile([P, J // 16], U16, name="offsets")
+        nc.sync.dma_start(offsets[:], offs)
+        scale_window = sb([P, T // 4], I32, "scale_window")
+        nc.sync.dma_start(scale_window[0:32, :], tab_scales.rearrange("a q t -> (a q) t").bitcast(I32))
+        al8_rows = al8_words.rearrange("a p n i -> p a (n i)").bitcast(I32)
+        al8_head = sb([P, COLS], I32, "al8_head")
+        nc.sync.dma_start(al8_head[:], al8_rows[:, 0, 0:COLS])
+        word_window = placed([P, T], I32, "word_window", WORDS_AT)
+        nc.sync.dma_start(word_window[:], tab_words[0].rearrange("p t b -> p (t b)").bitcast(I32))
+
         x_raw = {}
 
         def load_x(a, hf, tile):
@@ -46,130 +58,115 @@ def tile_list_kernl_sigm_res_silu_kernel(
             rows = x[a * KP : (a + 1) * KP, hf * HALF : (hf + 1) * HALF]
             nc.sync.dma_start(tile, rows.rearrange("(p i) m -> p i m", i=PACK))
 
-        x_first = placed([P, PACK, M], F32, "x_first", 61440)
-        nc.sync.dma_start(x_first[:], x[0:KP, :].rearrange("(p i) m -> p i m", i=PACK))
-        for hf in range(2):
-            x_raw[0, hf] = x_first[:, :, hf * HALF : (hf + 1) * HALF]
+        load_x(0, 0, sb([P, PACK, HALF], F32, "x_00")[:])
+        load_x(1, 0, sb([P, PACK, HALF], F32, "x_10")[:])
 
-        offsets = held.tile([P, J // 16], U16, name="offsets")
-        nc.sync.dma_start(offsets[:], offs)
+        cb_sb = sb([P, 2, PACK], F32, "cb_sb")
+        cw_sb = sb([P, 2, PACK], F32, "cw_sb")
+        nc.scalar.dma_start(cb_sb[:], cb.rearrange("(a p t) -> p a t", a=2, t=PACK))
+        nc.scalar.dma_start(cw_sb[:], cw.rearrange("(a p t) -> p a t", a=2, t=PACK))
 
-        warm_in = placed([P, 7 * 1024 + 32], F32, "warm_in", 4096)
-        nc.vector.memset(warm_in[:, 0:32], 0.0)
+        warm_in = sb([P, 32], F32, "warm_in")
+        nc.vector.memset(warm_in[:], 0.0)
         warm_out = sb([P, 32], F32, "warm_out")
-        nc.scalar.activation(warm_out[:], warm_in[:, 0:32], ACT.Sigmoid)
+        nc.scalar.activation(warm_out[:], warm_in[:], ACT.Sigmoid)
 
-        scale_window = placed([P, T // 4], I32, "scale_window", 49152)
-        nc.vector.memset(scale_window[:], 0)
+        nc.vector.memset(scale_window[32:64, :], 0)
+        nc.vector.memset(scale_window[64:P, :], 0)
         tab_plane1 = sb([P, J // 4], I32, "tab_plane1")
         nc.vector.memset(tab_plane1[:], 0)
-        for a in range(2):
-            nc.sync.dma_start(scale_window[4 * a : P : 8, :], tab_scales[a].bitcast(I32))
 
-        word_window = placed([P, T], I32, "word_window", 4096)
-        nc.sync.dma_start(word_window[:], tab_words[0].rearrange("p t b -> p (t b)").bitcast(I32))
-        load_x(1, 0, placed([P, PACK, HALF], F32, "x_10", 20480)[:])
-        load_x(1, 1, placed([P, PACK, HALF], F32, "x_11", 32768)[:])
+        picked_scales = placed([P, 10 * J], U8, "picked_scales", X01_AT - J)[:, 0:J]
+        nc.vector.tensor_copy(picked_scales, scale_window[:].bitcast(U8).indirect(offsets[:]))
+        tab_plane0 = sb([P, J // 4], I32, "tab_plane0")
+        nc.vector.tensor_copy(
+            tab_plane0[:].bitcast(U8).rearrange("p (t c i) -> p c t i", t=PACK, i=16),
+            picked_scales.rearrange("p (c i t) -> p c t i", t=PACK, i=16),
+        )
+        for q in range(1, 4):
+            nc.scalar.dma_start(tab_plane0[32 * q : 32 * q + 4, :], tab_plane0[4 * q : 4 * q + 4, :])
+        for q in range(4):
+            queue = nc.gpsimd if q >= 2 else nc.scalar
+            queue.dma_start(tab_plane1[32 * q : 32 * q + 4, :], tab_plane0[16 + 4 * q : 20 + 4 * q, :])
+        planes = placed([P, 2, 2, N // 4], I32, "al_planes", PLANES_AT)
+        nc.vector.memset(planes[:], 0)
+        al_planes = [planes[:, w].bitcast(U8) for w in range(2)]
+        tab_planes = (tab_plane0[:].bitcast(U8), tab_plane1[:].bitcast(U8))
+
+        load_x(0, 1, placed([P, 2 * PACK, HALF], F32, "x_01", X01_AT)[:, 0:PACK, :])
+        load_x(1, 1, placed([P, PACK, HALF], F32, "x_11", X11_AT)[:])
 
         x_bf16, x_codes, x_scales = {}, {}, {}
 
         def interleave_x(a, hf, copy):
-            name = "x_bf16_%d%d" % (a, hf)
-            if (a, hf) == (0, 1):
-                x_bf16[a, hf] = placed([P, HALF, PACK], BF16, name, 73728 - 1024)
-            else:
-                x_bf16[a, hf] = sb([P, HALF, PACK], BF16, name)
+            x_bf16[a, hf] = sb([P, HALF, PACK], BF16, "x_bf16_%d%d" % (a, hf))
             copy(
                 x_bf16[a, hf][:].rearrange("p (c i) t -> p c t i", i=4),
                 x_raw[a, hf].rearrange("p t (c i) -> p c t i", i=4),
             )
 
-        for hf in range(2):
-            interleave_x(0, hf, nc.scalar.copy)
-
-        picked_scales = placed([P, 2 * J], U8, "picked_scales", 40960 - J)
-        nc.vector.tensor_copy(picked_scales[:, 0:J], scale_window[:].bitcast(U8).indirect(offsets[:]))
-        tab_plane0 = placed([P, J // 4], I32, "tab_plane0", 61440)
-        nc.vector.tensor_copy(
-            tab_plane0[:].bitcast(U8).rearrange("p (t c i) -> p c t i", t=PACK, i=16),
-            picked_scales[:, 0:J].rearrange("p (c i t) -> p c t i", t=PACK, i=16),
-        )
-        for r in range(1, 4):
-            nc.scalar.dma_start(tab_plane0[r:P:32, :], tab_plane0[8 * r : P : 32, :])
-        for r in range(4):
-            queue = nc.gpsimd if r == 3 else nc.scalar
-            queue.dma_start(tab_plane1[r:P:32, :], tab_plane0[8 * r + 4 : P : 32, :])
-        tab_planes = (tab_plane0[:].bitcast(U8), tab_plane1[:].bitcast(U8))
-
-        al_planes = {}
-
-        def load_al_planes():
-            planes = placed([P, 2, 2, N // 4], I32, "al_planes", 53248)
-            nc.vector.memset(planes[:], 0)
-            for w, scales in enumerate((al8_scales, al4_scales)):
-                al_planes[w] = planes[:, w].bitcast(U8)
-                for r in range(4):
-                    nc.sync.dma_start(
-                        planes[r:P:32, w], scales.bitcast(I32)[:, r:16:4, :].rearrange("a q n -> q a n")
-                    )
-
         def quantize(src, codes, scales):
             nc.vector.quantize_mx(codes.bitcast(FP8X4), scales, src[:].rearrange("p m t -> p (m t)"))
 
         def quantize_x(a, hf):
-            if hf == 0:
-                x_codes[a] = placed([P, M], U32, "x_codes%d" % a, (40960, 55296)[a])
-                x_scales[a] = sb([P, M], U8, "x_scales%d" % a)
-            cols = slice(hf * HALF, (hf + 1) * HALF)
-            quantize(x_bf16[a, hf], x_codes[a][:, cols], x_scales[a][:, cols])
+            x_codes[a, hf] = sb([P, HALF], U32, "x_codes%d%d" % (a, hf))
+            x_scales[a, hf] = sb([P, HALF], U8, "x_scales%d%d" % (a, hf))
+            quantize(x_bf16[a, hf], x_codes[a, hf][:], x_scales[a, hf][:])
 
         picked_words, tab_codes = {}, {}
 
         def gather_words(g):
-            picked_words[g] = placed([P, (2 - g) * KP], U32, "picked_words%d" % g, (53248, 22528)[g])[:, 0:KP]
+            if g == 0:
+                picked_words[g] = placed([P, 3 * KP], U32, "picked_words0", AL_AT)[:, 0:KP]
+            else:
+                picked_words[g] = sb([P, KP], U32, "picked_words1")[:]
             nc.vector.tensor_copy(
                 picked_words[g], word_window[:].bitcast(U32).indirect(offsets[:, 32 * g : 32 * (g + 1)])
             )
 
         def part_words(g):
-            tab_codes[g] = placed([P, 2 * PACK * 2 * COLS], U8, "tab_codes%d" % g, (57344, 32896)[g])
+            tab_codes[g] = sb([P, 2 * PACK * 2 * COLS], U8, "tab_codes%d" % g, tag=(None, "x_bf16_10")[g])
             parted = tab_codes[g][:].bitcast(U16).rearrange("p (a t c i) -> p a c t i", a=2, t=PACK, i=4)
             paired = picked_words[g].bitcast(U16).rearrange("p (c i t a) -> p a c t i", a=2, t=PACK, i=4)
             for a in range(2):
                 nc.vector.tensor_copy(parted[:, a], paired[:, a])
 
-        for hf in range(2):
-            quantize_x(0, hf)
-        cb_cw = sb([P, 2, 2, PACK], F32, "cb_cw", tag="x_bf16_00")
-        cb_sb, cw_sb = cb_cw[:, 0], cb_cw[:, 1]
-        nc.sync.dma_start(cb_sb, cb.rearrange("(a p t) -> p a t", a=2, t=PACK))
-        nc.sync.dma_start(cw_sb, cw.rearrange("(a p t) -> p a t", a=2, t=PACK))
-        al8_codes = placed([P, 2, N], I32, "al8_codes", 69632)
-        nc.sync.dma_start(al8_codes[:], al8_words.rearrange("a p n i -> p a (n i)").bitcast(I32))
-        al4_codes = placed([P, 2, N // 2], I32, "al4_codes", 73728)
-        nc.sync.dma_start(al4_codes[:], al4_words.rearrange("a p n -> p a n").bitcast(I32))
+        gather_words(0)
         warm_bank = psum.tile([P, 2 * HALF], F32, name="warm_bank", tag="bank7")
-        for n in range(6):
+        for n in range(WARM_PASSES):
             nc.tensor.matmul_mx(
-                warm_bank[:, (n % 2) * HALF : (n % 2 + 1) * HALF],
-                lhsT=x_codes[0][:, HALF : HALF + COLS].bitcast(FP8X4),
-                lhsT_scale=x_scales[0][:, HALF : HALF + COLS],
-                rhs=x_codes[0][:, HALF:M].bitcast(FP8X4),
-                rhs_scale=x_scales[0][:, HALF:M],
+                warm_bank[:, (n % 4) * COLS : (n % 4 + 1) * COLS],
+                lhsT=picked_words[0][:, 0 : COLS // 2].bitcast(FP4X4),
+                lhsT_scale=al_planes[1][:, 0, 0:COLS],
+                rhs=al8_head[:].bitcast(FP8X4),
+                rhs_scale=al_planes[0][:, 0, 0:COLS],
                 start=True,
                 stop=True,
             )
-        gather_words(0)
+        gather_words(1)
         part_words(0)
-        load_al_planes()
+        interleave_x(0, 0, nc.scalar.copy)
+        quantize_x(0, 0)
         interleave_x(1, 0, nc.scalar.copy)
         quantize_x(1, 0)
-        gather_words(1)
-        interleave_x(1, 1, nc.scalar.copy)
-        quantize_x(1, 1)
         part_words(1)
+        interleave_x(0, 1, nc.scalar.copy)
+        quantize_x(0, 1)
+        interleave_x(1, 1, nc.vector.tensor_copy)
+        quantize_x(1, 1)
 
-        b_sb = placed([P, N // P], F32, "b_sb", 12288)
+        al8_rest = placed([P, N - COLS], I32, "al8_rest", AL_AT)
+        nc.sync.dma_start(al8_rest[:], al8_rows[:, 0, COLS:N])
+        al4_codes = placed([P, 2, N // 2], I32, "al4_codes", AL_AT + 2048)
+        nc.sync.dma_start(al4_codes[:], al4_words.rearrange("a p n -> p a n").bitcast(I32))
+        al8_late = placed([P, N], I32, "al8_late", AL_AT + 4096)
+        nc.sync.dma_start(al8_late[:], al8_rows[:, 1, :])
+        for w, scales in enumerate((al8_scales, al4_scales)):
+            for r in range(4):
+                nc.sync.dma_start(
+                    planes[r:P:32, w], scales.bitcast(I32)[:, r:16:4, :].rearrange("a q n -> q a n")
+                )
+        b_sb = sb([P, N // P], F32, "b_sb", tag="x_bf16_01")
         with nc.allow_non_contiguous_dma(reason="one bias value to a partition"):
             nc.sync.dma_start(b_sb[:], b.rearrange("(c p) -> p c", p=P))
 
@@ -178,28 +175,28 @@ def tile_list_kernl_sigm_res_silu_kernel(
 
         d = {}
 
-        def first_product(g, target, m0, width, step):
+        def first_product(hf, g):
+            d[hf, g] = [bank(PACK * g + t, "d%d%d%d" % (hf, g, t))[:, 0:HALF] for t in range(PACK)]
             for a in range(2):
-                for q0 in range(0, width, step):
-                    cols = slice(m0 + q0, m0 + q0 + step)
+                for q0 in range(0, HALF, COLS):
                     for t in range(PACK):
                         codes = tab_codes[g][:, (a * PACK + t) * 2 * COLS : (a * PACK + t + 1) * 2 * COLS]
                         nc.tensor.matmul_mx(
-                            target[t][:, q0 : q0 + step],
+                            d[hf, g][t][:, q0 : q0 + COLS],
                             lhsT=codes.bitcast(FP4X4),
                             lhsT_scale=tab_planes[a][:, (2 * t + g) * COLS : (2 * t + g + 1) * COLS],
-                            rhs=x_codes[a][:, cols].bitcast(FP8X4),
-                            rhs_scale=x_scales[a][:, cols],
+                            rhs=x_codes[a, hf][:, q0 : q0 + COLS].bitcast(FP8X4),
+                            rhs_scale=x_scales[a, hf][:, q0 : q0 + COLS],
                             start=(a == 0 and q0 == 0),
-                            stop=(a == 1 and q0 + step == width),
+                            stop=(a == 1 and q0 + COLS == HALF),
                         )
 
         logistic, h_bf16, h_codes, h_scales = {}, {}, {}, {}
 
         def sigmoids(hf, g):
             name = "logistic%d%d" % (hf, g)
-            if (hf, g) == (0, 0):
-                logistic[hf, g] = placed([P, HALF // 4, PACK, 4], F32, name, 28736)
+            if hf == 0:
+                logistic[hf, g] = placed([P, HALF // 4, PACK, 4], F32, name, X01_AT + 4096 * g)
             else:
                 logistic[hf, g] = sb([P, HALF // 4, PACK, 4], F32, name)
             for t in range(PACK):
@@ -210,36 +207,41 @@ def tile_list_kernl_sigm_res_silu_kernel(
                     bias=cb_sb[:, g, t : t + 1],
                 )
 
-        def weigh(hf, g, m0, width):
-            key = (hf, g, m0)
-            h_bf16[key] = sb([P, width, PACK], BF16, "h_bf16_%d%d_%d" % key, tag="h_bf16_%d_%d" % (hf, m0))
+        def weigh(hf, g, m0):
+            piece = (4 * hf + 2 * g + m0 // COLS) % 3
+            h_bf16[hf, g, m0] = sb(
+                [P, COLS, PACK], BF16, "h_bf16_%d%d_%d" % (hf, g, m0), tag=("x_bf16_11", "h_b", "h_c")[piece]
+            )
             nc.vector.tensor_tensor(
-                h_bf16[key][:].rearrange("p (c i) t -> p c t i", i=4),
-                logistic[hf, g][:, m0 // 4 : (m0 + width) // 4],
-                cw_sb[:, g, :].unsqueeze(1).unsqueeze(3).to_broadcast([P, width // 4, PACK, 4]),
+                h_bf16[hf, g, m0][:].rearrange("p (c i) t -> p c t i", i=4),
+                logistic[hf, g][:, m0 // 4 : (m0 + COLS) // 4],
+                cw_sb[:, g, :].unsqueeze(1).unsqueeze(3).to_broadcast([P, COLS // 4, PACK, 4]),
                 ALU.mult,
             )
 
-        def quantize_h(hf, g, m0, width):
-            key = (hf, g, m0)
-            name = "h%d%d_%d" % key
-            h_codes[key] = sb([P, width], U32, name + "_codes")[:]
-            h_scales[key] = sb([P, width], U8, name + "_scales")[:]
-            quantize(h_bf16[key], h_codes[key], h_scales[key])
+        def quantize_h(hf, g, m0):
+            if m0 == 0:
+                h_codes[hf, g] = sb([P, HALF], U32, "h_codes%d%d" % (hf, g), tag="h_codes%d" % g)
+                h_scales[hf, g] = sb([P, HALF], U8, "h_scales%d%d" % (hf, g))
+            quantize(h_bf16[hf, g, m0], h_codes[hf, g][:, m0 : m0 + COLS], h_scales[hf, g][:, m0 : m0 + COLS])
 
         y_banks = {}
 
         def second_product(hf, g, m0, width, c):
-            key = (hf, g, m0)
+            key = (hf, g)
             if g == 0:
-                y_banks[hf, c] = bank(PACK * (1 - hf) + c, "y%d%d" % (hf, c))[:, 0:HALF]
+                y_banks[hf, c] = bank(PACK * hf + c, "y%d%d" % (hf, c))[:, 0:HALF]
             n0 = c * COLS
+            if g == 1:
+                al8_codes = al8_late[:, n0 : n0 + COLS]
+            else:
+                al8_codes = al8_head[:] if c == 0 else al8_rest[:, n0 - COLS : n0]
             nc.tensor.matmul_mx(
                 y_banks[hf, c][:, m0 : m0 + width],
-                lhsT=al8_codes[:, g, n0 : n0 + COLS].bitcast(FP8X4),
+                lhsT=al8_codes.bitcast(FP8X4),
                 lhsT_scale=al_planes[0][:, g, n0 : n0 + COLS],
-                rhs=h_codes[key].bitcast(FP8X4),
-                rhs_scale=h_scales[key],
+                rhs=h_codes[key][:, m0 : m0 + width].bitcast(FP8X4),
+                rhs_scale=h_scales[key][:, m0 : m0 + width],
                 start=(g == 0),
                 stop=False,
             )
@@ -248,8 +250,8 @@ def tile_list_kernl_sigm_res_silu_kernel(
                     y_banks[hf, c][:, m0 + q0 : m0 + q0 + COLS],
                     lhsT=al4_codes[:, g, n0 // 2 : (n0 + COLS) // 2].bitcast(FP4X4),
                     lhsT_scale=al_planes[1][:, g, n0 : n0 + COLS],
-                    rhs=h_codes[key][:, q0 : q0 + COLS].bitcast(FP8X4),
-                    rhs_scale=h_scales[key][:, q0 : q0 + COLS],
+                    rhs=h_codes[key][:, m0 + q0 : m0 + q0 + COLS].bitcast(FP8X4),
+                    rhs_scale=h_scales[key][:, m0 + q0 : m0 + q0 + COLS],
                     start=False,
                     stop=(g == 1 and m0 + q0 + COLS == HALF),
                 )
@@ -260,21 +262,16 @@ def tile_list_kernl_sigm_res_silu_kernel(
             nc.sync.dma_start(out[c * COLS : (c + 1) * COLS, hf * HALF : (hf + 1) * HALF], result[:])
 
         for hf in range(2):
-            banks = [bank(PACK * hf + t, "d0%d%d" % (hf, t)) for t in range(PACK)]
-            first_product(0, banks, hf * HALF, HALF, COLS)
-            d[hf, 0] = [banks[t][:, 0:HALF] for t in range(PACK)]
-            sigmoids(hf, 0)
-        banks = [bank(t, "d1%d" % t) for t in range(PACK)]
-        first_product(1, banks, 0, M, M)
+            for g in range(2):
+                first_product(hf, g)
+                sigmoids(hf, g)
         for hf in range(2):
-            d[hf, 1] = [banks[t][:, hf * HALF : (hf + 1) * HALF] for t in range(PACK)]
-            sigmoids(hf, 1)
-        for g in range(2):
-            for hf in range(2):
+            for g in range(2):
+                for m0 in range(0, HALF, COLS):
+                    weigh(hf, g, m0)
+                    quantize_h(hf, g, m0)
                 width = COLS if (hf, g) == (1, 1) else HALF
                 for m0 in range(0, HALF, width):
-                    weigh(hf, g, m0, width)
-                    quantize_h(hf, g, m0, width)
                     for c in range(N // COLS):
                         second_product(hf, g, m0, width, c)
         for hf in range(2):

@@ -39,7 +39,12 @@ def tile_list_kernl_sigm_res_silu_kernel(
         def sb(shape, dtype, name, tag=None):
             return held.tile(shape, dtype, name=name, tag=tag or name, align_bytes=64)
 
-        WORDS_AT, X11_AT, X01_AT, PLANES_AT, AL_AT = 0, 16384, 20480, 28672, 30720
+        WORDS_AT, X11_AT, X01_AT, X10_BF16_AT = 0, 16384, 20480, 28672
+
+        cb_sb = sb([P, 2, PACK], F32, "cb_sb")
+        cw_sb = sb([P, 2, PACK], F32, "cw_sb")
+        nc.scalar.dma_start(cb_sb[:], cb.rearrange("(a p t) -> p a t", a=2, t=PACK))
+        nc.scalar.dma_start(cw_sb[:], cw.rearrange("(a p t) -> p a t", a=2, t=PACK))
 
         offsets = held.tile([P, J // 16], U16, name="offsets")
         nc.sync.dma_start(offsets[:], offs)
@@ -61,11 +66,6 @@ def tile_list_kernl_sigm_res_silu_kernel(
         load_x(0, 0, sb([P, PACK, HALF], F32, "x_00")[:])
         load_x(1, 0, sb([P, PACK, HALF], F32, "x_10")[:])
 
-        cb_sb = sb([P, 2, PACK], F32, "cb_sb")
-        cw_sb = sb([P, 2, PACK], F32, "cw_sb")
-        nc.scalar.dma_start(cb_sb[:], cb.rearrange("(a p t) -> p a t", a=2, t=PACK))
-        nc.scalar.dma_start(cw_sb[:], cw.rearrange("(a p t) -> p a t", a=2, t=PACK))
-
         warm_in = sb([P, 32], F32, "warm_in")
         nc.vector.memset(warm_in[:], 0.0)
         warm_out = sb([P, 32], F32, "warm_out")
@@ -76,21 +76,26 @@ def tile_list_kernl_sigm_res_silu_kernel(
         tab_plane1 = sb([P, J // 4], I32, "tab_plane1")
         nc.vector.memset(tab_plane1[:], 0)
 
-        picked_scales = placed([P, 10 * J], U8, "picked_scales", X01_AT - J)[:, 0:J]
-        nc.vector.tensor_copy(picked_scales, scale_window[:].bitcast(U8).indirect(offsets[:]))
+        planes = sb([P, 2, 2, N // 4], I32, "al_planes")
+        nc.gpsimd.memset(planes[:], 0)
+        al_planes = [planes[:, w].bitcast(U8) for w in range(2)]
+        picked_scales = placed([P, 2 * J], U8, "picked_scales", X01_AT - J)[:, 0:J]
+        for g in range(2):
+            nc.vector.tensor_copy(
+                picked_scales[:, g * KP : (g + 1) * KP],
+                scale_window[:].bitcast(U8).indirect(offsets[:, 32 * g : 32 * (g + 1)]),
+            )
         tab_plane0 = sb([P, J // 4], I32, "tab_plane0")
-        nc.vector.tensor_copy(
-            tab_plane0[:].bitcast(U8).rearrange("p (t c i) -> p c t i", t=PACK, i=16),
-            picked_scales.rearrange("p (c i t) -> p c t i", t=PACK, i=16),
-        )
+        for g in range(2):
+            nc.vector.tensor_copy(
+                tab_plane0[:].bitcast(U8).rearrange("p (t g c i) -> p g c t i", t=PACK, g=2, i=16)[:, g],
+                picked_scales[:, g * KP : (g + 1) * KP].rearrange("p (c i t) -> p c t i", t=PACK, i=16),
+            )
         for q in range(1, 4):
             nc.scalar.dma_start(tab_plane0[32 * q : 32 * q + 4, :], tab_plane0[4 * q : 4 * q + 4, :])
         for q in range(4):
             queue = nc.gpsimd if q >= 2 else nc.scalar
             queue.dma_start(tab_plane1[32 * q : 32 * q + 4, :], tab_plane0[16 + 4 * q : 20 + 4 * q, :])
-        planes = placed([P, 2, 2, N // 4], I32, "al_planes", PLANES_AT)
-        nc.vector.memset(planes[:], 0)
-        al_planes = [planes[:, w].bitcast(U8) for w in range(2)]
         tab_planes = (tab_plane0[:].bitcast(U8), tab_plane1[:].bitcast(U8))
 
         load_x(0, 1, placed([P, 2 * PACK, HALF], F32, "x_01", X01_AT)[:, 0:PACK, :])
@@ -99,7 +104,11 @@ def tile_list_kernl_sigm_res_silu_kernel(
         x_bf16, x_codes, x_scales = {}, {}, {}
 
         def interleave_x(a, hf, copy):
-            x_bf16[a, hf] = sb([P, HALF, PACK], BF16, "x_bf16_%d%d" % (a, hf))
+            name = "x_bf16_%d%d" % (a, hf)
+            if (a, hf) == (1, 0):
+                x_bf16[a, hf] = placed([P, HALF, PACK], BF16, name, X10_BF16_AT)
+            else:
+                x_bf16[a, hf] = sb([P, HALF, PACK], BF16, name)
             copy(
                 x_bf16[a, hf][:].rearrange("p (c i) t -> p c t i", i=4),
                 x_raw[a, hf].rearrange("p t (c i) -> p c t i", i=4),
@@ -116,20 +125,20 @@ def tile_list_kernl_sigm_res_silu_kernel(
         picked_words, tab_codes = {}, {}
 
         def gather_words(g):
-            if g == 0:
-                picked_words[g] = placed([P, 3 * KP], U32, "picked_words0", AL_AT)[:, 0:KP]
-            else:
-                picked_words[g] = sb([P, KP], U32, "picked_words1")[:]
+            picked_words[g] = sb([P, KP], U32, "picked_words%d" % g)[:]
             nc.vector.tensor_copy(
                 picked_words[g], word_window[:].bitcast(U32).indirect(offsets[:, 32 * g : 32 * (g + 1)])
             )
 
-        def part_words(g):
-            tab_codes[g] = sb([P, 2 * PACK * 2 * COLS], U8, "tab_codes%d" % g, tag=(None, "x_bf16_10")[g])
-            parted = tab_codes[g][:].bitcast(U16).rearrange("p (a t c i) -> p a c t i", a=2, t=PACK, i=4)
+        def part_words(g, a):
+            name = "tab_codes%d%d" % (g, a)
+            if g == 1:
+                tab_codes[g, a] = placed([P, PACK * 2 * COLS], U8, name, X10_BF16_AT + 1024 * a)
+            else:
+                tab_codes[g, a] = sb([P, PACK * 2 * COLS], U8, name, tag=(None, "x_bf16_00")[a])
+            parted = tab_codes[g, a][:].bitcast(U16).rearrange("p (t c i) -> p c t i", t=PACK, i=4)
             paired = picked_words[g].bitcast(U16).rearrange("p (c i t a) -> p a c t i", a=2, t=PACK, i=4)
-            for a in range(2):
-                nc.vector.tensor_copy(parted[:, a], paired[:, a])
+            nc.vector.tensor_copy(parted, paired[:, a])
 
         gather_words(0)
         warm_bank = psum.tile([P, 2 * HALF], F32, name="warm_bank", tag="bank7")
@@ -144,29 +153,31 @@ def tile_list_kernl_sigm_res_silu_kernel(
                 stop=True,
             )
         gather_words(1)
-        part_words(0)
+        part_words(0, 0)
         interleave_x(0, 0, nc.scalar.copy)
         quantize_x(0, 0)
+        part_words(0, 1)
         interleave_x(1, 0, nc.scalar.copy)
         quantize_x(1, 0)
-        part_words(1)
+        part_words(1, 0)
+        part_words(1, 1)
         interleave_x(0, 1, nc.scalar.copy)
         quantize_x(0, 1)
         interleave_x(1, 1, nc.vector.tensor_copy)
         quantize_x(1, 1)
 
-        al8_rest = placed([P, N - COLS], I32, "al8_rest", AL_AT)
+        al8_rest = placed([P, N - COLS], I32, "al8_rest", WORDS_AT)
         nc.sync.dma_start(al8_rest[:], al8_rows[:, 0, COLS:N])
-        al4_codes = placed([P, 2, N // 2], I32, "al4_codes", AL_AT + 2048)
+        al4_codes = placed([P, 2, N // 2], I32, "al4_codes", WORDS_AT + 2048)
         nc.sync.dma_start(al4_codes[:], al4_words.rearrange("a p n -> p a n").bitcast(I32))
-        al8_late = placed([P, N], I32, "al8_late", AL_AT + 4096)
-        nc.sync.dma_start(al8_late[:], al8_rows[:, 1, :])
         for w, scales in enumerate((al8_scales, al4_scales)):
             for r in range(4):
                 nc.sync.dma_start(
                     planes[r:P:32, w], scales.bitcast(I32)[:, r:16:4, :].rearrange("a q n -> q a n")
                 )
-        b_sb = sb([P, N // P], F32, "b_sb", tag="x_bf16_01")
+        al8_late = sb([P, N], I32, "al8_late", tag="x_bf16_01")
+        nc.sync.dma_start(al8_late[:], al8_rows[:, 1, :])
+        b_sb = placed([P, N // P], F32, "b_sb", X11_AT)
         with nc.allow_non_contiguous_dma(reason="one bias value to a partition"):
             nc.sync.dma_start(b_sb[:], b.rearrange("(c p) -> p c", p=P))
 
@@ -180,7 +191,7 @@ def tile_list_kernl_sigm_res_silu_kernel(
             for a in range(2):
                 for q0 in range(0, HALF, COLS):
                     for t in range(PACK):
-                        codes = tab_codes[g][:, (a * PACK + t) * 2 * COLS : (a * PACK + t + 1) * 2 * COLS]
+                        codes = tab_codes[g, a][:, t * 2 * COLS : (t + 1) * 2 * COLS]
                         nc.tensor.matmul_mx(
                             d[hf, g][t][:, q0 : q0 + COLS],
                             lhsT=codes.bitcast(FP4X4),
@@ -259,7 +270,8 @@ def tile_list_kernl_sigm_res_silu_kernel(
         def finish(hf, c):
             result = sb([P, HALF], F32, "result%d%d" % (hf, c))
             nc.scalar.activation(result[:], y_banks[hf, c], ACT.Silu, bias=b_sb[:, c : c + 1])
-            nc.sync.dma_start(out[c * COLS : (c + 1) * COLS, hf * HALF : (hf + 1) * HALF], result[:])
+            queue = nc.scalar if (hf, c) == (1, 3) else nc.sync
+            queue.dma_start(out[c * COLS : (c + 1) * COLS, hf * HALF : (hf + 1) * HALF], result[:])
 
         for hf in range(2):
             for g in range(2):
@@ -270,10 +282,8 @@ def tile_list_kernl_sigm_res_silu_kernel(
                 for m0 in range(0, HALF, COLS):
                     weigh(hf, g, m0)
                     quantize_h(hf, g, m0)
-                width = COLS if (hf, g) == (1, 1) else HALF
-                for m0 in range(0, HALF, width):
-                    for c in range(N // COLS):
-                        second_product(hf, g, m0, width, c)
+                for c in range(N // COLS):
+                    second_product(hf, g, 0, HALF, c)
         for hf in range(2):
             for c in range(N // COLS):
                 finish(hf, c)

@@ -21,7 +21,7 @@ PACK = 4
 KP = P * PACK
 HALF = M // 2
 COLS = 128
-WARM_PASSES = 12
+WARM_PASSES = 3
 
 
 def tile_list_kernl_sigm_res_silu_kernel(
@@ -144,11 +144,11 @@ def tile_list_kernl_sigm_res_silu_kernel(
         warm_bank = psum.tile([P, 2 * HALF], F32, name="warm_bank", tag="bank7")
         for n in range(WARM_PASSES):
             nc.tensor.matmul_mx(
-                warm_bank[:, (n % 4) * COLS : (n % 4 + 1) * COLS],
-                lhsT=picked_words[0][:, 0 : COLS // 2].bitcast(FP4X4),
-                lhsT_scale=al_planes[1][:, 0, 0:COLS],
-                rhs=al8_head[:].bitcast(FP8X4),
-                rhs_scale=al_planes[0][:, 0, 0:COLS],
+                warm_bank[:],
+                lhsT=al8_head[:].bitcast(FP8X4),
+                lhsT_scale=al_planes[0][:, 0, 0:COLS],
+                rhs=picked_words[0][:, 0:HALF].bitcast(FP4X4),
+                rhs_scale=al_planes[1][:, 0, :],
                 start=True,
                 stop=True,
             )
@@ -189,18 +189,17 @@ def tile_list_kernl_sigm_res_silu_kernel(
         def first_product(hf, g):
             d[hf, g] = [bank(PACK * g + t, "d%d%d%d" % (hf, g, t))[:, 0:HALF] for t in range(PACK)]
             for a in range(2):
-                for q0 in range(0, HALF, COLS):
-                    for t in range(PACK):
-                        codes = tab_codes[g, a][:, t * 2 * COLS : (t + 1) * 2 * COLS]
-                        nc.tensor.matmul_mx(
-                            d[hf, g][t][:, q0 : q0 + COLS],
-                            lhsT=codes.bitcast(FP4X4),
-                            lhsT_scale=tab_planes[a][:, (2 * t + g) * COLS : (2 * t + g + 1) * COLS],
-                            rhs=x_codes[a, hf][:, q0 : q0 + COLS].bitcast(FP8X4),
-                            rhs_scale=x_scales[a, hf][:, q0 : q0 + COLS],
-                            start=(a == 0 and q0 == 0),
-                            stop=(a == 1 and q0 + COLS == HALF),
-                        )
+                for t in range(PACK):
+                    codes = tab_codes[g, a][:, t * 2 * COLS : (t + 1) * 2 * COLS]
+                    nc.tensor.matmul_mx(
+                        d[hf, g][t],
+                        lhsT=codes.bitcast(FP4X4),
+                        lhsT_scale=tab_planes[a][:, (2 * t + g) * COLS : (2 * t + g + 1) * COLS],
+                        rhs=x_codes[a, hf][:].bitcast(FP8X4),
+                        rhs_scale=x_scales[a, hf][:],
+                        start=(a == 0),
+                        stop=(a == 1),
+                    )
 
         logistic, h_bf16, h_codes, h_scales = {}, {}, {}, {}
 
@@ -256,16 +255,15 @@ def tile_list_kernl_sigm_res_silu_kernel(
                 start=(g == 0),
                 stop=False,
             )
-            for q0 in range(0, width, COLS):
-                nc.tensor.matmul_mx(
-                    y_banks[hf, c][:, m0 + q0 : m0 + q0 + COLS],
-                    lhsT=al4_codes[:, g, n0 // 2 : (n0 + COLS) // 2].bitcast(FP4X4),
-                    lhsT_scale=al_planes[1][:, g, n0 : n0 + COLS],
-                    rhs=h_codes[key][:, m0 + q0 : m0 + q0 + COLS].bitcast(FP8X4),
-                    rhs_scale=h_scales[key][:, m0 + q0 : m0 + q0 + COLS],
-                    start=False,
-                    stop=(g == 1 and m0 + q0 + COLS == HALF),
-                )
+            nc.tensor.matmul_mx(
+                y_banks[hf, c][:, m0 : m0 + width],
+                lhsT=al4_codes[:, g, n0 // 2 : (n0 + COLS) // 2].bitcast(FP4X4),
+                lhsT_scale=al_planes[1][:, g, n0 : n0 + COLS],
+                rhs=h_codes[key][:, m0 : m0 + width].bitcast(FP8X4),
+                rhs_scale=h_scales[key][:, m0 : m0 + width],
+                start=False,
+                stop=(g == 1),
+            )
 
         def finish(hf, c):
             result = sb([P, HALF], F32, "result%d%d" % (hf, c))

@@ -21,7 +21,6 @@ PACK = 4
 KP = P * PACK
 HALF = M // 2
 COLS = 128
-WARM_PASSES = 3
 
 
 def tile_list_kernl_sigm_res_silu_kernel(
@@ -141,17 +140,6 @@ def tile_list_kernl_sigm_res_silu_kernel(
             nc.vector.tensor_copy(parted, paired[:, a])
 
         gather_words(0)
-        warm_bank = psum.tile([P, 2 * HALF], F32, name="warm_bank", tag="bank7")
-        for n in range(WARM_PASSES):
-            nc.tensor.matmul_mx(
-                warm_bank[:],
-                lhsT=al8_head[:].bitcast(FP8X4),
-                lhsT_scale=al_planes[0][:, 0, 0:COLS],
-                rhs=picked_words[0][:, 0:HALF].bitcast(FP4X4),
-                rhs_scale=al_planes[1][:, 0, :],
-                start=True,
-                stop=True,
-            )
         gather_words(1)
         part_words(0, 0)
         interleave_x(0, 0, nc.scalar.copy)

@@ -38,7 +38,7 @@ def tile_list_kernl_sigm_res_silu_kernel(
         def sb(shape, dtype, name, tag=None):
             return held.tile(shape, dtype, name=name, tag=tag or name, align_bytes=64)
 
-        WORDS_AT, X11_AT, X01_AT, X10_BF16_AT = 0, 16384, 20480, 28672
+        WORDS_AT, PLANES_AT, X11_AT, X01_AT, X10_BF16_AT = 0, 16384, 18432, 22528, 30720
 
         cb_sb = sb([P, 2, PACK], F32, "cb_sb")
         cw_sb = sb([P, 2, PACK], F32, "cw_sb")
@@ -50,8 +50,6 @@ def tile_list_kernl_sigm_res_silu_kernel(
         scale_window = sb([P, T // 4], I32, "scale_window")
         nc.sync.dma_start(scale_window[0:32, :], tab_scales.rearrange("a q t -> (a q) t").bitcast(I32))
         al8_rows = al8_words.rearrange("a p n i -> p a (n i)").bitcast(I32)
-        al8_head = sb([P, COLS], I32, "al8_head")
-        nc.sync.dma_start(al8_head[:], al8_rows[:, 0, 0:COLS])
         word_window = placed([P, T], I32, "word_window", WORDS_AT)
         nc.sync.dma_start(word_window[:], tab_words[0].rearrange("p t b -> p (t b)").bitcast(I32))
 
@@ -64,6 +62,7 @@ def tile_list_kernl_sigm_res_silu_kernel(
 
         load_x(0, 0, sb([P, PACK, HALF], F32, "x_00")[:])
         load_x(1, 0, sb([P, PACK, HALF], F32, "x_10")[:])
+        load_x(0, 1, placed([P, 2 * PACK, HALF], F32, "x_01", X01_AT)[:, 0:PACK, :])
 
         warm_in = sb([P, 32], F32, "warm_in")
         nc.vector.memset(warm_in[:], 0.0)
@@ -75,10 +74,7 @@ def tile_list_kernl_sigm_res_silu_kernel(
         tab_plane1 = sb([P, J // 4], I32, "tab_plane1")
         nc.vector.memset(tab_plane1[:], 0)
 
-        planes = sb([P, 2, 2, N // 4], I32, "al_planes")
-        nc.gpsimd.memset(planes[:], 0)
-        al_planes = [planes[:, w].bitcast(U8) for w in range(2)]
-        picked_scales = placed([P, 2 * J], U8, "picked_scales", X01_AT - J)[:, 0:J]
+        picked_scales = placed([P, 2 * J], U8, "picked_scales", X11_AT - J)[:, 0:J]
         for g in range(2):
             nc.vector.tensor_copy(
                 picked_scales[:, g * KP : (g + 1) * KP],
@@ -97,8 +93,11 @@ def tile_list_kernl_sigm_res_silu_kernel(
             queue.dma_start(tab_plane1[32 * q : 32 * q + 4, :], tab_plane0[16 + 4 * q : 20 + 4 * q, :])
         tab_planes = (tab_plane0[:].bitcast(U8), tab_plane1[:].bitcast(U8))
 
-        load_x(0, 1, placed([P, 2 * PACK, HALF], F32, "x_01", X01_AT)[:, 0:PACK, :])
         load_x(1, 1, placed([P, PACK, HALF], F32, "x_11", X11_AT)[:])
+
+        planes = placed([P, 2, 2, N // 4], I32, "al_planes", PLANES_AT)
+        nc.vector.memset(planes[:], 0)
+        al_planes = [planes[:, w].bitcast(U8) for w in range(2)]
 
         x_bf16, x_codes, x_scales = {}, {}, {}
 
@@ -154,8 +153,8 @@ def tile_list_kernl_sigm_res_silu_kernel(
         interleave_x(1, 1, nc.vector.tensor_copy)
         quantize_x(1, 1)
 
-        al8_rest = placed([P, N - COLS], I32, "al8_rest", WORDS_AT)
-        nc.sync.dma_start(al8_rest[:], al8_rows[:, 0, COLS:N])
+        al8_early = placed([P, N], I32, "al8_early", WORDS_AT)
+        nc.sync.dma_start(al8_early[:], al8_rows[:, 0, :])
         al4_codes = placed([P, 2, N // 2], I32, "al4_codes", WORDS_AT + 2048)
         nc.sync.dma_start(al4_codes[:], al4_words.rearrange("a p n -> p a n").bitcast(I32))
         for w, scales in enumerate((al8_scales, al4_scales)):
@@ -230,10 +229,7 @@ def tile_list_kernl_sigm_res_silu_kernel(
             if g == 0:
                 y_banks[hf, c] = bank(PACK * hf + c, "y%d%d" % (hf, c))[:, 0:HALF]
             n0 = c * COLS
-            if g == 1:
-                al8_codes = al8_late[:, n0 : n0 + COLS]
-            else:
-                al8_codes = al8_head[:] if c == 0 else al8_rest[:, n0 - COLS : n0]
+            al8_codes = (al8_early, al8_late)[g][:, n0 : n0 + COLS]
             nc.tensor.matmul_mx(
                 y_banks[hf, c][:, m0 : m0 + width],
                 lhsT=al8_codes.bitcast(FP8X4),
@@ -263,11 +259,13 @@ def tile_list_kernl_sigm_res_silu_kernel(
             for g in range(2):
                 first_product(hf, g)
                 sigmoids(hf, g)
-        for hf in range(2):
-            for g in range(2):
-                for m0 in range(0, HALF, COLS):
-                    weigh(hf, g, m0)
-                    quantize_h(hf, g, m0)
+        pieces = [(hf, g, m0) for hf in range(2) for g in range(2) for m0 in range(0, HALF, COLS)]
+        weigh(*pieces[0])
+        for n, (hf, g, m0) in enumerate(pieces):
+            if n + 1 < len(pieces):
+                weigh(*pieces[n + 1])
+            quantize_h(hf, g, m0)
+            if m0 > 0:
                 for c in range(N // COLS):
                     second_product(hf, g, 0, HALF, c)
         for hf in range(2):

@@ -1,6 +1,7 @@
 from contextlib import ExitStack
 
 import concourse.mybir as mybir
+from concourse.masks import make_identity
 
 K, M, N, J, T = 1024, 512, 512, 1024, 4096
 FLOPS = 2 * K * J * M + 2 * 2 * J * N * M
@@ -21,6 +22,7 @@ PACK = 4
 KP = P * PACK
 HALF = M // 2
 COLS = 128
+POOL_COLS = 64
 
 
 def tile_list_kernl_sigm_res_silu_kernel(
@@ -38,18 +40,21 @@ def tile_list_kernl_sigm_res_silu_kernel(
         def sb(shape, dtype, name, tag=None):
             return held.tile(shape, dtype, name=name, tag=tag or name, align_bytes=64)
 
-        WORDS_AT, PLANES_AT, X11_AT, X01_AT, X10_BF16_AT = 0, 16384, 18432, 22528, 30720
+        def bank(index, name):
+            return psum.tile([P, 2 * HALF], F32, name=name, tag="bank%d" % index)
+
+        WORDS_AT, PLANES_AT, TURNED_AT, X11_AT, XB00_AT, XB10_AT = 0, 16384, 18432, 18944, 23040, 25088
 
         cb_sb = sb([P, 2, PACK], F32, "cb_sb")
-        cw_sb = sb([P, 2, PACK], F32, "cw_sb")
         nc.scalar.dma_start(cb_sb[:], cb.rearrange("(a p t) -> p a t", a=2, t=PACK))
-        nc.scalar.dma_start(cw_sb[:], cw.rearrange("(a p t) -> p a t", a=2, t=PACK))
+        cw_square = sb([P, P], F32, "cw_square")
+        cw_sb = cw_square[:, 0 : 2 * PACK].rearrange("p (a t) -> p a t", a=2)
+        nc.scalar.dma_start(cw_sb, cw.rearrange("(a p t) -> p a t", a=2, t=PACK))
 
         offsets = held.tile([P, J // 16], U16, name="offsets")
         nc.sync.dma_start(offsets[:], offs)
         scale_window = sb([P, T // 4], I32, "scale_window")
         nc.sync.dma_start(scale_window[0:32, :], tab_scales.rearrange("a q t -> (a q) t").bitcast(I32))
-        al8_rows = al8_words.rearrange("a p n i -> p a (n i)").bitcast(I32)
         word_window = placed([P, T], I32, "word_window", WORDS_AT)
         nc.sync.dma_start(word_window[:], tab_words[0].rearrange("p t b -> p (t b)").bitcast(I32))
 
@@ -62,7 +67,7 @@ def tile_list_kernl_sigm_res_silu_kernel(
 
         load_x(0, 0, sb([P, PACK, HALF], F32, "x_00")[:])
         load_x(1, 0, sb([P, PACK, HALF], F32, "x_10")[:])
-        load_x(0, 1, placed([P, 2 * PACK, HALF], F32, "x_01", X01_AT)[:, 0:PACK, :])
+        load_x(0, 1, sb([P, PACK, HALF], F32, "x_01")[:])
 
         warm_in = sb([P, 32], F32, "warm_in")
         nc.vector.memset(warm_in[:], 0.0)
@@ -74,7 +79,13 @@ def tile_list_kernl_sigm_res_silu_kernel(
         tab_plane1 = sb([P, J // 4], I32, "tab_plane1")
         nc.vector.memset(tab_plane1[:], 0)
 
-        picked_scales = placed([P, 2 * J], U8, "picked_scales", X11_AT - J)[:, 0:J]
+        identity = sb([P, P], F32, "identity")
+        make_identity(nc, identity[:])
+        nc.vector.memset(cw_square[:, 2 * PACK : P], 0.0)
+        cw_turned_ps = bank(6, "cw_turned_ps")[:, 0:P]
+        nc.tensor.transpose(cw_turned_ps, cw_square[:], identity[:])
+
+        picked_scales = placed([P, 2 * J], U8, "picked_scales", TURNED_AT - J)[:, 0:J]
         for g in range(2):
             nc.vector.tensor_copy(
                 picked_scales[:, g * KP : (g + 1) * KP],
@@ -95,30 +106,32 @@ def tile_list_kernl_sigm_res_silu_kernel(
 
         load_x(1, 1, placed([P, PACK, HALF], F32, "x_11", X11_AT)[:])
 
+        cw_turned = placed([P, P], F32, "cw_turned", TURNED_AT)
+        nc.scalar.copy(cw_turned[:], cw_turned_ps)
+        cw_bank = bank(7, "cw_bank")[:, 0:P]
+        nc.tensor.transpose(cw_bank, cw_turned[:], identity[:])
+        cw_ps = cw_bank[:, 0 : 2 * PACK].rearrange("p (a t) -> p a t", a=2)
+
         planes = placed([P, 2, 2, N // 4], I32, "al_planes", PLANES_AT)
         nc.vector.memset(planes[:], 0)
         al_planes = [planes[:, w].bitcast(U8) for w in range(2)]
 
         x_bf16, x_codes, x_scales = {}, {}, {}
 
-        def interleave_x(a, hf, copy):
-            name = "x_bf16_%d%d" % (a, hf)
-            if (a, hf) == (1, 0):
-                x_bf16[a, hf] = placed([P, HALF, PACK], BF16, name, X10_BF16_AT)
-            else:
-                x_bf16[a, hf] = sb([P, HALF, PACK], BF16, name)
+        def interleave_x(a, hf, tile, copy):
+            x_bf16[a, hf] = tile
             copy(
-                x_bf16[a, hf][:].rearrange("p (c i) t -> p c t i", i=4),
+                tile[:].rearrange("p (c i) t -> p c t i", i=4),
                 x_raw[a, hf].rearrange("p t (c i) -> p c t i", i=4),
             )
 
         def quantize(src, codes, scales):
-            nc.vector.quantize_mx(codes.bitcast(FP8X4), scales, src[:].rearrange("p m t -> p (m t)"))
+            nc.vector.quantize_mx(codes.bitcast(FP8X4), scales, src.rearrange("p m t -> p (m t)"))
 
         def quantize_x(a, hf):
             x_codes[a, hf] = sb([P, HALF], U32, "x_codes%d%d" % (a, hf))
             x_scales[a, hf] = sb([P, HALF], U8, "x_scales%d%d" % (a, hf))
-            quantize(x_bf16[a, hf], x_codes[a, hf][:], x_scales[a, hf][:])
+            quantize(x_bf16[a, hf][:], x_codes[a, hf][:], x_scales[a, hf][:])
 
         picked_words, tab_codes = {}, {}
 
@@ -128,74 +141,79 @@ def tile_list_kernl_sigm_res_silu_kernel(
                 picked_words[g], word_window[:].bitcast(U32).indirect(offsets[:, 32 * g : 32 * (g + 1)])
             )
 
-        def part_words(g, a):
-            name = "tab_codes%d%d" % (g, a)
-            if g == 1:
-                tab_codes[g, a] = placed([P, PACK * 2 * COLS], U8, name, X10_BF16_AT + 1024 * a)
-            else:
-                tab_codes[g, a] = sb([P, PACK * 2 * COLS], U8, name, tag=(None, "x_bf16_00")[a])
-            parted = tab_codes[g, a][:].bitcast(U16).rearrange("p (t c i) -> p c t i", t=PACK, i=4)
+        def part_words(g, a, tile):
+            tab_codes[g, a] = tile
+            parted = tile[:].bitcast(U16).rearrange("p (t c i) -> p c t i", t=PACK, i=4)
             paired = picked_words[g].bitcast(U16).rearrange("p (c i t a) -> p a c t i", a=2, t=PACK, i=4)
             nc.vector.tensor_copy(parted, paired[:, a])
 
+        codes_shape = [P, PACK * 2 * COLS]
+        bf16_shape = [P, HALF, PACK]
         gather_words(0)
         gather_words(1)
-        part_words(0, 0)
-        interleave_x(0, 0, nc.scalar.copy)
+        part_words(0, 0, sb(codes_shape, U8, "tab_codes00"))
+        interleave_x(0, 0, placed(bf16_shape, BF16, "x_bf16_00", XB00_AT), nc.scalar.copy)
         quantize_x(0, 0)
-        part_words(0, 1)
-        interleave_x(1, 0, nc.scalar.copy)
+        part_words(0, 1, placed(codes_shape, U8, "tab_codes01", XB00_AT))
+        part_words(1, 0, placed(codes_shape, U8, "tab_codes10", XB00_AT + 1024))
+        interleave_x(1, 0, placed(bf16_shape, BF16, "x_bf16_10", XB10_AT), nc.scalar.copy)
         quantize_x(1, 0)
-        part_words(1, 0)
-        part_words(1, 1)
-        interleave_x(0, 1, nc.scalar.copy)
-        quantize_x(0, 1)
-        interleave_x(1, 1, nc.vector.tensor_copy)
+        part_words(1, 1, placed(codes_shape, U8, "tab_codes11", XB10_AT))
+        x01_halves = []
+        for m0, tag, copy in ((0, None, nc.scalar.copy), (COLS, "picked_words1", nc.vector.tensor_copy)):
+            half = sb([P, COLS, PACK], BF16, "x_bf16_01_%d" % m0, tag=tag)
+            copy(
+                half[:].rearrange("p (c i) t -> p c t i", i=4),
+                x_raw[0, 1][:, :, m0 : m0 + COLS].rearrange("p t (c i) -> p c t i", i=4),
+            )
+            x01_halves.append(half)
+        x_codes[0, 1] = sb([P, HALF], U32, "x_codes01")
+        x_scales[0, 1] = sb([P, HALF], U8, "x_scales01")
+        quantize(x01_halves[0][:], x_codes[0, 1][:, 0:COLS], x_scales[0, 1][:, 0:COLS])
+        quantize(x01_halves[1][:], x_codes[0, 1][:, COLS:HALF], x_scales[0, 1][:, COLS:HALF])
+        interleave_x(1, 1, sb(bf16_shape, BF16, "x_bf16_11"), nc.vector.tensor_copy)
         quantize_x(1, 1)
 
+        al8_rows = al8_words.rearrange("a p n i -> p a (n i)").bitcast(I32)
         al8_early = placed([P, N], I32, "al8_early", WORDS_AT)
         nc.sync.dma_start(al8_early[:], al8_rows[:, 0, :])
-        al4_codes = placed([P, 2, N // 2], I32, "al4_codes", WORDS_AT + 2048)
-        nc.sync.dma_start(al4_codes[:], al4_words.rearrange("a p n -> p a n").bitcast(I32))
         for w, scales in enumerate((al8_scales, al4_scales)):
             for r in range(4):
                 nc.sync.dma_start(
                     planes[r:P:32, w], scales.bitcast(I32)[:, r:16:4, :].rearrange("a q n -> q a n")
                 )
-        al8_late = sb([P, N], I32, "al8_late", tag="x_bf16_01")
+        al4_codes = placed([P, 2, N // 2], I32, "al4_codes", WORDS_AT + 2048)
+        nc.sync.dma_start(al4_codes[:], al4_words.rearrange("a p n -> p a n").bitcast(I32))
+        al8_late = sb([P, N], I32, "al8_late", tag="x_01")
         nc.sync.dma_start(al8_late[:], al8_rows[:, 1, :])
         b_sb = placed([P, N // P], F32, "b_sb", X11_AT)
         with nc.allow_non_contiguous_dma(reason="one bias value to a partition"):
             nc.sync.dma_start(b_sb[:], b.rearrange("(c p) -> p c", p=P))
 
-        def bank(index, name):
-            return psum.tile([P, 2 * HALF], F32, name=name, tag="bank%d" % index)
-
-        d = {}
+        d, logistic = {}, {}
 
         def first_product(hf, g):
-            d[hf, g] = [bank(PACK * g + t, "d%d%d%d" % (hf, g, t))[:, 0:HALF] for t in range(PACK)]
-            for a in range(2):
-                for t in range(PACK):
-                    codes = tab_codes[g, a][:, t * 2 * COLS : (t + 1) * 2 * COLS]
-                    nc.tensor.matmul_mx(
-                        d[hf, g][t],
-                        lhsT=codes.bitcast(FP4X4),
-                        lhsT_scale=tab_planes[a][:, (2 * t + g) * COLS : (2 * t + g + 1) * COLS],
-                        rhs=x_codes[a, hf][:].bitcast(FP8X4),
-                        rhs_scale=x_scales[a, hf][:],
-                        start=(a == 0),
-                        stop=(a == 1),
-                    )
-
-        logistic, h_bf16, h_codes, h_scales = {}, {}, {}, {}
+            if g == 0:
+                d[hf, g] = [bank(t, "d%d%d%d" % (hf, g, t))[:, 0:HALF] for t in range(PACK)]
+                order = [(a, t) for a in range(2) for t in range(PACK)]
+            else:
+                pair = [bank(4 + u, "d%d%d%d" % (hf, g, u)) for u in range(2)]
+                d[hf, g] = [pair[t // 2][:, (t % 2) * HALF : (t % 2 + 1) * HALF] for t in range(PACK)]
+                order = [(a, t) for t in range(PACK) for a in range(2)]
+            for a, t in order:
+                codes = tab_codes[g, a][:, t * 2 * COLS : (t + 1) * 2 * COLS]
+                nc.tensor.matmul_mx(
+                    d[hf, g][t],
+                    lhsT=codes.bitcast(FP4X4),
+                    lhsT_scale=tab_planes[a][:, (2 * t + g) * COLS : (2 * t + g + 1) * COLS],
+                    rhs=x_codes[a, hf][:].bitcast(FP8X4),
+                    rhs_scale=x_scales[a, hf][:],
+                    start=(a == 0),
+                    stop=(a == 1),
+                )
 
         def sigmoids(hf, g):
-            name = "logistic%d%d" % (hf, g)
-            if hf == 0:
-                logistic[hf, g] = placed([P, HALF // 4, PACK, 4], F32, name, X01_AT + 4096 * g)
-            else:
-                logistic[hf, g] = sb([P, HALF // 4, PACK, 4], F32, name)
+            logistic[hf, g] = sb([P, HALF // 4, PACK, 4], F32, "logistic%d%d" % (hf, g))
             for t in range(PACK):
                 nc.scalar.activation(
                     logistic[hf, g][:, :, t, :],
@@ -204,70 +222,70 @@ def tile_list_kernl_sigm_res_silu_kernel(
                     bias=cb_sb[:, g, t : t + 1],
                 )
 
-        def weigh(hf, g, m0):
-            piece = (4 * hf + 2 * g + m0 // COLS) % 3
-            h_bf16[hf, g, m0] = sb(
-                [P, COLS, PACK], BF16, "h_bf16_%d%d_%d" % (hf, g, m0), tag=("x_bf16_11", "h_b", "h_c")[piece]
-            )
-            nc.vector.tensor_tensor(
-                h_bf16[hf, g, m0][:].rearrange("p (c i) t -> p c t i", i=4),
-                logistic[hf, g][:, m0 // 4 : (m0 + COLS) // 4],
-                cw_sb[:, g, :].unsqueeze(1).unsqueeze(3).to_broadcast([P, COLS // 4, PACK, 4]),
-                ALU.mult,
-            )
-
-        def quantize_h(hf, g, m0):
-            if m0 == 0:
-                h_codes[hf, g] = sb([P, HALF], U32, "h_codes%d%d" % (hf, g), tag="h_codes%d" % g)
-                h_scales[hf, g] = sb([P, HALF], U8, "h_scales%d%d" % (hf, g))
-            quantize(h_bf16[hf, g, m0], h_codes[hf, g][:, m0 : m0 + COLS], h_scales[hf, g][:, m0 : m0 + COLS])
-
-        y_banks = {}
-
-        def second_product(hf, g, m0, width, c):
-            key = (hf, g)
-            if g == 0:
-                y_banks[hf, c] = bank(PACK * hf + c, "y%d%d" % (hf, c))[:, 0:HALF]
-            n0 = c * COLS
-            al8_codes = (al8_early, al8_late)[g][:, n0 : n0 + COLS]
-            nc.tensor.matmul_mx(
-                y_banks[hf, c][:, m0 : m0 + width],
-                lhsT=al8_codes.bitcast(FP8X4),
-                lhsT_scale=al_planes[0][:, g, n0 : n0 + COLS],
-                rhs=h_codes[key][:, m0 : m0 + width].bitcast(FP8X4),
-                rhs_scale=h_scales[key][:, m0 : m0 + width],
-                start=(g == 0),
-                stop=False,
-            )
-            nc.tensor.matmul_mx(
-                y_banks[hf, c][:, m0 : m0 + width],
-                lhsT=al4_codes[:, g, n0 // 2 : (n0 + COLS) // 2].bitcast(FP4X4),
-                lhsT_scale=al_planes[1][:, g, n0 : n0 + COLS],
-                rhs=h_codes[key][:, m0 : m0 + width].bitcast(FP8X4),
-                rhs_scale=h_scales[key][:, m0 : m0 + width],
-                start=False,
-                stop=(g == 1),
-            )
-
-        def finish(hf, c):
-            result = sb([P, HALF], F32, "result%d%d" % (hf, c))
-            nc.scalar.activation(result[:], y_banks[hf, c], ACT.Silu, bias=b_sb[:, c : c + 1])
-            queue = nc.scalar if (hf, c) == (1, 3) else nc.sync
-            queue.dma_start(out[c * COLS : (c + 1) * COLS, hf * HALF : (hf + 1) * HALF], result[:])
-
         for hf in range(2):
             for g in range(2):
                 first_product(hf, g)
                 sigmoids(hf, g)
-        pieces = [(hf, g, m0) for hf in range(2) for g in range(2) for m0 in range(0, HALF, COLS)]
-        weigh(*pieces[0])
-        for n, (hf, g, m0) in enumerate(pieces):
-            if n + 1 < len(pieces):
-                weigh(*pieces[n + 1])
-            quantize_h(hf, g, m0)
-            if m0 > 0:
-                for c in range(N // COLS):
-                    second_product(hf, g, 0, HALF, c)
+
+        h_bf16 = {}
+
+        def weigh(engine, weights, hf, g, m0, m1):
+            engine.tensor_tensor(
+                h_bf16[hf, g][:, m0:m1, :].rearrange("p (c i) t -> p c t i", i=4),
+                logistic[hf, g][:, m0 // 4 : m1 // 4],
+                weights[:, g, :].unsqueeze(1).unsqueeze(3).to_broadcast([P, (m1 - m0) // 4, PACK, 4]),
+                ALU.mult,
+            )
+
+        y = {}
+
+        def second_product(hf, g, h_codes, h_scales):
+            if g == 0 and hf == 0:
+                pair = [bank(index, "y0_%d" % index) for index in (6, 0)]
+                y[0] = [pair[c // 2][:, (c % 2) * HALF : (c % 2 + 1) * HALF] for c in range(4)]
+            elif g == 0:
+                y[1] = [bank(1 + c, "y1_%d" % c)[:, 0:HALF] for c in range(4)]
+            for c in range(N // COLS):
+                n0 = c * COLS
+                nc.tensor.matmul_mx(
+                    y[hf][c],
+                    lhsT=(al8_early, al8_late)[g][:, n0 : n0 + COLS].bitcast(FP8X4),
+                    lhsT_scale=al_planes[0][:, g, n0 : n0 + COLS],
+                    rhs=h_codes[:].bitcast(FP8X4),
+                    rhs_scale=h_scales[:],
+                    start=(g == 0 and (hf == 1 or c % 2 == 0)),
+                    stop=False,
+                )
+                nc.tensor.matmul_mx(
+                    y[hf][c],
+                    lhsT=al4_codes[:, g, n0 // 2 : (n0 + COLS) // 2].bitcast(FP4X4),
+                    lhsT_scale=al_planes[1][:, g, n0 : n0 + COLS],
+                    rhs=h_codes[:].bitcast(FP8X4),
+                    rhs_scale=h_scales[:],
+                    start=False,
+                    stop=(g == 1 and (hf == 1 or c % 2 == 1)),
+                )
+
+        tiles = [(hf, g) for hf in range(2) for g in range(2)]
+        for n, (hf, g) in enumerate(tiles):
+            h_bf16[hf, g] = sb(bf16_shape, BF16, "h_bf16_%d%d" % (hf, g), tag=("picked_words1", "x_bf16_11")[n % 2])
+            if n == 0:
+                weigh(nc.vector, cw_ps, hf, g, 0, COLS)
+            else:
+                weigh(nc.gpsimd, cw_sb, hf, g, 0, POOL_COLS)
+                weigh(nc.vector, cw_ps, hf, g, POOL_COLS, COLS)
+            weigh(nc.vector, cw_ps, hf, g, COLS, HALF)
+            h_codes = sb([P, HALF], U32, "h_codes%d%d" % (hf, g), tag="h_codes%d" % g)
+            h_scales = sb([P, HALF], U8, "h_scales%d%d" % (hf, g))
+            for m0 in range(0, HALF, COLS):
+                quantize(
+                    h_bf16[hf, g][:, m0 : m0 + COLS, :], h_codes[:, m0 : m0 + COLS], h_scales[:, m0 : m0 + COLS]
+                )
+            second_product(hf, g, h_codes, h_scales)
+
         for hf in range(2):
             for c in range(N // COLS):
-                finish(hf, c)
+                result = sb([P, HALF], F32, "result%d%d" % (hf, c))
+                nc.scalar.activation(result[:], y[hf][c], ACT.Silu, bias=b_sb[:, c : c + 1])
+                queue = nc.scalar if (hf, c) == (1, 3) else nc.sync
+                queue.dma_start(out[c * COLS : (c + 1) * COLS, hf * HALF : (hf + 1) * HALF], result[:])

@@ -22,7 +22,7 @@ PACK = 4
 KP = P * PACK
 HALF = M // 2
 COLS = 128
-POOL_COLS = 64
+POOL_COLS = 56
 
 
 def tile_list_kernl_sigm_res_silu_kernel(
@@ -43,18 +43,20 @@ def tile_list_kernl_sigm_res_silu_kernel(
         def bank(index, name):
             return psum.tile([P, 2 * HALF], F32, name=name, tag="bank%d" % index)
 
-        WORDS_AT, PLANES_AT, TURNED_AT, X11_AT, XB00_AT, XB10_AT = 0, 16384, 18432, 18944, 23040, 25088
+        WORDS_AT, WINDOW_AT, PLANES_AT, X11_AT = 0, 16384, 19456, 21504
+        X00_AT, X10_AT, X11_BF16_AT = 25600, 29696, 33792
 
         cb_sb = sb([P, 2, PACK], F32, "cb_sb")
-        nc.scalar.dma_start(cb_sb[:], cb.rearrange("(a p t) -> p a t", a=2, t=PACK))
         cw_square = sb([P, P], F32, "cw_square")
         cw_sb = cw_square[:, 0 : 2 * PACK].rearrange("p (a t) -> p a t", a=2)
+        nc.scalar.dma_start(cb_sb[:], cb.rearrange("(a p t) -> p a t", a=2, t=PACK))
         nc.scalar.dma_start(cw_sb, cw.rearrange("(a p t) -> p a t", a=2, t=PACK))
 
         offsets = held.tile([P, J // 16], U16, name="offsets")
         nc.sync.dma_start(offsets[:], offs)
-        scale_window = sb([P, T // 4], I32, "scale_window")
+        scale_window = placed([P, T // 4], I32, "scale_window", WINDOW_AT)
         nc.sync.dma_start(scale_window[0:32, :], tab_scales.rearrange("a q t -> (a q) t").bitcast(I32))
+        al8_rows = al8_words.rearrange("a p n i -> p a (n i)").bitcast(I32)
         word_window = placed([P, T], I32, "word_window", WORDS_AT)
         nc.sync.dma_start(word_window[:], tab_words[0].rearrange("p t b -> p (t b)").bitcast(I32))
 
@@ -65,8 +67,8 @@ def tile_list_kernl_sigm_res_silu_kernel(
             rows = x[a * KP : (a + 1) * KP, hf * HALF : (hf + 1) * HALF]
             nc.sync.dma_start(tile, rows.rearrange("(p i) m -> p i m", i=PACK))
 
-        load_x(0, 0, sb([P, PACK, HALF], F32, "x_00")[:])
-        load_x(1, 0, sb([P, PACK, HALF], F32, "x_10")[:])
+        load_x(0, 0, placed([P, PACK, HALF], F32, "x_00", X00_AT)[:])
+        load_x(1, 0, placed([P, PACK, HALF], F32, "x_10", X10_AT)[:])
         load_x(0, 1, sb([P, PACK, HALF], F32, "x_01")[:])
 
         warm_in = sb([P, 32], F32, "warm_in")
@@ -81,11 +83,16 @@ def tile_list_kernl_sigm_res_silu_kernel(
 
         identity = sb([P, P], F32, "identity")
         make_identity(nc, identity[:])
-        nc.vector.memset(cw_square[:, 2 * PACK : P], 0.0)
+        nc.gpsimd.memset(cw_square[:, 2 * PACK : P], 0.0)
         cw_turned_ps = bank(6, "cw_turned_ps")[:, 0:P]
         nc.tensor.transpose(cw_turned_ps, cw_square[:], identity[:])
+        cw_turned = sb([P, P], F32, "cw_turned")
+        nc.scalar.copy(cw_turned[:], cw_turned_ps)
+        cw_bank = bank(7, "cw_bank")[:, 0:P]
+        nc.tensor.transpose(cw_bank, cw_turned[:], identity[:])
+        cw_ps = cw_bank[:, 0 : 2 * PACK].rearrange("p (a t) -> p a t", a=2)
 
-        picked_scales = placed([P, 2 * J], U8, "picked_scales", TURNED_AT - J)[:, 0:J]
+        picked_scales = placed([P, 2 * J], U8, "picked_scales", X11_AT - J)[:, 0:J]
         for g in range(2):
             nc.vector.tensor_copy(
                 picked_scales[:, g * KP : (g + 1) * KP],
@@ -106,24 +113,17 @@ def tile_list_kernl_sigm_res_silu_kernel(
 
         load_x(1, 1, placed([P, PACK, HALF], F32, "x_11", X11_AT)[:])
 
-        cw_turned = placed([P, P], F32, "cw_turned", TURNED_AT)
-        nc.scalar.copy(cw_turned[:], cw_turned_ps)
-        cw_bank = bank(7, "cw_bank")[:, 0:P]
-        nc.tensor.transpose(cw_bank, cw_turned[:], identity[:])
-        cw_ps = cw_bank[:, 0 : 2 * PACK].rearrange("p (a t) -> p a t", a=2)
-
         planes = placed([P, 2, 2, N // 4], I32, "al_planes", PLANES_AT)
-        nc.vector.memset(planes[:], 0)
         al_planes = [planes[:, w].bitcast(U8) for w in range(2)]
 
         x_bf16, x_codes, x_scales = {}, {}, {}
 
-        def interleave_x(a, hf, tile, copy):
-            x_bf16[a, hf] = tile
-            copy(
-                tile[:].rearrange("p (c i) t -> p c t i", i=4),
-                x_raw[a, hf].rearrange("p t (c i) -> p c t i", i=4),
-            )
+        def interleave(tile, raw, copy):
+            copy(tile.rearrange("p (c i) t -> p c t i", i=2), raw.rearrange("p t (c i) -> p c t i", i=2))
+
+        def interleave_x(a, hf):
+            x_bf16[a, hf] = sb([P, HALF, PACK], BF16, "x_bf16_%d%d" % (a, hf))
+            interleave(x_bf16[a, hf][:], x_raw[a, hf], nc.scalar.copy)
 
         def quantize(src, codes, scales):
             nc.vector.quantize_mx(codes.bitcast(FP8X4), scales, src.rearrange("p m t -> p (m t)"))
@@ -143,54 +143,56 @@ def tile_list_kernl_sigm_res_silu_kernel(
 
         def part_words(g, a, tile):
             tab_codes[g, a] = tile
-            parted = tile[:].bitcast(U16).rearrange("p (t c i) -> p c t i", t=PACK, i=4)
+            parted = tab_codes[g, a][:].bitcast(U16).rearrange("p (t c i) -> p c t i", t=PACK, i=4)
             paired = picked_words[g].bitcast(U16).rearrange("p (c i t a) -> p a c t i", a=2, t=PACK, i=4)
             nc.vector.tensor_copy(parted, paired[:, a])
 
         codes_shape = [P, PACK * 2 * COLS]
-        bf16_shape = [P, HALF, PACK]
         gather_words(0)
         gather_words(1)
         part_words(0, 0, sb(codes_shape, U8, "tab_codes00"))
-        interleave_x(0, 0, placed(bf16_shape, BF16, "x_bf16_00", XB00_AT), nc.scalar.copy)
+        interleave_x(0, 0)
         quantize_x(0, 0)
-        part_words(0, 1, placed(codes_shape, U8, "tab_codes01", XB00_AT))
-        part_words(1, 0, placed(codes_shape, U8, "tab_codes10", XB00_AT + 1024))
-        interleave_x(1, 0, placed(bf16_shape, BF16, "x_bf16_10", XB10_AT), nc.scalar.copy)
+        part_words(0, 1, placed(codes_shape, U8, "tab_codes01", X00_AT))
+        part_words(1, 1, placed(codes_shape, U8, "tab_codes11", X00_AT + 1024))
+        interleave_x(1, 0)
         quantize_x(1, 0)
-        part_words(1, 1, placed(codes_shape, U8, "tab_codes11", XB10_AT))
-        x01_halves = []
-        for m0, tag, copy in ((0, None, nc.scalar.copy), (COLS, "picked_words1", nc.vector.tensor_copy)):
-            half = sb([P, COLS, PACK], BF16, "x_bf16_01_%d" % m0, tag=tag)
-            copy(
-                half[:].rearrange("p (c i) t -> p c t i", i=4),
-                x_raw[0, 1][:, :, m0 : m0 + COLS].rearrange("p t (c i) -> p c t i", i=4),
-            )
-            x01_halves.append(half)
+        part_words(1, 0, placed(codes_shape, U8, "tab_codes10", X10_AT))
         x_codes[0, 1] = sb([P, HALF], U32, "x_codes01")
         x_scales[0, 1] = sb([P, HALF], U8, "x_scales01")
-        quantize(x01_halves[0][:], x_codes[0, 1][:, 0:COLS], x_scales[0, 1][:, 0:COLS])
-        quantize(x01_halves[1][:], x_codes[0, 1][:, COLS:HALF], x_scales[0, 1][:, COLS:HALF])
-        interleave_x(1, 1, sb(bf16_shape, BF16, "x_bf16_11"), nc.vector.tensor_copy)
-        quantize_x(1, 1)
+        x01_halves = {
+            0: sb([P, COLS, PACK], BF16, "x_bf16_01_0"),
+            COLS: placed([P, COLS, PACK], BF16, "x_bf16_01_128", X10_AT + 1024),
+        }
+        for m0, copy in ((0, nc.scalar.copy), (COLS, nc.vector.tensor_copy)):
+            interleave(x01_halves[m0][:], x_raw[0, 1][:, :, m0 : m0 + COLS], copy)
+        for m0 in (0, COLS):
+            quantize(x01_halves[m0][:], x_codes[0, 1][:, m0 : m0 + COLS], x_scales[0, 1][:, m0 : m0 + COLS])
+        x_codes[1, 1] = sb([P, HALF], U32, "x_codes11")
+        x_scales[1, 1] = sb([P, HALF], U8, "x_scales11")
+        x11_halves = {}
+        for m0 in (0, COLS):
+            x11_halves[m0] = placed([P, COLS, PACK], BF16, "x_bf16_11_%d" % m0, X11_BF16_AT + 8 * m0)
+            interleave(x11_halves[m0][:], x_raw[1, 1][:, :, m0 : m0 + COLS], nc.vector.tensor_copy)
+        for m0 in (0, COLS):
+            quantize(x11_halves[m0][:], x_codes[1, 1][:, m0 : m0 + COLS], x_scales[1, 1][:, m0 : m0 + COLS])
 
-        al8_rows = al8_words.rearrange("a p n i -> p a (n i)").bitcast(I32)
         al8_early = placed([P, N], I32, "al8_early", WORDS_AT)
         nc.sync.dma_start(al8_early[:], al8_rows[:, 0, :])
+        al4_codes = placed([P, 2, N // 2], I32, "al4_codes", WORDS_AT + 2048)
+        nc.sync.dma_start(al4_codes[:], al4_words.rearrange("a p n -> p a n").bitcast(I32))
         for w, scales in enumerate((al8_scales, al4_scales)):
             for r in range(4):
                 nc.sync.dma_start(
                     planes[r:P:32, w], scales.bitcast(I32)[:, r:16:4, :].rearrange("a q n -> q a n")
                 )
-        al4_codes = placed([P, 2, N // 2], I32, "al4_codes", WORDS_AT + 2048)
-        nc.sync.dma_start(al4_codes[:], al4_words.rearrange("a p n -> p a n").bitcast(I32))
-        al8_late = sb([P, N], I32, "al8_late", tag="x_01")
+        al8_late = placed([P, N], I32, "al8_late", X10_AT + 1024)
         nc.sync.dma_start(al8_late[:], al8_rows[:, 1, :])
         b_sb = placed([P, N // P], F32, "b_sb", X11_AT)
         with nc.allow_non_contiguous_dma(reason="one bias value to a partition"):
             nc.sync.dma_start(b_sb[:], b.rearrange("(c p) -> p c", p=P))
 
-        d, logistic = {}, {}
+        d = {}
 
         def first_product(hf, g):
             if g == 0:
@@ -212,80 +214,86 @@ def tile_list_kernl_sigm_res_silu_kernel(
                     stop=(a == 1),
                 )
 
+        logistic, h_codes, h_scales = {}, {}, {}
+
         def sigmoids(hf, g):
-            logistic[hf, g] = sb([P, HALF // 4, PACK, 4], F32, "logistic%d%d" % (hf, g))
+            name = "logistic%d%d" % (hf, g)
+            logistic[hf, g] = sb([P, PACK, HALF], F32, name)
             for t in range(PACK):
                 nc.scalar.activation(
-                    logistic[hf, g][:, :, t, :],
-                    d[hf, g][t].rearrange("p (c i) -> p c i", i=4),
+                    logistic[hf, g][:, t, :],
+                    d[hf, g][t],
                     ACT.Sigmoid,
                     bias=cb_sb[:, g, t : t + 1],
                 )
+
+        h_bf16 = placed([P, HALF, PACK], BF16, "h_bf16", X11_BF16_AT - 1024)
+
+        def weigh(engine, weights, hf, g, m0, m1):
+            engine.tensor_tensor(
+                h_bf16[:, m0:m1, :].rearrange("p (c i) t -> p c t i", i=2),
+                logistic[hf, g][:, :, m0:m1].rearrange("p t (c i) -> p c t i", i=2),
+                weights[:, g, :].unsqueeze(1).unsqueeze(3).to_broadcast([P, (m1 - m0) // 2, PACK, 2]),
+                ALU.mult,
+            )
+
+        def quantize_h(hf, g, m0):
+            if m0 == 0:
+                h_codes[hf, g] = sb([P, HALF], U32, "h_codes%d%d" % (hf, g), tag="h_codes%d" % g)
+                h_scales[hf, g] = sb([P, HALF], U8, "h_scales%d%d" % (hf, g))
+            quantize(
+                h_bf16[:, m0 : m0 + COLS, :], h_codes[hf, g][:, m0 : m0 + COLS], h_scales[hf, g][:, m0 : m0 + COLS]
+            )
+
+        y_banks = {}
+
+        def second_product(hf, g, m0, width, c):
+            key = (hf, g)
+            if g == 0 and hf == 1:
+                y_banks[hf, c] = bank(1 + c, "y%d%d" % (hf, c))[:, 0:HALF]
+            elif g == 0 and c % 2 == 0:
+                pair = bank((6, 0)[c // 2], "y%d%d" % (hf, c))
+                y_banks[hf, c], y_banks[hf, c + 1] = pair[:, 0:HALF], pair[:, HALF : 2 * HALF]
+            n0 = c * COLS
+            al8_codes = (al8_early, al8_late)[g][:, n0 : n0 + COLS]
+            nc.tensor.matmul_mx(
+                y_banks[hf, c][:, m0 : m0 + width],
+                lhsT=al8_codes.bitcast(FP8X4),
+                lhsT_scale=al_planes[0][:, g, n0 : n0 + COLS],
+                rhs=h_codes[key][:, m0 : m0 + width].bitcast(FP8X4),
+                rhs_scale=h_scales[key][:, m0 : m0 + width],
+                start=(g == 0 and (hf == 1 or c % 2 == 0)),
+                stop=False,
+            )
+            nc.tensor.matmul_mx(
+                y_banks[hf, c][:, m0 : m0 + width],
+                lhsT=al4_codes[:, g, n0 // 2 : (n0 + COLS) // 2].bitcast(FP4X4),
+                lhsT_scale=al_planes[1][:, g, n0 : n0 + COLS],
+                rhs=h_codes[key][:, m0 : m0 + width].bitcast(FP8X4),
+                rhs_scale=h_scales[key][:, m0 : m0 + width],
+                start=False,
+                stop=(g == 1 and (hf == 1 or c % 2 == 1)),
+            )
+
+        def finish(hf, c):
+            result = sb([P, HALF], F32, "result%d%d" % (hf, c))
+            nc.scalar.activation(result[:], y_banks[hf, c], ACT.Silu, bias=b_sb[:, c : c + 1])
+            queue = nc.scalar if (hf, c) == (1, 3) else nc.sync
+            queue.dma_start(out[c * COLS : (c + 1) * COLS, hf * HALF : (hf + 1) * HALF], result[:])
 
         for hf in range(2):
             for g in range(2):
                 first_product(hf, g)
                 sigmoids(hf, g)
-
-        h_bf16 = {}
-
-        def weigh(engine, weights, hf, g, m0, m1):
-            engine.tensor_tensor(
-                h_bf16[hf, g][:, m0:m1, :].rearrange("p (c i) t -> p c t i", i=4),
-                logistic[hf, g][:, m0 // 4 : m1 // 4],
-                weights[:, g, :].unsqueeze(1).unsqueeze(3).to_broadcast([P, (m1 - m0) // 4, PACK, 4]),
-                ALU.mult,
-            )
-
-        y = {}
-
-        def second_product(hf, g, h_codes, h_scales):
-            if g == 0 and hf == 0:
-                pair = [bank(index, "y0_%d" % index) for index in (6, 0)]
-                y[0] = [pair[c // 2][:, (c % 2) * HALF : (c % 2 + 1) * HALF] for c in range(4)]
-            elif g == 0:
-                y[1] = [bank(1 + c, "y1_%d" % c)[:, 0:HALF] for c in range(4)]
-            for c in range(N // COLS):
-                n0 = c * COLS
-                nc.tensor.matmul_mx(
-                    y[hf][c],
-                    lhsT=(al8_early, al8_late)[g][:, n0 : n0 + COLS].bitcast(FP8X4),
-                    lhsT_scale=al_planes[0][:, g, n0 : n0 + COLS],
-                    rhs=h_codes[:].bitcast(FP8X4),
-                    rhs_scale=h_scales[:],
-                    start=(g == 0 and (hf == 1 or c % 2 == 0)),
-                    stop=False,
-                )
-                nc.tensor.matmul_mx(
-                    y[hf][c],
-                    lhsT=al4_codes[:, g, n0 // 2 : (n0 + COLS) // 2].bitcast(FP4X4),
-                    lhsT_scale=al_planes[1][:, g, n0 : n0 + COLS],
-                    rhs=h_codes[:].bitcast(FP8X4),
-                    rhs_scale=h_scales[:],
-                    start=False,
-                    stop=(g == 1 and (hf == 1 or c % 2 == 1)),
-                )
-
-        tiles = [(hf, g) for hf in range(2) for g in range(2)]
-        for n, (hf, g) in enumerate(tiles):
-            h_bf16[hf, g] = sb(bf16_shape, BF16, "h_bf16_%d%d" % (hf, g), tag=("picked_words1", "x_bf16_11")[n % 2])
-            if n == 0:
-                weigh(nc.vector, cw_ps, hf, g, 0, COLS)
-            else:
+        for hf in range(2):
+            for g in range(2):
                 weigh(nc.gpsimd, cw_sb, hf, g, 0, POOL_COLS)
                 weigh(nc.vector, cw_ps, hf, g, POOL_COLS, COLS)
-            weigh(nc.vector, cw_ps, hf, g, COLS, HALF)
-            h_codes = sb([P, HALF], U32, "h_codes%d%d" % (hf, g), tag="h_codes%d" % g)
-            h_scales = sb([P, HALF], U8, "h_scales%d%d" % (hf, g))
-            for m0 in range(0, HALF, COLS):
-                quantize(
-                    h_bf16[hf, g][:, m0 : m0 + COLS, :], h_codes[:, m0 : m0 + COLS], h_scales[:, m0 : m0 + COLS]
-                )
-            second_product(hf, g, h_codes, h_scales)
-
+                weigh(nc.vector, cw_ps, hf, g, COLS, HALF)
+                for m0 in (0, COLS):
+                    quantize_h(hf, g, m0)
+                for c in range(N // COLS):
+                    second_product(hf, g, 0, HALF, c)
         for hf in range(2):
             for c in range(N // COLS):
-                result = sb([P, HALF], F32, "result%d%d" % (hf, c))
-                nc.scalar.activation(result[:], y[hf][c], ACT.Silu, bias=b_sb[:, c : c + 1])
-                queue = nc.scalar if (hf, c) == (1, 3) else nc.sync
-                queue.dma_start(out[c * COLS : (c + 1) * COLS, hf * HALF : (hf + 1) * HALF], result[:])
+                finish(hf, c)

@@ -43,8 +43,8 @@ def tile_list_kernl_sigm_res_silu_kernel(
         def bank(index, name):
             return psum.tile([P, 2 * HALF], F32, name=name, tag="bank%d" % index)
 
-        WORDS_AT, WINDOW_AT, PLANES_AT, X11_AT = 0, 16384, 19456, 21504
-        X00_AT, X10_AT, X11_BF16_AT = 25600, 29696, 33792
+        WORDS_AT, WINDOW_AT, PLANES_AT, TURNED_AT, X11_AT = 0, 16384, 19456, 21504, 22016
+        X00_AT, X10_AT, X11_BF16_AT = 26112, 30208, 34304
 
         cb_sb = sb([P, 2, PACK], F32, "cb_sb")
         cw_square = sb([P, P], F32, "cw_square")
@@ -78,21 +78,14 @@ def tile_list_kernl_sigm_res_silu_kernel(
 
         nc.vector.memset(scale_window[32:64, :], 0)
         nc.vector.memset(scale_window[64:P, :], 0)
-        tab_plane1 = sb([P, J // 4], I32, "tab_plane1")
-        nc.vector.memset(tab_plane1[:], 0)
 
         identity = sb([P, P], F32, "identity")
         make_identity(nc, identity[:])
         nc.gpsimd.memset(cw_square[:, 2 * PACK : P], 0.0)
         cw_turned_ps = bank(6, "cw_turned_ps")[:, 0:P]
         nc.tensor.transpose(cw_turned_ps, cw_square[:], identity[:])
-        cw_turned = sb([P, P], F32, "cw_turned")
-        nc.scalar.copy(cw_turned[:], cw_turned_ps)
-        cw_bank = bank(7, "cw_bank")[:, 0:P]
-        nc.tensor.transpose(cw_bank, cw_turned[:], identity[:])
-        cw_ps = cw_bank[:, 0 : 2 * PACK].rearrange("p (a t) -> p a t", a=2)
 
-        picked_scales = placed([P, 2 * J], U8, "picked_scales", X11_AT - J)[:, 0:J]
+        picked_scales = placed([P, 2 * J], U8, "picked_scales", TURNED_AT - J)[:, 0:J]
         for g in range(2):
             nc.vector.tensor_copy(
                 picked_scales[:, g * KP : (g + 1) * KP],
@@ -104,6 +97,7 @@ def tile_list_kernl_sigm_res_silu_kernel(
                 tab_plane0[:].bitcast(U8).rearrange("p (t g c i) -> p g c t i", t=PACK, g=2, i=16)[:, g],
                 picked_scales[:, g * KP : (g + 1) * KP].rearrange("p (c i t) -> p c t i", t=PACK, i=16),
             )
+        tab_plane1 = placed([P, J // 4], I32, "tab_plane1", WINDOW_AT)
         for q in range(1, 4):
             nc.scalar.dma_start(tab_plane0[32 * q : 32 * q + 4, :], tab_plane0[4 * q : 4 * q + 4, :])
         for q in range(4):
@@ -112,6 +106,28 @@ def tile_list_kernl_sigm_res_silu_kernel(
         tab_planes = (tab_plane0[:].bitcast(U8), tab_plane1[:].bitcast(U8))
 
         load_x(1, 1, placed([P, PACK, HALF], F32, "x_11", X11_AT)[:])
+
+        cw_turned = placed([P, P], F32, "cw_turned", TURNED_AT)
+        nc.scalar.copy(cw_turned[:], cw_turned_ps)
+        cw_bank = bank(7, "cw_bank")[:, 0:P]
+        nc.tensor.transpose(cw_bank, cw_turned[:], identity[:])
+        cw_ps = cw_bank[:, 0 : 2 * PACK].rearrange("p (a t) -> p a t", a=2)
+
+        x11_codes = sb([P, HALF], U32, "x_codes11")
+        x11_scales = sb([P, HALF], U8, "x_scales11")
+        nc.vector.memset(x11_codes[:].bitcast(I32), 0)
+        nc.vector.memset(x11_scales[:].bitcast(I32), 0)
+        warm_bank = bank(6, "warm_bank")[:, 0:HALF]
+        for n in range(6):
+            nc.tensor.matmul_mx(
+                warm_bank,
+                lhsT=x11_codes[:, 0:COLS].bitcast(FP8X4),
+                lhsT_scale=x11_scales[:, 0:COLS],
+                rhs=x11_codes[:].bitcast(FP8X4),
+                rhs_scale=x11_scales[:],
+                start=True,
+                stop=True,
+            )
 
         planes = placed([P, 2, 2, N // 4], I32, "al_planes", PLANES_AT)
         al_planes = [planes[:, w].bitcast(U8) for w in range(2)]
@@ -168,8 +184,7 @@ def tile_list_kernl_sigm_res_silu_kernel(
             interleave(x01_halves[m0][:], x_raw[0, 1][:, :, m0 : m0 + COLS], copy)
         for m0 in (0, COLS):
             quantize(x01_halves[m0][:], x_codes[0, 1][:, m0 : m0 + COLS], x_scales[0, 1][:, m0 : m0 + COLS])
-        x_codes[1, 1] = sb([P, HALF], U32, "x_codes11")
-        x_scales[1, 1] = sb([P, HALF], U8, "x_scales11")
+        x_codes[1, 1], x_scales[1, 1] = x11_codes, x11_scales
         x11_halves = {}
         for m0 in (0, COLS):
             x11_halves[m0] = placed([P, COLS, PACK], BF16, "x_bf16_11_%d" % m0, X11_BF16_AT + 8 * m0)

@@ -46,11 +46,10 @@ def tile_list_kernl_sigm_res_silu_kernel(
         WORDS_AT, WINDOW_AT, PLANES_AT, TURNED_AT, X11_AT = 0, 16384, 19456, 21504, 22016
         X00_AT, X10_AT, X11_BF16_AT = 26112, 30208, 34304
 
-        cb_sb = sb([P, 2, PACK], F32, "cb_sb")
-        cw_square = sb([P, P], F32, "cw_square")
-        cw_sb = cw_square[:, 0 : 2 * PACK].rearrange("p (a t) -> p a t", a=2)
-        nc.scalar.dma_start(cb_sb[:], cb.rearrange("(a p t) -> p a t", a=2, t=PACK))
-        nc.scalar.dma_start(cw_sb, cw.rearrange("(a p t) -> p a t", a=2, t=PACK))
+        rows = sb([P, KP], F32, "rows")
+        nc.scalar.dma_start(rows[124:126, :], cb.rearrange("(g j) -> g j", g=2))
+        nc.scalar.dma_start(rows[126:128, :], cw.rearrange("(g j) -> g j", g=2))
+        nc.gpsimd.memset(rows[0:124, :], 0.0)
 
         offsets = held.tile([P, J // 16], U16, name="offsets")
         nc.sync.dma_start(offsets[:], offs)
@@ -64,8 +63,8 @@ def tile_list_kernl_sigm_res_silu_kernel(
 
         def load_x(a, hf, tile):
             x_raw[a, hf] = tile
-            rows = x[a * KP : (a + 1) * KP, hf * HALF : (hf + 1) * HALF]
-            nc.sync.dma_start(tile, rows.rearrange("(p i) m -> p i m", i=PACK))
+            part = x[a * KP : (a + 1) * KP, hf * HALF : (hf + 1) * HALF]
+            nc.sync.dma_start(tile, part.rearrange("(p i) m -> p i m", i=PACK))
 
         load_x(0, 0, placed([P, PACK, HALF], F32, "x_00", X00_AT)[:])
         load_x(1, 0, placed([P, PACK, HALF], F32, "x_10", X10_AT)[:])
@@ -81,9 +80,11 @@ def tile_list_kernl_sigm_res_silu_kernel(
 
         identity = sb([P, P], F32, "identity")
         make_identity(nc, identity[:])
-        nc.gpsimd.memset(cw_square[:, 2 * PACK : P], 0.0)
-        cw_turned_ps = bank(6, "cw_turned_ps")[:, 0:P]
-        nc.tensor.transpose(cw_turned_ps, cw_square[:], identity[:])
+        vec_bank, cw_bank = bank(6, "vec_bank"), bank(7, "cw_bank")
+        for turned in (vec_bank, cw_bank):
+            for t in range(PACK):
+                nc.tensor.transpose(turned[:, t : KP : PACK], rows[:, t : KP : PACK], identity[:])
+        cw_ps = cw_bank[:, 126 * PACK : KP].rearrange("p (a t) -> p a t", a=2)
 
         picked_scales = placed([P, 2 * J], U8, "picked_scales", TURNED_AT - J)[:, 0:J]
         for g in range(2):
@@ -107,11 +108,9 @@ def tile_list_kernl_sigm_res_silu_kernel(
 
         load_x(1, 1, placed([P, PACK, HALF], F32, "x_11", X11_AT)[:])
 
-        cw_turned = placed([P, P], F32, "cw_turned", TURNED_AT)
-        nc.scalar.copy(cw_turned[:], cw_turned_ps)
-        cw_bank = bank(7, "cw_bank")[:, 0:P]
-        nc.tensor.transpose(cw_bank, cw_turned[:], identity[:])
-        cw_ps = cw_bank[:, 0 : 2 * PACK].rearrange("p (a t) -> p a t", a=2)
+        vec_sb = placed([P, 4, PACK], F32, "vec_sb", TURNED_AT)
+        nc.scalar.copy(vec_sb[:].rearrange("p r t -> p (r t)"), vec_bank[:, 124 * PACK : KP])
+        cb_sb, cw_sb = vec_sb[:, 0:2, :], vec_sb[:, 2:4, :]
 
         x11_codes = sb([P, HALF], U32, "x_codes11")
         x11_scales = sb([P, HALF], U8, "x_scales11")

@@ -22,7 +22,7 @@ PACK = 4
 KP = P * PACK
 HALF = M // 2
 COLS = 128
-POOL_COLS = 56
+POOL_COLS = 48
 
 
 def tile_list_kernl_sigm_res_silu_kernel(
@@ -44,7 +44,7 @@ def tile_list_kernl_sigm_res_silu_kernel(
             return psum.tile([P, 2 * HALF], F32, name=name, tag="bank%d" % index)
 
         WORDS_AT, WINDOW_AT, PLANES_AT, TURNED_AT, X11_AT = 0, 16384, 19456, 21504, 22016
-        X00_AT, X10_AT, X11_BF16_AT = 26112, 30208, 34304
+        X00_AT, X10_AT, X11_BF16_AT = 26112, 30208, 35328
 
         rows = sb([P, KP], F32, "rows")
         nc.scalar.dma_start(rows[124:126, :], cb.rearrange("(g j) -> g j", g=2))
@@ -172,7 +172,6 @@ def tile_list_kernl_sigm_res_silu_kernel(
         part_words(1, 1, placed(codes_shape, U8, "tab_codes11", X00_AT + 1024))
         interleave_x(1, 0)
         quantize_x(1, 0)
-        part_words(1, 0, placed(codes_shape, U8, "tab_codes10", X10_AT))
         x_codes[0, 1] = sb([P, HALF], U32, "x_codes01")
         x_scales[0, 1] = sb([P, HALF], U8, "x_scales01")
         x01_halves = {
@@ -181,6 +180,7 @@ def tile_list_kernl_sigm_res_silu_kernel(
         }
         for m0, copy in ((0, nc.scalar.copy), (COLS, nc.vector.tensor_copy)):
             interleave(x01_halves[m0][:], x_raw[0, 1][:, :, m0 : m0 + COLS], copy)
+        part_words(1, 0, placed(codes_shape, U8, "tab_codes10", X10_AT))
         for m0 in (0, COLS):
             quantize(x01_halves[m0][:], x_codes[0, 1][:, m0 : m0 + COLS], x_scales[0, 1][:, m0 : m0 + COLS])
         x_codes[1, 1], x_scales[1, 1] = x11_codes, x11_scales
@@ -241,23 +241,29 @@ def tile_list_kernl_sigm_res_silu_kernel(
                     bias=cb_sb[:, g, t : t + 1],
                 )
 
-        h_bf16 = placed([P, HALF, PACK], BF16, "h_bf16", X11_BF16_AT - 1024)
+        h_shared = placed([P, COLS, PACK], BF16, "h_shared", X11_BF16_AT + 1024)
+        ring = ctx.enter_context(tc.tile_pool(name="ring", bufs=1))
 
-        def weigh(engine, weights, hf, g, m0, m1):
+        def weigh(engine, weights, hf, g, tile, m0, m1):
             engine.tensor_tensor(
-                h_bf16[:, m0:m1, :].rearrange("p (c i) t -> p c t i", i=2),
+                tile.rearrange("p (c i) t -> p c t i", i=2),
                 logistic[hf, g][:, :, m0:m1].rearrange("p t (c i) -> p c t i", i=2),
                 weights[:, g, :].unsqueeze(1).unsqueeze(3).to_broadcast([P, (m1 - m0) // 2, PACK, 2]),
                 ALU.mult,
             )
 
-        def quantize_h(hf, g, m0):
-            if m0 == 0:
-                h_codes[hf, g] = sb([P, HALF], U32, "h_codes%d%d" % (hf, g), tag="h_codes%d" % g)
-                h_scales[hf, g] = sb([P, HALF], U8, "h_scales%d%d" % (hf, g))
-            quantize(
-                h_bf16[:, m0 : m0 + COLS, :], h_codes[hf, g][:, m0 : m0 + COLS], h_scales[hf, g][:, m0 : m0 + COLS]
-            )
+        def make_h(hf, g):
+            h_codes[hf, g] = sb([P, HALF], U32, "h_codes%d%d" % (hf, g), tag="h_codes%d" % g)
+            h_scales[hf, g] = sb([P, HALF], U8, "h_scales%d%d" % (hf, g))
+            mid = COLS + COLS // 2
+            h_early = ring.tile([P, COLS // 2, PACK], BF16, name="h_early", align_bytes=64)
+            h_late = ring.tile([P, COLS // 2, PACK], BF16, name="h_late", align_bytes=64)
+            weigh(nc.gpsimd, cw_sb, hf, g, h_shared[:, 0:POOL_COLS, :], 0, POOL_COLS)
+            weigh(nc.vector, cw_ps, hf, g, h_early[:], COLS, mid)
+            weigh(nc.vector, cw_ps, hf, g, h_shared[:, POOL_COLS:COLS, :], POOL_COLS, COLS)
+            weigh(nc.vector, cw_ps, hf, g, h_late[:], mid, HALF)
+            for tile, m0, m1 in ((h_early, COLS, mid), (h_shared, 0, COLS), (h_late, mid, HALF)):
+                quantize(tile[:], h_codes[hf, g][:, m0:m1], h_scales[hf, g][:, m0:m1])
 
         y_banks = {}
 
@@ -301,11 +307,7 @@ def tile_list_kernl_sigm_res_silu_kernel(
                 sigmoids(hf, g)
         for hf in range(2):
             for g in range(2):
-                weigh(nc.gpsimd, cw_sb, hf, g, 0, POOL_COLS)
-                weigh(nc.vector, cw_ps, hf, g, POOL_COLS, COLS)
-                weigh(nc.vector, cw_ps, hf, g, COLS, HALF)
-                for m0 in (0, COLS):
-                    quantize_h(hf, g, m0)
+                make_h(hf, g)
                 for c in range(N // COLS):
                     second_product(hf, g, 0, HALF, c)
         for hf in range(2):

@@ -267,33 +267,37 @@ def tile_list_kernl_sigm_res_silu_kernel(
 
         y_banks = {}
 
-        def second_product(hf, g, m0, width, c):
-            key = (hf, g)
-            if g == 0 and hf == 1:
-                y_banks[hf, c] = bank(1 + c, "y%d%d" % (hf, c))[:, 0:HALF]
-            elif g == 0 and c % 2 == 0:
-                pair = bank((6, 0)[c // 2], "y%d%d" % (hf, c))
-                y_banks[hf, c], y_banks[hf, c + 1] = pair[:, 0:HALF], pair[:, HALF : 2 * HALF]
-            n0 = c * COLS
-            al8_codes = (al8_early, al8_late)[g][:, n0 : n0 + COLS]
-            nc.tensor.matmul_mx(
-                y_banks[hf, c][:, m0 : m0 + width],
-                lhsT=al8_codes.bitcast(FP8X4),
-                lhsT_scale=al_planes[0][:, g, n0 : n0 + COLS],
-                rhs=h_codes[key][:, m0 : m0 + width].bitcast(FP8X4),
-                rhs_scale=h_scales[key][:, m0 : m0 + width],
-                start=(g == 0 and (hf == 1 or c % 2 == 0)),
-                stop=False,
-            )
-            nc.tensor.matmul_mx(
-                y_banks[hf, c][:, m0 : m0 + width],
-                lhsT=al4_codes[:, g, n0 // 2 : (n0 + COLS) // 2].bitcast(FP4X4),
-                lhsT_scale=al_planes[1][:, g, n0 : n0 + COLS],
-                rhs=h_codes[key][:, m0 : m0 + width].bitcast(FP8X4),
-                rhs_scale=h_scales[key][:, m0 : m0 + width],
-                start=False,
-                stop=(g == 1 and (hf == 1 or c % 2 == 1)),
-            )
+        def open_y(hf):
+            if hf == 1:
+                for c in range(N // COLS):
+                    y_banks[hf, c] = bank(1 + c, "y%d%d" % (hf, c))[:, 0:HALF]
+            else:
+                for c in (0, 2):
+                    pair = bank((6, 0)[c // 2], "y%d%d" % (hf, c))
+                    y_banks[hf, c], y_banks[hf, c + 1] = pair[:, 0:HALF], pair[:, HALF : 2 * HALF]
+
+        def second_product(hf, g):
+            blocks = range(N // COLS)
+            if hf == 1:
+                order = [(w, c) for c in blocks for w in range(2)]
+            else:
+                order = [(w, c) for w in ((0, 1), (1, 0))[g] for c in blocks]
+            group = {c: c if hf == 1 else c // 2 for c in blocks}
+            for n, (w, c) in enumerate(order):
+                n0 = c * COLS
+                if w == 0:
+                    codes = (al8_early, al8_late)[g][:, n0 : n0 + COLS].bitcast(FP8X4)
+                else:
+                    codes = al4_codes[:, g, n0 // 2 : (n0 + COLS) // 2].bitcast(FP4X4)
+                nc.tensor.matmul_mx(
+                    y_banks[hf, c],
+                    lhsT=codes,
+                    lhsT_scale=al_planes[w][:, g, n0 : n0 + COLS],
+                    rhs=h_codes[hf, g][:].bitcast(FP8X4),
+                    rhs_scale=h_scales[hf, g][:],
+                    start=(g == 0 and all(group[e] != group[c] for v, e in order[:n])),
+                    stop=(g == 1 and all(group[e] != group[c] for v, e in order[n + 1 :])),
+                )
 
         def finish(hf, c):
             result = sb([P, HALF], F32, "result%d%d" % (hf, c))
@@ -306,10 +310,10 @@ def tile_list_kernl_sigm_res_silu_kernel(
                 first_product(hf, g)
                 sigmoids(hf, g)
         for hf in range(2):
+            open_y(hf)
             for g in range(2):
                 make_h(hf, g)
-                for c in range(N // COLS):
-                    second_product(hf, g, 0, HALF, c)
+                second_product(hf, g)
         for hf in range(2):
             for c in range(N // COLS):
                 finish(hf, c)

@@ -80,11 +80,9 @@ def tile_list_kernl_sigm_res_silu_kernel(
 
         identity = sb([P, P], F32, "identity")
         make_identity(nc, identity[:])
-        vec_bank, cw_bank = bank(6, "vec_bank"), bank(7, "cw_bank")
-        for turned in (vec_bank, cw_bank):
-            for t in range(PACK):
-                nc.tensor.transpose(turned[:, t : KP : PACK], rows[:, t : KP : PACK], identity[:])
-        cw_ps = cw_bank[:, 126 * PACK : KP].rearrange("p (a t) -> p a t", a=2)
+        vec_banks = (bank(7, "vec_bank0"), bank(6, "vec_bank1"))
+        for t in range(PACK):
+            nc.tensor.transpose(vec_banks[t // 2][:, t % 2 : 2 * P : 2], rows[:, t : KP : PACK], identity[:])
 
         picked_scales = placed([P, 2 * J], U8, "picked_scales", TURNED_AT - J)[:, 0:J]
         for g in range(2):
@@ -108,8 +106,15 @@ def tile_list_kernl_sigm_res_silu_kernel(
 
         load_x(1, 1, placed([P, PACK, HALF], F32, "x_11", X11_AT)[:])
 
-        vec_sb = placed([P, 4, PACK], F32, "vec_sb", TURNED_AT)
-        nc.scalar.copy(vec_sb[:].rearrange("p r t -> p (r t)"), vec_bank[:, 124 * PACK : KP])
+        vec_sb = placed([P, 4, PACK], F32, "vec_sb", WINDOW_AT + 2048)
+        for u in range(2):
+            nc.scalar.copy(
+                vec_sb[:, :, 2 * u : 2 * u + 2], vec_banks[u][:, 2 * 124 : 2 * P].rearrange("p (r t) -> p r t", t=2)
+            )
+        cw_bank = bank(7, "cw_bank")
+        for t in range(PACK):
+            nc.tensor.transpose(cw_bank[:, t : KP : PACK], rows[:, t : KP : PACK], identity[:])
+        cw_ps = cw_bank[:, 126 * PACK : KP].rearrange("p (a t) -> p a t", a=2)
         cb_sb, cw_sb = vec_sb[:, 0:2, :], vec_sb[:, 2:4, :]
 
         x11_codes = sb([P, HALF], U32, "x_codes11")

@@ -43,8 +43,8 @@ def tile_list_kernl_sigm_res_silu_kernel(
         def bank(index, name):
             return psum.tile([P, 2 * HALF], F32, name=name, tag="bank%d" % index)
 
-        WORDS_AT, WINDOW_AT, PLANES_AT, TURNED_AT, X11_AT = 0, 16384, 19456, 21504, 22016
-        X00_AT, X10_AT, X11_BF16_AT = 26112, 30208, 35328
+        WORDS_AT, WINDOW_AT, PLANES_AT, TURNED_AT, X11_AT = 0, 16384, 19456, 21504, 22784
+        X00_AT, X10_AT, X11_BF16_AT = 26880, 30976, 36096
 
         rows = sb([P, KP], F32, "rows")
         nc.scalar.dma_start(rows[124:126, :], cb.rearrange("(g j) -> g j", g=2))
@@ -84,7 +84,7 @@ def tile_list_kernl_sigm_res_silu_kernel(
         for t in range(PACK):
             nc.tensor.transpose(vec_banks[t // 2][:, t % 2 : 2 * P : 2], rows[:, t : KP : PACK], identity[:])
 
-        picked_scales = placed([P, 2 * J], U8, "picked_scales", TURNED_AT - J)[:, 0:J]
+        picked_scales = placed([P, X11_AT + 64 - (TURNED_AT - J)], U8, "picked_scales", TURNED_AT - J)[:, 0:J]
         for g in range(2):
             nc.vector.tensor_copy(
                 picked_scales[:, g * KP : (g + 1) * KP],
@@ -117,8 +117,8 @@ def tile_list_kernl_sigm_res_silu_kernel(
         cw_ps = cw_bank[:, 126 * PACK : KP].rearrange("p (a t) -> p a t", a=2)
         cb_sb, cw_sb = vec_sb[:, 0:2, :], vec_sb[:, 2:4, :]
 
-        x11_codes = sb([P, HALF], U32, "x_codes11")
-        x11_scales = sb([P, HALF], U8, "x_scales11")
+        x11_codes = placed([P, HALF], U32, "x_codes11", TURNED_AT)
+        x11_scales = placed([P, HALF], U8, "x_scales11", TURNED_AT + 1024)
         nc.vector.memset(x11_codes[:].bitcast(I32), 0)
         nc.vector.memset(x11_scales[:].bitcast(I32), 0)
         warm_bank = bank(6, "warm_bank")[:, 0:HALF]
@@ -154,9 +154,10 @@ def tile_list_kernl_sigm_res_silu_kernel(
             quantize(x_bf16[a, hf][:], x_codes[a, hf][:], x_scales[a, hf][:])
 
         picked_words, tab_codes = {}, {}
+        picked_all = sb([P, J], U32, "picked_words")
 
         def gather_words(g):
-            picked_words[g] = sb([P, KP], U32, "picked_words%d" % g)[:]
+            picked_words[g] = picked_all[:, g * KP : (g + 1) * KP]
             nc.vector.tensor_copy(
                 picked_words[g], word_window[:].bitcast(U32).indirect(offsets[:, 32 * g : 32 * (g + 1)])
             )
@@ -173,8 +174,12 @@ def tile_list_kernl_sigm_res_silu_kernel(
         part_words(0, 0, sb(codes_shape, U8, "tab_codes00"))
         interleave_x(0, 0)
         quantize_x(0, 0)
-        part_words(0, 1, placed(codes_shape, U8, "tab_codes01", X00_AT))
-        part_words(1, 1, placed(codes_shape, U8, "tab_codes11", X00_AT + 1024))
+        second_pass = placed([P, 2, PACK * 2 * COLS], U8, "tab_codes_pass1", X00_AT)
+        nc.vector.tensor_copy(
+            second_pass[:].bitcast(U16).rearrange("p g (t c i) -> p g c t i", t=PACK, i=4),
+            picked_all[:].bitcast(U16).rearrange("p (g c i t a) -> p a g c t i", g=2, a=2, t=PACK, i=4)[:, 1],
+        )
+        tab_codes[0, 1], tab_codes[1, 1] = second_pass[:, 0, :], second_pass[:, 1, :]
         interleave_x(1, 0)
         quantize_x(1, 0)
         x_codes[0, 1] = sb([P, HALF], U32, "x_codes01")

from contextlib import ExitStack

import concourse.mybir as mybir
from concourse.masks import make_identity

K, M, N, J, T = 1024, 512, 512, 1024, 4096
FLOPS = 2 * K * J * M + 2 * 2 * J * N * M

F32 = mybir.dt.float32
BF16 = mybir.dt.bfloat16
I32 = mybir.dt.int32
U32 = mybir.dt.uint32
U16 = mybir.dt.uint16
U8 = mybir.dt.uint8
FP8X4 = mybir.dt.float8_e4m3fn_x4
FP4X4 = mybir.dt.float4_e2m1fn_x4
ACT = mybir.ActivationFunctionType
ALU = mybir.AluOpType

P = 128
PACK = 4
KP = P * PACK
HALF = M // 2
COLS = 128
POOL_COLS = 48


def tile_list_kernl_sigm_res_silu_kernel(
    tc, x, tab_words, tab_scales, cw, cb, al4_words, al4_scales, al8_words, al8_scales, b, offs, out
):
    nc = tc.nc
    with ExitStack() as ctx:
        held = ctx.enter_context(tc.tile_pool(name="held", bufs=1))
        shared = ctx.enter_context(tc.tile_pool(name="shared", bufs=1))
        psum = ctx.enter_context(tc.psum_pool(name="psum", bufs=1))

        def placed(shape, dtype, name, offset):
            return shared.tile(shape, dtype, name=name, tag=name, align_bytes=64, offset=offset)

        def sb(shape, dtype, name, tag=None):
            return held.tile(shape, dtype, name=name, tag=tag or name, align_bytes=64)

        def bank(index, name):
            return psum.tile([P, 2 * HALF], F32, name=name, tag="bank%d" % index)

        WORDS_AT, WINDOW_AT, PLANES_AT, TURNED_AT, X11_AT = 0, 16384, 19456, 21504, 22784
        X00_AT, X10_AT, X11_BF16_AT = 26880, 30976, 36096

        rows = sb([P, KP], F32, "rows")
        nc.scalar.dma_start(rows[124:126, :], cb.rearrange("(g j) -> g j", g=2))
        nc.scalar.dma_start(rows[126:128, :], cw.rearrange("(g j) -> g j", g=2))
        nc.gpsimd.memset(rows[0:124, :], 0.0)

        offsets = held.tile([P, J // 16], U16, name="offsets")
        nc.sync.dma_start(offsets[:], offs)
        scale_window = placed([P, T // 4], I32, "scale_window", WINDOW_AT)
        nc.sync.dma_start(scale_window[0:32, :], tab_scales.rearrange("a q t -> (a q) t").bitcast(I32))
        al8_rows = al8_words.rearrange("a p n i -> p a (n i)").bitcast(I32)
        word_window = placed([P, T], I32, "word_window", WORDS_AT)
        nc.sync.dma_start(word_window[:], tab_words[0].rearrange("p t b -> p (t b)").bitcast(I32))

        x_raw = {}

        def load_x(a, hf, tile):
            x_raw[a, hf] = tile
            part = x[a * KP : (a + 1) * KP, hf * HALF : (hf + 1) * HALF]
            nc.sync.dma_start(tile, part.rearrange("(p i) m -> p i m", i=PACK))

        load_x(0, 0, placed([P, PACK, HALF], F32, "x_00", X00_AT)[:])
        load_x(1, 0, placed([P, PACK, HALF], F32, "x_10", X10_AT)[:])
        load_x(0, 1, sb([P, PACK, HALF], F32, "x_01")[:])

        warm_in = sb([P, 32], F32, "warm_in")
        nc.vector.memset(warm_in[:], 0.0)
        warm_out = sb([P, 32], F32, "warm_out")
        nc.scalar.activation(warm_out[:], warm_in[:], ACT.Sigmoid)

        nc.vector.memset(scale_window[32:64, :], 0)
        nc.vector.memset(scale_window[64:P, :], 0)

        identity = sb([P, P], F32, "identity")
        make_identity(nc, identity[:])
        vec_banks = (bank(7, "vec_bank0"), bank(6, "vec_bank1"))
        for t in range(PACK):
            nc.tensor.transpose(vec_banks[t // 2][:, t % 2 : 2 * P : 2], rows[:, t : KP : PACK], identity[:])

        picked_scales = placed([P, X11_AT + 64 - (TURNED_AT - J)], U8, "picked_scales", TURNED_AT - J)[:, 0:J]
        for g in range(2):
            nc.vector.tensor_copy(
                picked_scales[:, g * KP : (g + 1) * KP],
                scale_window[:].bitcast(U8).indirect(offsets[:, 32 * g : 32 * (g + 1)]),
            )
        tab_plane0 = sb([P, J // 4], I32, "tab_plane0")
        for g in range(2):
            nc.vector.tensor_copy(
                tab_plane0[:].bitcast(U8).rearrange("p (t g c i) -> p g c t i", t=PACK, g=2, i=16)[:, g],
                picked_scales[:, g * KP : (g + 1) * KP].rearrange("p (c i t) -> p c t i", t=PACK, i=16),
            )
        tab_plane1 = placed([P, J // 4], I32, "tab_plane1", WINDOW_AT)
        for q in range(1, 4):
            nc.scalar.dma_start(tab_plane0[32 * q : 32 * q + 4, :], tab_plane0[4 * q : 4 * q + 4, :])
        for q in range(4):
            queue = nc.gpsimd if q >= 2 else nc.scalar
            queue.dma_start(tab_plane1[32 * q : 32 * q + 4, :], tab_plane0[16 + 4 * q : 20 + 4 * q, :])
        tab_planes = (tab_plane0[:].bitcast(U8), tab_plane1[:].bitcast(U8))

        load_x(1, 1, placed([P, PACK, HALF], F32, "x_11", X11_AT)[:])

        vec_sb = placed([P, 4, PACK], F32, "vec_sb", WINDOW_AT + 2048)
        for u in range(2):
            nc.scalar.copy(
                vec_sb[:, :, 2 * u : 2 * u + 2], vec_banks[u][:, 2 * 124 : 2 * P].rearrange("p (r t) -> p r t", t=2)
            )
        cw_bank = bank(7, "cw_bank")
        for t in range(PACK):
            nc.tensor.transpose(cw_bank[:, t : KP : PACK], rows[:, t : KP : PACK], identity[:])
        cw_ps = cw_bank[:, 126 * PACK : KP].rearrange("p (a t) -> p a t", a=2)
        cb_sb, cw_sb = vec_sb[:, 0:2, :], vec_sb[:, 2:4, :]

        x11_codes = placed([P, HALF], U32, "x_codes11", TURNED_AT)
        x11_scales = placed([P, HALF], U8, "x_scales11", TURNED_AT + 1024)
        nc.vector.memset(x11_codes[:].bitcast(I32), 0)
        nc.vector.memset(x11_scales[:].bitcast(I32), 0)
        warm_bank = bank(6, "warm_bank")[:, 0:HALF]
        for n in range(6):
            nc.tensor.matmul_mx(
                warm_bank,
                lhsT=x11_codes[:, 0:COLS].bitcast(FP8X4),
                lhsT_scale=x11_scales[:, 0:COLS],
                rhs=x11_codes[:].bitcast(FP8X4),
                rhs_scale=x11_scales[:],
                start=True,
                stop=True,
            )

        planes = placed([P, 2, 2, N // 4], I32, "al_planes", PLANES_AT)
        al_planes = [planes[:, w].bitcast(U8) for w in range(2)]

        x_bf16, x_codes, x_scales = {}, {}, {}

        def interleave(tile, raw, copy):
            copy(tile.rearrange("p (c i) t -> p c t i", i=2), raw.rearrange("p t (c i) -> p c t i", i=2))

        def interleave_x(a, hf):
            x_bf16[a, hf] = sb([P, HALF, PACK], BF16, "x_bf16_%d%d" % (a, hf))
            interleave(x_bf16[a, hf][:], x_raw[a, hf], nc.scalar.copy)

        def quantize(src, codes, scales):
            nc.vector.quantize_mx(codes.bitcast(FP8X4), scales, src.rearrange("p m t -> p (m t)"))

        def quantize_x(a, hf):
            x_codes[a, hf] = sb([P, HALF], U32, "x_codes%d%d" % (a, hf))
            x_scales[a, hf] = sb([P, HALF], U8, "x_scales%d%d" % (a, hf))
            quantize(x_bf16[a, hf][:], x_codes[a, hf][:], x_scales[a, hf][:])

        picked_words, tab_codes = {}, {}
        picked_all = sb([P, J], U32, "picked_words")

        def gather_words(g):
            picked_words[g] = picked_all[:, g * KP : (g + 1) * KP]
            nc.vector.tensor_copy(
                picked_words[g], word_window[:].bitcast(U32).indirect(offsets[:, 32 * g : 32 * (g + 1)])
            )

        def part_words(g, a, tile):
            tab_codes[g, a] = tile
            parted = tab_codes[g, a][:].bitcast(U16).rearrange("p (t c i) -> p c t i", t=PACK, i=4)
            paired = picked_words[g].bitcast(U16).rearrange("p (c i t a) -> p a c t i", a=2, t=PACK, i=4)
            nc.vector.tensor_copy(parted, paired[:, a])

        codes_shape = [P, PACK * 2 * COLS]
        gather_words(0)
        gather_words(1)
        part_words(0, 0, sb(codes_shape, U8, "tab_codes00"))
        interleave_x(0, 0)
        quantize_x(0, 0)
        second_pass = placed([P, 2, PACK * 2 * COLS], U8, "tab_codes_pass1", X00_AT)
        nc.vector.tensor_copy(
            second_pass[:].bitcast(U16).rearrange("p g (t c i) -> p g c t i", t=PACK, i=4),
            picked_all[:].bitcast(U16).rearrange("p (g c i t a) -> p a g c t i", g=2, a=2, t=PACK, i=4)[:, 1],
        )
        tab_codes[0, 1], tab_codes[1, 1] = second_pass[:, 0, :], second_pass[:, 1, :]
        interleave_x(1, 0)
        quantize_x(1, 0)
        x_codes[0, 1] = sb([P, HALF], U32, "x_codes01")
        x_scales[0, 1] = sb([P, HALF], U8, "x_scales01")
        x01_halves = {
            0: sb([P, COLS, PACK], BF16, "x_bf16_01_0"),
            COLS: placed([P, COLS, PACK], BF16, "x_bf16_01_128", X10_AT + 1024),
        }
        for m0, copy in ((0, nc.scalar.copy), (COLS, nc.vector.tensor_copy)):
            interleave(x01_halves[m0][:], x_raw[0, 1][:, :, m0 : m0 + COLS], copy)
        part_words(1, 0, placed(codes_shape, U8, "tab_codes10", X10_AT))
        for m0 in (0, COLS):
            quantize(x01_halves[m0][:], x_codes[0, 1][:, m0 : m0 + COLS], x_scales[0, 1][:, m0 : m0 + COLS])
        x_codes[1, 1], x_scales[1, 1] = x11_codes, x11_scales
        x11_halves = {}
        for m0 in (0, COLS):
            x11_halves[m0] = placed([P, COLS, PACK], BF16, "x_bf16_11_%d" % m0, X11_BF16_AT + 8 * m0)
            interleave(x11_halves[m0][:], x_raw[1, 1][:, :, m0 : m0 + COLS], nc.vector.tensor_copy)
        for m0 in (0, COLS):
            quantize(x11_halves[m0][:], x_codes[1, 1][:, m0 : m0 + COLS], x_scales[1, 1][:, m0 : m0 + COLS])

        al8_early = placed([P, N], I32, "al8_early", WORDS_AT)
        nc.sync.dma_start(al8_early[:], al8_rows[:, 0, :])
        al4_codes = placed([P, 2, N // 2], I32, "al4_codes", WORDS_AT + 2048)
        nc.sync.dma_start(al4_codes[:], al4_words.rearrange("a p n -> p a n").bitcast(I32))
        for w, scales in enumerate((al8_scales, al4_scales)):
            for r in range(4):
                nc.sync.dma_start(
                    planes[r:P:32, w], scales.bitcast(I32)[:, r:16:4, :].rearrange("a q n -> q a n")
                )
        al8_late = placed([P, N], I32, "al8_late", X10_AT + 1024)
        nc.sync.dma_start(al8_late[:], al8_rows[:, 1, :])
        b_sb = placed([P, N // P], F32, "b_sb", X11_AT)
        with nc.allow_non_contiguous_dma(reason="one bias value to a partition"):
            nc.sync.dma_start(b_sb[:], b.rearrange("(c p) -> p c", p=P))

        d = {}

        def first_product(hf, g):
            if g == 0:
                d[hf, g] = [bank(t, "d%d%d%d" % (hf, g, t))[:, 0:HALF] for t in range(PACK)]
                order = [(a, t) for a in range(2) for t in range(PACK)]
            else:
                pair = [bank(4 + u, "d%d%d%d" % (hf, g, u)) for u in range(2)]
                d[hf, g] = [pair[t // 2][:, (t % 2) * HALF : (t % 2 + 1) * HALF] for t in range(PACK)]
                order = [(a, t) for t in range(PACK) for a in range(2)]
            for a, t in order:
                codes = tab_codes[g, a][:, t * 2 * COLS : (t + 1) * 2 * COLS]
                nc.tensor.matmul_mx(
                    d[hf, g][t],
                    lhsT=codes.bitcast(FP4X4),
                    lhsT_scale=tab_planes[a][:, (2 * t + g) * COLS : (2 * t + g + 1) * COLS],
                    rhs=x_codes[a, hf][:].bitcast(FP8X4),
                    rhs_scale=x_scales[a, hf][:],
                    start=(a == 0),
                    stop=(a == 1),
                )

        logistic, h_codes, h_scales = {}, {}, {}

        def sigmoids(hf, g):
            name = "logistic%d%d" % (hf, g)
            logistic[hf, g] = sb([P, PACK, HALF], F32, name)
            for t in range(PACK):
                nc.scalar.activation(
                    logistic[hf, g][:, t, :],
                    d[hf, g][t],
                    ACT.Sigmoid,
                    bias=cb_sb[:, g, t : t + 1],
                )

        h_shared = placed([P, COLS, PACK], BF16, "h_shared", X11_BF16_AT + 1024)
        ring = ctx.enter_context(tc.tile_pool(name="ring", bufs=1))

        def weigh(engine, weights, hf, g, tile, m0, m1):
            engine.tensor_tensor(
                tile.rearrange("p (c i) t -> p c t i", i=2),
                logistic[hf, g][:, :, m0:m1].rearrange("p t (c i) -> p c t i", i=2),
                weights[:, g, :].unsqueeze(1).unsqueeze(3).to_broadcast([P, (m1 - m0) // 2, PACK, 2]),
                ALU.mult,
            )

        def make_h(hf, g):
            h_codes[hf, g] = sb([P, HALF], U32, "h_codes%d%d" % (hf, g), tag="h_codes%d" % g)
            h_scales[hf, g] = sb([P, HALF], U8, "h_scales%d%d" % (hf, g))
            mid = COLS + COLS // 2
            h_early = ring.tile([P, COLS // 2, PACK], BF16, name="h_early", align_bytes=64)
            h_late = ring.tile([P, COLS // 2, PACK], BF16, name="h_late", align_bytes=64)
            weigh(nc.gpsimd, cw_sb, hf, g, h_shared[:, 0:POOL_COLS, :], 0, POOL_COLS)
            weigh(nc.vector, cw_ps, hf, g, h_early[:], COLS, mid)
            weigh(nc.vector, cw_ps, hf, g, h_shared[:, POOL_COLS:COLS, :], POOL_COLS, COLS)
            weigh(nc.vector, cw_ps, hf, g, h_late[:], mid, HALF)
            for tile, m0, m1 in ((h_early, COLS, mid), (h_shared, 0, COLS), (h_late, mid, HALF)):
                quantize(tile[:], h_codes[hf, g][:, m0:m1], h_scales[hf, g][:, m0:m1])

        y_banks = {}

        def open_y(hf):
            if hf == 1:
                for c in range(N // COLS):
                    y_banks[hf, c] = bank(1 + c, "y%d%d" % (hf, c))[:, 0:HALF]
            else:
                for c in (0, 2):
                    pair = bank((6, 0)[c // 2], "y%d%d" % (hf, c))
                    y_banks[hf, c], y_banks[hf, c + 1] = pair[:, 0:HALF], pair[:, HALF : 2 * HALF]

        def second_product(hf, g):
            blocks = range(N // COLS)
            if hf == 1:
                order = [(w, c) for c in blocks for w in range(2)]
            else:
                order = [(w, c) for w in ((0, 1), (1, 0))[g] for c in blocks]
            group = {c: c if hf == 1 else c // 2 for c in blocks}
            for n, (w, c) in enumerate(order):
                n0 = c * COLS
                if w == 0:
                    codes = (al8_early, al8_late)[g][:, n0 : n0 + COLS].bitcast(FP8X4)
                else:
                    codes = al4_codes[:, g, n0 // 2 : (n0 + COLS) // 2].bitcast(FP4X4)
                nc.tensor.matmul_mx(
                    y_banks[hf, c],
                    lhsT=codes,
                    lhsT_scale=al_planes[w][:, g, n0 : n0 + COLS],
                    rhs=h_codes[hf, g][:].bitcast(FP8X4),
                    rhs_scale=h_scales[hf, g][:],
                    start=(g == 0 and all(group[e] != group[c] for v, e in order[:n])),
                    stop=(g == 1 and all(group[e] != group[c] for v, e in order[n + 1 :])),
                )

        def finish(hf, c):
            result = sb([P, HALF], F32, "result%d%d" % (hf, c))
            nc.scalar.activation(result[:], y_banks[hf, c], ACT.Silu, bias=b_sb[:, c : c + 1])
            queue = nc.scalar if (hf, c) == (1, 3) else nc.sync
            queue.dma_start(out[c * COLS : (c + 1) * COLS, hf * HALF : (hf + 1) * HALF], result[:])

        for hf in range(2):
            for g in range(2):
                first_product(hf, g)
                sigmoids(hf, g)
        for hf in range(2):
            open_y(hf)
            for g in range(2):
                make_h(hf, g)
                second_product(hf, g)
        for hf in range(2):
            for c in range(N // COLS):
                finish(hf, c)
